import numpy as np
import ml_dtypes


def mxq(x, axis, fmt="e4m3"):
    dtype, down = {"e4m3": (ml_dtypes.float8_e4m3fn, 7), "e5m2": (ml_dtypes.float8_e5m2, 14)}[fmt]
    v = np.moveaxis(np.asarray(x, np.float32).astype(ml_dtypes.bfloat16).astype(np.float64), axis, -1)
    blocks = v.reshape(v.shape[:-1] + (-1, 32))
    amax = np.abs(blocks).max(-1, keepdims=True)
    byte = np.maximum(np.where(amax > 0, np.frexp(amax)[1] - 1 + 127, 0) - down, 1)
    scale = np.exp2(byte - 127.0)
    codes = (blocks / scale).astype(np.float32).astype(dtype).astype(np.float64)
    return np.moveaxis((codes * scale).reshape(v.shape), -1, axis)


WIDE = False


def mx_kscale(k):
    if not WIDE:
        return np.ones(k)
    levels = np.array([18, -18])
    if k % 512:
        return np.exp2(np.random.permutation(np.resize(levels, k // 32))).repeat(32)
    a = np.empty((k // 512, 16))
    for p in range(k // 512):
        a[p, :8] = np.random.permutation(np.resize(levels, 8))
        for g in range(8):
            far = levels[np.abs(levels - a[p, g]) >= 10]
            a[p, g + 8] = far[np.random.randint(len(far))]
    return np.exp2(a.ravel()).repeat(32)


def f64(x):
    return np.asarray(x).astype(np.float64)


def striped(idx):
    return np.tile(np.asarray(idx).reshape(-1, 16).T, (8, 1)).astype(np.uint16)


def unstriped(offs):
    return offs[:16].T.reshape(-1).astype(np.int64)


B, N, T, D, DV, R = 1, 512, 2048, 512, 512, 1024


def setup_inputs():
    n = np.random.standard_normal
    idx = np.random.permutation(T)[:B * N]
    s = mx_kscale(D)[:, None]
    z = mx_kscale(R)[:, None]
    q = n((B, D, R))
    do = n((B, DV, R))
    return {
        "qT": (q * s).astype(np.float32),
        "kT": (n((D, T)) * (0.50 / np.sqrt(D)) / s).astype(np.float32),
        "lse": (np.log(N) + 0.12 + 0.1 * n((B, R, 1))).astype(np.float32),
        "rw": (np.random.uniform(0.5, 1.5, (B, R, 1)) * N / np.sqrt(R) * z).astype(np.float32),
        "dom": (do.transpose(0, 2, 1) / z).astype(np.float32),
        "offs": striped(idx),
    }


def reference(qT, kT, lse, rw, dom, offs):
    idx = unstriped(offs)
    pick = lambda x: x[:, idx].reshape(x.shape[0], B, N).transpose(1, 0, 2)
    a = mxq(f64(qT), 1, "e4m3").transpose(0, 2, 1) @ mxq(pick(f64(kT)), 1, "e4m3")
    p = np.exp(a - f64(lse))
    dv = mxq(f64(dom), 1, "e5m2").transpose(0, 2, 1) @ mxq(f64(rw) * p, 1, "e4m3")
    gv = np.zeros((DV, T))
    gv[:, idx] = dv.transpose(1, 0, 2).reshape(DV, B * N)
    return gv

@@ -1,0 +1,132 @@
+from contextlib import ExitStack
+
+import concourse.mybir as mybir
+
+N, T, D, DV, R = 512, 2048, 512, 512, 1024
+FLOPS = 2 * D * R * N + 2 * R * DV * N
+
+F32 = mybir.dt.float32
+BF16 = mybir.dt.bfloat16
+U32 = mybir.dt.uint32
+U16 = mybir.dt.uint16
+U8 = mybir.dt.uint8
+E4M3 = mybir.dt.float8_e4m3fn_x4
+E5M2 = mybir.dt.float8_e5m2_x4
+EXP = mybir.ActivationFunctionType.Exp
+MULT = mybir.AluOpType.mult
+
+P = 128
+PACK = 4
+PASSES = R // (P * PACK)
+HALVES = 2
+HALF = N // HALVES
+RUN = 4
+E_BLOCKS = DV // P
+
+
+def tile_attend_gat_lse_v_kernel(tc, qT, kT, lse, rw, dom, offs, out):
+    nc = tc.nc
+    with ExitStack() as ctx:
+        sb = ctx.enter_context(tc.tile_pool(name="sb", bufs=1))
+        ps_scores = ctx.enter_context(tc.psum_pool(name="ps_scores", bufs=2))
+        ps_out = ctx.enter_context(tc.psum_pool(name="ps_out", bufs=E_BLOCKS))
+
+        def quantise(name, grouped, words, fmt):
+            codes = sb.tile([P, words], U32, name=name + "_codes", align_bytes=64)
+            scales = sb.tile([P, words], U8, name=name + "_scales", align_bytes=64)
+            nc.vector.quantize_mx(out=codes[:].bitcast(fmt), scales=scales[:], in_=grouped)
+            return codes, scales
+
+        offsets = sb.tile([P, N // 16], U16, name="offsets")
+        nc.sync.dma_start(offsets[:], offs)
+        lse_sb = sb.tile([P, PASSES, PACK], F32, name="lse_sb")
+        rw_sb = sb.tile([P, PASSES, PACK], F32, name="rw_sb")
+        nc.scalar.dma_start(lse_sb[:], lse[0].rearrange("(g p t) o -> p g (t o)", p=P, t=PACK))
+        nc.scalar.dma_start(rw_sb[:], rw[0].rearrange("(g p t) o -> p g (t o)", p=P, t=PACK))
+
+        q_rows = qT[0].rearrange("(p j) (g c) -> g p j c", j=PACK, g=PASSES)
+        k_rows = kT.rearrange("(p j) c -> j p c", j=PACK)
+        dom_rows = dom[0].rearrange("(g p j) e -> g p j e", p=P, j=PACK)
+        q_raw = [sb.tile([P, PACK, P * PACK], F32, name="q_raw%d" % g) for g in range(PASSES)]
+        k_plane = [sb.tile([P, T], F32, name="k_plane%d" % j) for j in range(PACK)]
+        dom_raw = [sb.tile([P, PACK, DV], F32, name="dom_raw%d" % g) for g in range(PASSES)]
+        nc.sync.dma_start(q_raw[0][:], q_rows[0])
+        for j in range(PACK):
+            nc.sync.dma_start(k_plane[j][:], k_rows[j])
+        nc.sync.dma_start(q_raw[1][:], q_rows[1])
+        for g in range(PASSES):
+            nc.sync.dma_start(dom_raw[g][:], dom_rows[g])
+
+        window = [sb.tile([P, T], F32, name="window%d" % b) for b in range(E_BLOCKS)]
+        for b in range(E_BLOCKS):
+            nc.vector.memset(window[b][:], 0.0)
+        neg_lse = sb.tile([P, PASSES, PACK], F32, name="neg_lse")
+        nc.vector.tensor_scalar(neg_lse[:], lse_sb[:], -1.0, None, op0=MULT)
+
+        def cast_q(g, copy):
+            grouped = sb.tile([P, PACK, P, PACK], BF16, name="q_grouped%d" % g, align_bytes=64)
+            copy(grouped[:].rearrange("p t m j -> p m j t"), q_raw[g][:].rearrange("p j (m t) -> p m j t", t=PACK))
+            return grouped[:].rearrange("p t m j -> p (t m j)")
+
+        q_mx = [None] * PASSES
+        q_mx[0] = quantise("q0", cast_q(0, nc.scalar.copy), PACK * P, E4M3)
+
+        k_grouped = [sb.tile([P, HALF, PACK], BF16, name="k_grouped%d" % h, align_bytes=64) for h in range(HALVES)]
+        k_mx = [None] * HALVES
+        for j in range(PACK):
+            for h in range(HALVES):
+                cols = slice(h * HALF // 16, (h + 1) * HALF // 16)
+                nc.vector.tensor_copy(k_grouped[h][:, :, j], k_plane[j][:].indirect(offsets[:, cols]))
+                if j == PACK - 1:
+                    k_mx[h] = quantise("k%d" % h, k_grouped[h][:].rearrange("p i j -> p (i j)"), HALF, E4M3)
+
+        q_mx[1] = quantise("q1", cast_q(1, nc.vector.tensor_copy), PACK * P, E4M3)
+
+        pw_codes = [sb.tile([P, N], U32, name="pw_codes%d" % g, align_bytes=64) for g in range(PASSES)]
+        pw_scales = [sb.tile([P, N], U8, name="pw_scales%d" % g, align_bytes=64) for g in range(PASSES)]
+        pw_grouped = {}
+
+        def weigh(g, h):
+            scores = ps_scores.tile([P, PACK, HALF], F32, name="scores")
+            q_codes, q_scales = q_mx[g]
+            k_codes, k_scales = k_mx[h]
+            for t in range(PACK):
+                m = slice(t * P, (t + 1) * P)
+                nc.tensor.matmul_mx(out=scores[:, t, :], lhsT=q_codes[:, m].bitcast(E4M3), lhsT_scale=q_scales[:, m],
+                                    rhs=k_codes[:].bitcast(E4M3), rhs_scale=k_scales[:], start=True, stop=True)
+            p32 = sb.tile([P, PACK, HALF], F32, name="p32_%d%d" % (g, h))
+            for t in range(PACK):
+                nc.scalar.activation(p32[:, t, :], scores[:, t, :], EXP, bias=neg_lse[:, g, t : t + 1])
+            pw = sb.tile([P, HALF, PACK], BF16, name="pw_%d%d" % (g, h), align_bytes=64)
+            gate = rw_sb[:, g, :].unsqueeze(1).unsqueeze(3).to_broadcast([P, HALF // RUN, PACK, RUN])
+            nc.vector.tensor_tensor(pw[:].rearrange("p (c i) t -> p c t i", i=RUN),
+                                    p32[:].rearrange("p t (c i) -> p c t i", i=RUN), gate, MULT)
+            pw_grouped[(g, h)] = pw
+
+        def quantise_pw(g, h):
+            cols = slice(h * HALF, (h + 1) * HALF)
+            nc.vector.quantize_mx(out=pw_codes[g][:, cols].bitcast(E4M3), scales=pw_scales[g][:, cols],
+                                  in_=pw_grouped[(g, h)][:].rearrange("p i t -> p (i t)"))
+
+        for g in range(PASSES):
+            for h in range(HALVES):
+                weigh(g, h)
+                quantise_pw(g, h)
+
+        for b in range(E_BLOCKS):
+            e = slice(b * P, (b + 1) * P)
+            grouped = sb.tile([P, PASSES, P, PACK], BF16, name="dom_grouped%d" % b, align_bytes=64)
+            for g in range(PASSES):
+                nc.scalar.copy(grouped[:, g].rearrange("p (c i) j -> p c j i", i=RUN),
+                               dom_raw[g][:, :, e].rearrange("p j (c i) -> p c j i", i=RUN))
+            d_codes, d_scales = quantise("dom%d" % b, grouped[:].rearrange("p g e j -> p (g e j)"), PASSES * P, E5M2)
+            acc = ps_out.tile([P, N], F32, name="acc")
+            for g in range(PASSES):
+                m = slice(g * P, (g + 1) * P)
+                nc.tensor.matmul_mx(out=acc[:], lhsT=d_codes[:, m].bitcast(E5M2), lhsT_scale=d_scales[:, m],
+                                    rhs=pw_codes[g][:].bitcast(E4M3), rhs_scale=pw_scales[g][:],
+                                    start=(g == 0), stop=(g == PASSES - 1))
+            dv = sb.tile([P, N], F32, name="dv%d" % b)
+            nc.scalar.copy(dv[:], acc[:])
+            nc.vector.tensor_copy(window[b][:].indirect(offsets[:]), dv[:])
+            nc.sync.dma_start(out[e, :], window[b][:])

@@ -22,6 +22,8 @@ HALVES = 2
 HALF = N // HALVES
 RUN = 4
 E_BLOCKS = DV // P
+WINDOWS = 3
+Q_LOADS = [(0, 0, 64), (0, 64, 128), (1, 0, 128)]
 
 
 def tile_attend_gat_lse_v_kernel(tc, qT, kT, lse, rw, dom, offs, out):
@@ -38,7 +40,6 @@ def tile_attend_gat_lse_v_kernel(tc, qT, kT, lse, rw, dom, offs, out):
             return codes, scales
 
         offsets = sb.tile([P, N // 16], U16, name="offsets")
-        nc.sync.dma_start(offsets[:], offs)
         lse_sb = sb.tile([P, PASSES, PACK], F32, name="lse_sb")
         rw_sb = sb.tile([P, PASSES, PACK], F32, name="rw_sb")
         nc.scalar.dma_start(lse_sb[:], lse[0].rearrange("(g p t) o -> p g (t o)", p=P, t=PACK))
@@ -47,79 +48,82 @@ def tile_attend_gat_lse_v_kernel(tc, qT, kT, lse, rw, dom, offs, out):
         q_rows = qT[0].rearrange("(p j) (g c) -> g p j c", j=PACK, g=PASSES)
         k_rows = kT.rearrange("(p j) c -> j p c", j=PACK)
         dom_rows = dom[0].rearrange("(g p j) e -> g p j e", p=P, j=PACK)
-        q_raw = [sb.tile([P, PACK, P * PACK], F32, name="q_raw%d" % g) for g in range(PASSES)]
+        q_raw = {}
+        for g, m0, m1 in Q_LOADS:
+            q_raw[(g, m0)] = sb.tile([P, PACK, (m1 - m0) * PACK], F32, name="q_raw%d_%d" % (g, m0))
         k_plane = [sb.tile([P, T], F32, name="k_plane%d" % j) for j in range(PACK)]
         dom_raw = [sb.tile([P, PACK, DV], F32, name="dom_raw%d" % g) for g in range(PASSES)]
-        nc.sync.dma_start(q_raw[0][:], q_rows[0])
-        for j in range(PACK):
-            nc.sync.dma_start(k_plane[j][:], k_rows[j])
-        nc.sync.dma_start(q_raw[1][:], q_rows[1])
+        nc.sync.dma_start(k_plane[0][:], k_rows[0])
+        nc.sync.dma_start(offsets[:], offs)
+        nc.sync.dma_start(k_plane[1][:], k_rows[1])
+        nc.sync.dma_start(k_plane[2][:], k_rows[2])
+        nc.sync.dma_start(k_plane[3][:], k_rows[3])
+        for g, m0, m1 in Q_LOADS:
+            nc.sync.dma_start(q_raw[(g, m0)][:], q_rows[g][:, :, m0 * PACK : m1 * PACK])
         for g in range(PASSES):
             nc.sync.dma_start(dom_raw[g][:], dom_rows[g])
 
-        window = [sb.tile([P, T], F32, name="window%d" % b) for b in range(E_BLOCKS)]
-        for b in range(E_BLOCKS):
+        window = [sb.tile([P, T], F32, name="window%d" % b) for b in range(WINDOWS)]
+        for b in range(WINDOWS):
             nc.vector.memset(window[b][:], 0.0)
         neg_lse = sb.tile([P, PASSES, PACK], F32, name="neg_lse")
         nc.vector.tensor_scalar(neg_lse[:], lse_sb[:], -1.0, None, op0=MULT)
 
-        def cast_q(g, copy):
-            grouped = sb.tile([P, PACK, P, PACK], BF16, name="q_grouped%d" % g, align_bytes=64)
-            copy(grouped[:].rearrange("p t m j -> p m j t"), q_raw[g][:].rearrange("p j (m t) -> p m j t", t=PACK))
-            return grouped[:].rearrange("p t m j -> p (t m j)")
-
+        q_grouped = [sb.tile([P, PACK, P, PACK], BF16, name="q_grouped%d" % g, align_bytes=64) for g in range(PASSES)]
         q_mx = [None] * PASSES
-        q_mx[0] = quantise("q0", cast_q(0, nc.scalar.copy), PACK * P, E4M3)
 
-        k_grouped = [sb.tile([P, HALF, PACK], BF16, name="k_grouped%d" % h, align_bytes=64) for h in range(HALVES)]
-        k_mx = [None] * HALVES
+        def cast_q(copy, g, m0, m1):
+            base = max(l0 for lg, l0, l1 in Q_LOADS if lg == g and l0 <= m0)
+            dst = q_grouped[g][:].rearrange("p t m j -> p m j t")
+            src = q_raw[(g, base)][:].rearrange("p j (m t) -> p m j t", t=PACK)
+            copy(dst[:, m0:m1], src[:, m0 - base : m1 - base])
+
+        def quantise_q(g):
+            q_mx[g] = quantise("q%d" % g, q_grouped[g][:].rearrange("p t m j -> p (t m j)"), PACK * P, E4M3)
+
+        k_grouped = sb.tile([P, N, PACK], BF16, name="k_grouped", align_bytes=64)
         for j in range(PACK):
-            for h in range(HALVES):
-                cols = slice(h * HALF // 16, (h + 1) * HALF // 16)
-                nc.vector.tensor_copy(k_grouped[h][:, :, j], k_plane[j][:].indirect(offsets[:, cols]))
-                if j == PACK - 1:
-                    k_mx[h] = quantise("k%d" % h, k_grouped[h][:].rearrange("p i j -> p (i j)"), HALF, E4M3)
-
-        q_mx[1] = quantise("q1", cast_q(1, nc.vector.tensor_copy), PACK * P, E4M3)
+            nc.vector.tensor_copy(k_grouped[:, :, j], k_plane[j][:].indirect(offsets[:]))
+        k_codes, k_scales = quantise("k", k_grouped[:].rearrange("p i j -> p (i j)"), N, E4M3)
 
         pw_codes = [sb.tile([P, N], U32, name="pw_codes%d" % g, align_bytes=64) for g in range(PASSES)]
         pw_scales = [sb.tile([P, N], U8, name="pw_scales%d" % g, align_bytes=64) for g in range(PASSES)]
-        pw_grouped = {}
+        pw = [sb.tile([P, N, PACK], BF16, name="pw%d" % g, align_bytes=64) for g in range(PASSES)]
+        p32 = {}
 
-        def weigh(g, h):
+        def probs(g, h):
             scores = ps_scores.tile([P, PACK, HALF], F32, name="scores")
             q_codes, q_scales = q_mx[g]
-            k_codes, k_scales = k_mx[h]
+            cols = slice(h * HALF, (h + 1) * HALF)
             for t in range(PACK):
                 m = slice(t * P, (t + 1) * P)
                 nc.tensor.matmul_mx(out=scores[:, t, :], lhsT=q_codes[:, m].bitcast(E4M3), lhsT_scale=q_scales[:, m],
-                                    rhs=k_codes[:].bitcast(E4M3), rhs_scale=k_scales[:], start=True, stop=True)
-            p32 = sb.tile([P, PACK, HALF], F32, name="p32_%d%d" % (g, h))
+                                    rhs=k_codes[:, cols].bitcast(E4M3), rhs_scale=k_scales[:, cols], start=True, stop=True)
+            p32[(g, h)] = sb.tile([P, PACK, HALF], F32, name="p32_%d%d" % (g, h))
             for t in range(PACK):
-                nc.scalar.activation(p32[:, t, :], scores[:, t, :], EXP, bias=neg_lse[:, g, t : t + 1])
-            pw = sb.tile([P, HALF, PACK], BF16, name="pw_%d%d" % (g, h), align_bytes=64)
+                nc.scalar.activation(p32[(g, h)][:, t, :], scores[:, t, :], EXP, bias=neg_lse[:, g, t : t + 1])
+
+        def weigh(g, h):
             gate = rw_sb[:, g, :].unsqueeze(1).unsqueeze(3).to_broadcast([P, HALF // RUN, PACK, RUN])
-            nc.vector.tensor_tensor(pw[:].rearrange("p (c i) t -> p c t i", i=RUN),
-                                    p32[:].rearrange("p t (c i) -> p c t i", i=RUN), gate, MULT)
-            pw_grouped[(g, h)] = pw
+            nc.vector.tensor_tensor(pw[g][:, h * HALF : (h + 1) * HALF, :].rearrange("p (c i) t -> p c t i", i=RUN),
+                                    p32[(g, h)][:].rearrange("p t (c i) -> p c t i", i=RUN), gate, MULT)
 
-        def quantise_pw(g, h):
-            cols = slice(h * HALF, (h + 1) * HALF)
-            nc.vector.quantize_mx(out=pw_codes[g][:, cols].bitcast(E4M3), scales=pw_scales[g][:, cols],
-                                  in_=pw_grouped[(g, h)][:].rearrange("p i t -> p (i t)"))
+        def quantise_pw(g, i0, i1):
+            nc.vector.quantize_mx(out=pw_codes[g][:, i0:i1].bitcast(E4M3), scales=pw_scales[g][:, i0:i1],
+                                  in_=pw[g][:, i0:i1, :].rearrange("p i t -> p (i t)"))
 
-        for g in range(PASSES):
-            for h in range(HALVES):
-                weigh(g, h)
-                quantise_pw(g, h)
+        dom_grouped = [sb.tile([P, PASSES, P, PACK], BF16, name="dom_grouped%d" % b, align_bytes=64) for b in range(E_BLOCKS)]
+        dom_mx = [None] * E_BLOCKS
 
-        for b in range(E_BLOCKS):
-            e = slice(b * P, (b + 1) * P)
-            grouped = sb.tile([P, PASSES, P, PACK], BF16, name="dom_grouped%d" % b, align_bytes=64)
-            for g in range(PASSES):
-                nc.scalar.copy(grouped[:, g].rearrange("p (c i) j -> p c j i", i=RUN),
-                               dom_raw[g][:, :, e].rearrange("p j (c i) -> p c j i", i=RUN))
-            d_codes, d_scales = quantise("dom%d" % b, grouped[:].rearrange("p g e j -> p (g e j)"), PASSES * P, E5M2)
+        def cast_dom(b, g):
+            nc.scalar.copy(dom_grouped[b][:, g].rearrange("p (c i) j -> p c j i", i=RUN),
+                           dom_raw[g][:, :, b * P : (b + 1) * P].rearrange("p j (c i) -> p c j i", i=RUN))
+
+        def quantise_dom(b):
+            dom_mx[b] = quantise("dom%d" % b, dom_grouped[b][:].rearrange("p g e j -> p (g e j)"), PASSES * P, E5M2)
+
+        def product(b, pieces):
+            d_codes, d_scales = dom_mx[b]
             acc = ps_out.tile([P, N], F32, name="acc")
             for g in range(PASSES):
                 m = slice(g * P, (g + 1) * P)
@@ -127,6 +131,51 @@ def tile_attend_gat_lse_v_kernel(tc, qT, kT, lse, rw, dom, offs, out):
                                     rhs=pw_codes[g][:].bitcast(E4M3), rhs_scale=pw_scales[g][:],
                                     start=(g == 0), stop=(g == PASSES - 1))
             dv = sb.tile([P, N], F32, name="dv%d" % b)
-            nc.scalar.copy(dv[:], acc[:])
-            nc.vector.tensor_copy(window[b][:].indirect(offsets[:]), dv[:])
-            nc.sync.dma_start(out[e, :], window[b][:])
+            width = N // pieces
+            for u in range(pieces):
+                nc.scalar.copy(dv[:, u * width : (u + 1) * width], acc[:, u * width : (u + 1) * width])
+            return dv
+
+        def scatter(b, dv, pieces):
+            width = N // pieces
+            win = window[b % WINDOWS]
+            for u in range(pieces):
+                nc.vector.tensor_copy(win[:].indirect(offsets[:, u * width // 16 : (u + 1) * width // 16]),
+                                      dv[:, u * width : (u + 1) * width])
+            nc.sync.dma_start(out[b * P : (b + 1) * P, :], win[:])
+
+        cast_q(nc.scalar.copy, 0, 0, 64)
+        cast_q(nc.vector.tensor_copy, 0, 64, 104)
+        cast_q(nc.scalar.copy, 0, 104, P)
+        quantise_q(0)
+        probs(0, 0)
+        cast_q(nc.vector.tensor_copy, 1, 0, 88)
+        cast_q(nc.scalar.copy, 1, 88, P)
+        weigh(0, 0)
+        quantise_q(1)
+        probs(0, 1)
+        probs(1, 0)
+        weigh(0, 1)
+        quantise_pw(0, 0, HALF)
+        probs(1, 1)
+        cast_dom(0, 0)
+        cast_dom(0, 1)
+        weigh(1, 0)
+        quantise_pw(0, HALF, N)
+        weigh(1, 1)
+        quantise_pw(1, 0, HALF)
+        quantise_dom(0)
+        quantise_pw(1, HALF, N)
+        dv = [None] * E_BLOCKS
+        dv[0] = product(0, 2)
+        for g in range(PASSES):
+            cast_dom(1, g)
+        quantise_dom(1)
+        for b in range(E_BLOCKS):
+            if b + 2 < E_BLOCKS:
+                for g in range(PASSES):
+                    cast_dom(b + 2, g)
+                quantise_dom(b + 2)
+            if b + 1 < E_BLOCKS:
+                dv[b + 1] = product(b + 1, 1)
+            scatter(b, dv[b], 2 if b == 0 else 1)

@@ -23,7 +23,7 @@ HALF = N // HALVES
 RUN = 4
 E_BLOCKS = DV // P
 WINDOWS = 3
-Q_LOADS = [(0, 0, 64), (0, 64, 128), (1, 0, 128)]
+Q_LOADS = [(0, 0, 64), (0, 64, 128), (1, 0, 64), (1, 64, 128)]
 
 
 def tile_attend_gat_lse_v_kernel(tc, qT, kT, lse, rw, dom, offs, out):
@@ -65,15 +65,17 @@ def tile_attend_gat_lse_v_kernel(tc, qT, kT, lse, rw, dom, offs, out):
 
         window = [sb.tile([P, T], F32, name="window%d" % b) for b in range(WINDOWS)]
         for b in range(WINDOWS):
-            nc.vector.memset(window[b][:], 0.0)
+            (nc.vector if b == 0 else nc.gpsimd).memset(window[b][:], 0.0)
         neg_lse = sb.tile([P, PASSES, PACK], F32, name="neg_lse")
         nc.vector.tensor_scalar(neg_lse[:], lse_sb[:], -1.0, None, op0=MULT)
 
-        q_grouped = [sb.tile([P, PACK, P, PACK], BF16, name="q_grouped%d" % g, align_bytes=64) for g in range(PASSES)]
+        q_grouped = {}
         q_mx = [None] * PASSES
 
         def cast_q(copy, g, m0, m1):
             base = max(l0 for lg, l0, l1 in Q_LOADS if lg == g and l0 <= m0)
+            if g not in q_grouped:
+                q_grouped[g] = sb.tile([P, PACK, P, PACK], BF16, name="q_grouped", align_bytes=64)
             dst = q_grouped[g][:].rearrange("p t m j -> p m j t")
             src = q_raw[(g, base)][:].rearrange("p j (m t) -> p m j t", t=PACK)
             copy(dst[:, m0:m1], src[:, m0 - base : m1 - base])
@@ -81,10 +83,12 @@ def tile_attend_gat_lse_v_kernel(tc, qT, kT, lse, rw, dom, offs, out):
         def quantise_q(g):
             q_mx[g] = quantise("q%d" % g, q_grouped[g][:].rearrange("p t m j -> p (t m j)"), PACK * P, E4M3)
 
-        k_grouped = sb.tile([P, N, PACK], BF16, name="k_grouped", align_bytes=64)
+        k_grouped = [sb.tile([P, HALF, PACK], BF16, name="k_grouped%d" % h, align_bytes=64) for h in range(HALVES)]
         for j in range(PACK):
-            nc.vector.tensor_copy(k_grouped[:, :, j], k_plane[j][:].indirect(offsets[:]))
-        k_codes, k_scales = quantise("k", k_grouped[:].rearrange("p i j -> p (i j)"), N, E4M3)
+            for h in range(HALVES):
+                entries = offsets[:, h * HALF // 16 : (h + 1) * HALF // 16]
+                nc.vector.tensor_copy(k_grouped[h][:, :, j], k_plane[j][:].indirect(entries))
+        k_mx = [quantise("k%d" % h, k_grouped[h][:].rearrange("p i j -> p (i j)"), HALF, E4M3) for h in range(HALVES)]
 
         pw_codes = [sb.tile([P, N], U32, name="pw_codes%d" % g, align_bytes=64) for g in range(PASSES)]
         pw_scales = [sb.tile([P, N], U8, name="pw_scales%d" % g, align_bytes=64) for g in range(PASSES)]
@@ -94,12 +98,12 @@ def tile_attend_gat_lse_v_kernel(tc, qT, kT, lse, rw, dom, offs, out):
         def probs(g, h):
             scores = ps_scores.tile([P, PACK, HALF], F32, name="scores")
             q_codes, q_scales = q_mx[g]
-            cols = slice(h * HALF, (h + 1) * HALF)
+            k_codes, k_scales = k_mx[h]
             for t in range(PACK):
                 m = slice(t * P, (t + 1) * P)
                 nc.tensor.matmul_mx(out=scores[:, t, :], lhsT=q_codes[:, m].bitcast(E4M3), lhsT_scale=q_scales[:, m],
-                                    rhs=k_codes[:, cols].bitcast(E4M3), rhs_scale=k_scales[:, cols], start=True, stop=True)
-            p32[(g, h)] = sb.tile([P, PACK, HALF], F32, name="p32_%d%d" % (g, h))
+                                    rhs=k_codes[:].bitcast(E4M3), rhs_scale=k_scales[:], start=True, stop=True)
+            p32[(g, h)] = sb.tile([P, PACK, HALF], F32, name="p32_%d%d" % (g, h), align_bytes=64)
             for t in range(PACK):
                 nc.scalar.activation(p32[(g, h)][:, t, :], scores[:, t, :], EXP, bias=neg_lse[:, g, t : t + 1])
 
@@ -112,15 +116,18 @@ def tile_attend_gat_lse_v_kernel(tc, qT, kT, lse, rw, dom, offs, out):
             nc.vector.quantize_mx(out=pw_codes[g][:, i0:i1].bitcast(E4M3), scales=pw_scales[g][:, i0:i1],
                                   in_=pw[g][:, i0:i1, :].rearrange("p i t -> p (i t)"))
 
-        dom_grouped = [sb.tile([P, PASSES, P, PACK], BF16, name="dom_grouped%d" % b, align_bytes=64) for b in range(E_BLOCKS)]
+        dom_grouped = []
         dom_mx = [None] * E_BLOCKS
 
         def cast_dom(b, g):
+            if not dom_grouped:
+                whole = sb.tile([P, E_BLOCKS - 1, PASSES, P, PACK], BF16, name="dom_grouped", tag="p32_01", align_bytes=64)
+                dom_grouped.extend(whole[:, blk] for blk in range(E_BLOCKS - 1))
             nc.scalar.copy(dom_grouped[b][:, g].rearrange("p (c i) j -> p c j i", i=RUN),
                            dom_raw[g][:, :, b * P : (b + 1) * P].rearrange("p j (c i) -> p c j i", i=RUN))
 
         def quantise_dom(b):
-            dom_mx[b] = quantise("dom%d" % b, dom_grouped[b][:].rearrange("p g e j -> p (g e j)"), PASSES * P, E5M2)
+            dom_mx[b] = quantise("dom%d" % b, dom_grouped[b].rearrange("p g e j -> p (g e j)"), PASSES * P, E5M2)
 
         def product(b, pieces):
             d_codes, d_scales = dom_mx[b]
@@ -149,11 +156,11 @@ def tile_attend_gat_lse_v_kernel(tc, qT, kT, lse, rw, dom, offs, out):
         cast_q(nc.scalar.copy, 0, 104, P)
         quantise_q(0)
         probs(0, 0)
-        cast_q(nc.vector.tensor_copy, 1, 0, 88)
-        cast_q(nc.scalar.copy, 1, 88, P)
-        weigh(0, 0)
+        cast_q(nc.vector.tensor_copy, 1, 0, 64)
+        cast_q(nc.vector.tensor_copy, 1, 64, P)
         quantise_q(1)
         probs(0, 1)
+        weigh(0, 0)
         probs(1, 0)
         weigh(0, 1)
         quantise_pw(0, 0, HALF)
@@ -162,20 +169,30 @@ def tile_attend_gat_lse_v_kernel(tc, qT, kT, lse, rw, dom, offs, out):
         cast_dom(0, 1)
         weigh(1, 0)
         quantise_pw(0, HALF, N)
+        warm = ps_scores.tile([P, PACK, HALF], F32, name="scores")
+        for u in range(3):
+            nc.tensor.matmul_mx(out=warm[:, 0:2, :].rearrange("p a i -> p (a i)"), lhsT=q_mx[1][0][:, 0:P].bitcast(E4M3), lhsT_scale=q_mx[1][1][:, 0:P],
+                                rhs=pw_codes[0][:].bitcast(E4M3), rhs_scale=pw_scales[0][:], start=True, stop=True)
         weigh(1, 1)
-        quantise_pw(1, 0, HALF)
         quantise_dom(0)
+        quantise_pw(1, 0, HALF)
         quantise_pw(1, HALF, N)
+        for b in (1, 2):
+            for g in range(PASSES):
+                cast_dom(b, g)
         dv = [None] * E_BLOCKS
         dv[0] = product(0, 2)
-        for g in range(PASSES):
-            cast_dom(1, g)
         quantise_dom(1)
-        for b in range(E_BLOCKS):
-            if b + 2 < E_BLOCKS:
-                for g in range(PASSES):
-                    cast_dom(b + 2, g)
-                quantise_dom(b + 2)
-            if b + 1 < E_BLOCKS:
-                dv[b + 1] = product(b + 1, 1)
-            scatter(b, dv[b], 2 if b == 0 else 1)
+        quantise_dom(2)
+        last = sb.tile([P, PASSES, P, PACK], BF16, name="dom_grouped_last", tag="dom0_codes", align_bytes=64)
+        dom_grouped.append(last[:])
+        for g in range(PASSES):
+            cast_dom(3, g)
+        dv[1] = product(1, 1)
+        scatter(0, dv[0], 2)
+        quantise_dom(3)
+        dv[2] = product(2, 1)
+        scatter(1, dv[1], 1)
+        dv[3] = product(3, 1)
+        scatter(2, dv[2], 1)
+        scatter(3, dv[3], 1)

@@ -20,7 +20,7 @@ PACK = 4
 PASSES = R // (P * PACK)
 HALVES = 2
 HALF = N // HALVES
-RUN = 4
+RUN = 2
 E_BLOCKS = DV // P
 WINDOWS = 3
 Q_LOADS = [(0, 0, 64), (0, 64, 128), (1, 0, 64), (1, 64, 128)]
@@ -30,8 +30,7 @@ def tile_attend_gat_lse_v_kernel(tc, qT, kT, lse, rw, dom, offs, out):
     nc = tc.nc
     with ExitStack() as ctx:
         sb = ctx.enter_context(tc.tile_pool(name="sb", bufs=1))
-        ps_scores = ctx.enter_context(tc.psum_pool(name="ps_scores", bufs=2))
-        ps_out = ctx.enter_context(tc.psum_pool(name="ps_out", bufs=E_BLOCKS))
+        ps = ctx.enter_context(tc.psum_pool(name="ps", bufs=PASSES * PACK))
 
         def quantise(name, grouped, words, fmt):
             codes = sb.tile([P, words], U32, name=name + "_codes", align_bytes=64)
@@ -42,17 +41,15 @@ def tile_attend_gat_lse_v_kernel(tc, qT, kT, lse, rw, dom, offs, out):
         offsets = sb.tile([P, N // 16], U16, name="offsets")
         lse_sb = sb.tile([P, PASSES, PACK], F32, name="lse_sb")
         rw_sb = sb.tile([P, PASSES, PACK], F32, name="rw_sb")
-        nc.scalar.dma_start(lse_sb[:], lse[0].rearrange("(g p t) o -> p g (t o)", p=P, t=PACK))
-        nc.scalar.dma_start(rw_sb[:], rw[0].rearrange("(g p t) o -> p g (t o)", p=P, t=PACK))
 
         q_rows = qT[0].rearrange("(p j) (g c) -> g p j c", j=PACK, g=PASSES)
         k_rows = kT.rearrange("(p j) c -> j p c", j=PACK)
         dom_rows = dom[0].rearrange("(g p j) e -> g p j e", p=P, j=PACK)
         q_raw = {}
         for g, m0, m1 in Q_LOADS:
-            q_raw[(g, m0)] = sb.tile([P, PACK, (m1 - m0) * PACK], F32, name="q_raw%d_%d" % (g, m0))
+            q_raw[(g, m0)] = sb.tile([P, PACK, (m1 - m0) * PACK], F32, name="q_raw%d_%d" % (g, m0), align_bytes=64)
         k_plane = [sb.tile([P, T], F32, name="k_plane%d" % j) for j in range(PACK)]
-        dom_raw = [sb.tile([P, PACK, DV], F32, name="dom_raw%d" % g) for g in range(PASSES)]
+        dom_raw = {(g, u): sb.tile([P, PACK, DV // 2], F32, name="dom_raw%d%d" % (g, u)) for u in range(2) for g in range(PASSES)}
         nc.sync.dma_start(k_plane[0][:], k_rows[0])
         nc.sync.dma_start(offsets[:], offs)
         nc.sync.dma_start(k_plane[1][:], k_rows[1])
@@ -60,14 +57,22 @@ def tile_attend_gat_lse_v_kernel(tc, qT, kT, lse, rw, dom, offs, out):
         nc.sync.dma_start(k_plane[3][:], k_rows[3])
         for g, m0, m1 in Q_LOADS:
             nc.sync.dma_start(q_raw[(g, m0)][:], q_rows[g][:, :, m0 * PACK : m1 * PACK])
-        for g in range(PASSES):
-            nc.sync.dma_start(dom_raw[g][:], dom_rows[g])
+            if (g, m0) == (0, 0):
+                nc.sync.dma_start(lse_sb[:], lse[0].rearrange("(g p t) o -> p g (t o)", p=P, t=PACK))
+        nc.sync.dma_start(rw_sb[:], rw[0].rearrange("(g p t) o -> p g (t o)", p=P, t=PACK))
+        for u in range(2):
+            for g in range(PASSES):
+                nc.sync.dma_start(dom_raw[(g, u)][:], dom_rows[g][:, :, u * DV // 2 : (u + 1) * DV // 2])
 
         window = [sb.tile([P, T], F32, name="window%d" % b) for b in range(WINDOWS)]
         for b in range(WINDOWS):
-            (nc.vector if b == 0 else nc.gpsimd).memset(window[b][:], 0.0)
+            nc.vector.memset(window[b][:], 0.0)
+        pw_codes = [sb.tile([P, N], U32, name="pw_codes%d" % g, align_bytes=64) for g in range(PASSES)]
+        pw_scales = [sb.tile([P, N], U8, name="pw_scales%d" % g, align_bytes=64) for g in range(PASSES)]
+        nc.vector.memset(pw_codes[1][:, HALF:], 0)
+        nc.vector.memset(pw_scales[1][:, HALF:].bitcast(U32), 0)
         neg_lse = sb.tile([P, PASSES, PACK], F32, name="neg_lse")
-        nc.vector.tensor_scalar(neg_lse[:], lse_sb[:], -1.0, None, op0=MULT)
+        nc.scalar.mul(neg_lse[:], lse_sb[:], -1.0)
 
         q_grouped = {}
         q_mx = [None] * PASSES
@@ -80,8 +85,11 @@ def tile_attend_gat_lse_v_kernel(tc, qT, kT, lse, rw, dom, offs, out):
             src = q_raw[(g, base)][:].rearrange("p j (m t) -> p m j t", t=PACK)
             copy(dst[:, m0:m1], src[:, m0 - base : m1 - base])
 
-        def quantise_q(g):
-            q_mx[g] = quantise("q%d" % g, q_grouped[g][:].rearrange("p t m j -> p (t m j)"), PACK * P, E4M3)
+        def quantise_q(g, tiles):
+            q_mx[g] = []
+            for t in range(0, PACK, tiles):
+                codes, scales = quantise("q%d%d" % (g, t), q_grouped[g][:, t : t + tiles].rearrange("p t m j -> p (t m j)"), tiles * P, E4M3)
+                q_mx[g].extend((codes[:, u * P : (u + 1) * P], scales[:, u * P : (u + 1) * P]) for u in range(tiles))
 
         k_grouped = [sb.tile([P, HALF, PACK], BF16, name="k_grouped%d" % h, align_bytes=64) for h in range(HALVES)]
         for j in range(PACK):
@@ -90,24 +98,26 @@ def tile_attend_gat_lse_v_kernel(tc, qT, kT, lse, rw, dom, offs, out):
                 nc.vector.tensor_copy(k_grouped[h][:, :, j], k_plane[j][:].indirect(entries))
         k_mx = [quantise("k%d" % h, k_grouped[h][:].rearrange("p i j -> p (i j)"), HALF, E4M3) for h in range(HALVES)]
 
-        pw_codes = [sb.tile([P, N], U32, name="pw_codes%d" % g, align_bytes=64) for g in range(PASSES)]
-        pw_scales = [sb.tile([P, N], U8, name="pw_scales%d" % g, align_bytes=64) for g in range(PASSES)]
-        pw = [sb.tile([P, N, PACK], BF16, name="pw%d" % g, align_bytes=64) for g in range(PASSES)]
+        pw = {}
         p32 = {}
+        scores = {}
 
         def probs(g, h):
-            scores = ps_scores.tile([P, PACK, HALF], F32, name="scores")
-            q_codes, q_scales = q_mx[g]
+            if h == 0:
+                scores[g] = [ps.tile([P, N], F32, name="bank") for t in range(PACK)]
+            slots = slice(h * HALF, (h + 1) * HALF)
             k_codes, k_scales = k_mx[h]
             for t in range(PACK):
-                m = slice(t * P, (t + 1) * P)
-                nc.tensor.matmul_mx(out=scores[:, t, :], lhsT=q_codes[:, m].bitcast(E4M3), lhsT_scale=q_scales[:, m],
+                q_codes, q_scales = q_mx[g][t]
+                nc.tensor.matmul_mx(out=scores[g][t][:, slots], lhsT=q_codes.bitcast(E4M3), lhsT_scale=q_scales,
                                     rhs=k_codes[:].bitcast(E4M3), rhs_scale=k_scales[:], start=True, stop=True)
             p32[(g, h)] = sb.tile([P, PACK, HALF], F32, name="p32_%d%d" % (g, h), align_bytes=64)
             for t in range(PACK):
-                nc.scalar.activation(p32[(g, h)][:, t, :], scores[:, t, :], EXP, bias=neg_lse[:, g, t : t + 1])
+                nc.scalar.activation(p32[(g, h)][:, t, :], scores[g][t][:, slots], EXP, bias=neg_lse[:, g, t : t + 1])
 
         def weigh(g, h):
+            if h == 0:
+                pw[g] = sb.tile([P, N, PACK], BF16, name="pw%d" % g, tag="q_raw1_64" if g == 0 else "pw1", align_bytes=64)
             gate = rw_sb[:, g, :].unsqueeze(1).unsqueeze(3).to_broadcast([P, HALF // RUN, PACK, RUN])
             nc.vector.tensor_tensor(pw[g][:, h * HALF : (h + 1) * HALF, :].rearrange("p (c i) t -> p c t i", i=RUN),
                                     p32[(g, h)][:].rearrange("p t (c i) -> p c t i", i=RUN), gate, MULT)
@@ -116,83 +126,77 @@ def tile_attend_gat_lse_v_kernel(tc, qT, kT, lse, rw, dom, offs, out):
             nc.vector.quantize_mx(out=pw_codes[g][:, i0:i1].bitcast(E4M3), scales=pw_scales[g][:, i0:i1],
                                   in_=pw[g][:, i0:i1, :].rearrange("p i t -> p (i t)"))
 
-        dom_grouped = []
+        dom_grouped = {}
         dom_mx = [None] * E_BLOCKS
 
         def cast_dom(b, g):
-            if not dom_grouped:
-                whole = sb.tile([P, E_BLOCKS - 1, PASSES, P, PACK], BF16, name="dom_grouped", tag="p32_01", align_bytes=64)
-                dom_grouped.extend(whole[:, blk] for blk in range(E_BLOCKS - 1))
+            if b == 0 and g == 0:
+                first = sb.tile([P, PASSES, P, PACK], BF16, name="dom_first", tag="q_grouped", align_bytes=64)
+                dom_grouped[0] = first[:]
+            if b == 1 and g == 0:
+                rest = sb.tile([P, E_BLOCKS - 1, PASSES, P, PACK], BF16, name="dom_rest", tag="p32_10", align_bytes=64)
+                for blk in range(1, E_BLOCKS):
+                    dom_grouped[blk] = rest[:, blk - 1]
             nc.scalar.copy(dom_grouped[b][:, g].rearrange("p (c i) j -> p c j i", i=RUN),
-                           dom_raw[g][:, :, b * P : (b + 1) * P].rearrange("p j (c i) -> p c j i", i=RUN))
+                           dom_raw[(g, b // 2)][:, :, b % 2 * P : (b % 2 + 1) * P].rearrange("p j (c i) -> p c j i", i=RUN))
 
         def quantise_dom(b):
             dom_mx[b] = quantise("dom%d" % b, dom_grouped[b].rearrange("p g e j -> p (g e j)"), PASSES * P, E5M2)
 
-        def product(b, pieces):
+        def product(b, i0, i1):
             d_codes, d_scales = dom_mx[b]
-            acc = ps_out.tile([P, N], F32, name="acc")
-            for g in range(PASSES):
+            acc = ps.tile([P, N], F32, name="bank")
+            for n, g in enumerate(reversed(range(PASSES))):
                 m = slice(g * P, (g + 1) * P)
                 nc.tensor.matmul_mx(out=acc[:], lhsT=d_codes[:, m].bitcast(E5M2), lhsT_scale=d_scales[:, m],
                                     rhs=pw_codes[g][:].bitcast(E4M3), rhs_scale=pw_scales[g][:],
-                                    start=(g == 0), stop=(g == PASSES - 1))
-            dv = sb.tile([P, N], F32, name="dv%d" % b)
-            width = N // pieces
-            for u in range(pieces):
-                nc.scalar.copy(dv[:, u * width : (u + 1) * width], acc[:, u * width : (u + 1) * width])
+                                    start=(n == 0), stop=(n == PASSES - 1))
+            dv = sb.tile([P, i1 - i0], F32, name="dv%d_%d" % (b, i0))
+            nc.scalar.copy(dv[:], acc[:, i0:i1])
             return dv
 
-        def scatter(b, dv, pieces):
-            width = N // pieces
+        def scatter(b, dv, i0, i1):
             win = window[b % WINDOWS]
-            for u in range(pieces):
-                nc.vector.tensor_copy(win[:].indirect(offsets[:, u * width // 16 : (u + 1) * width // 16]),
-                                      dv[:, u * width : (u + 1) * width])
-            nc.sync.dma_start(out[b * P : (b + 1) * P, :], win[:])
+            nc.vector.tensor_copy(win[:].indirect(offsets[:, i0 // 16 : i1 // 16]), dv[:])
+            if i1 == N:
+                nc.sync.dma_start(out[b * P : (b + 1) * P, :], win[:])
 
         cast_q(nc.scalar.copy, 0, 0, 64)
         cast_q(nc.vector.tensor_copy, 0, 64, 104)
         cast_q(nc.scalar.copy, 0, 104, P)
-        quantise_q(0)
+        quantise_q(0, 1)
         probs(0, 0)
         cast_q(nc.vector.tensor_copy, 1, 0, 64)
         cast_q(nc.vector.tensor_copy, 1, 64, P)
-        quantise_q(1)
+        quantise_q(1, 2)
         probs(0, 1)
         weigh(0, 0)
         probs(1, 0)
         weigh(0, 1)
-        quantise_pw(0, 0, HALF)
-        probs(1, 1)
         cast_dom(0, 0)
         cast_dom(0, 1)
+        quantise_pw(0, 0, HALF)
         weigh(1, 0)
         quantise_pw(0, HALF, N)
-        warm = ps_scores.tile([P, PACK, HALF], F32, name="scores")
-        for u in range(3):
-            nc.tensor.matmul_mx(out=warm[:, 0:2, :].rearrange("p a i -> p (a i)"), lhsT=q_mx[1][0][:, 0:P].bitcast(E4M3), lhsT_scale=q_mx[1][1][:, 0:P],
-                                rhs=pw_codes[0][:].bitcast(E4M3), rhs_scale=pw_scales[0][:], start=True, stop=True)
-        weigh(1, 1)
-        quantise_dom(0)
         quantise_pw(1, 0, HALF)
-        quantise_pw(1, HALF, N)
-        for b in (1, 2):
-            for g in range(PASSES):
-                cast_dom(b, g)
-        dv = [None] * E_BLOCKS
-        dv[0] = product(0, 2)
+        quantise_dom(0)
+        probs(1, 1)
+        for g in range(PASSES):
+            cast_dom(1, g)
+        early = product(0, 0, HALF)
+        weigh(1, 1)
         quantise_dom(1)
+        quantise_pw(1, HALF, N)
+        scatter(0, early, 0, HALF)
+        for g in range(PASSES):
+            cast_dom(2, g)
+        late = product(0, HALF, N)
         quantise_dom(2)
-        last = sb.tile([P, PASSES, P, PACK], BF16, name="dom_grouped_last", tag="dom0_codes", align_bytes=64)
-        dom_grouped.append(last[:])
+        dv = [None, product(1, 0, N)]
+        scatter(0, late, HALF, N)
         for g in range(PASSES):
             cast_dom(3, g)
-        dv[1] = product(1, 1)
-        scatter(0, dv[0], 2)
         quantise_dom(3)
-        dv[2] = product(2, 1)
-        scatter(1, dv[1], 1)
-        dv[3] = product(3, 1)
-        scatter(2, dv[2], 1)
-        scatter(3, dv[3], 1)
+        dv.extend(product(b, 0, N) for b in (2, 3))
+        for b in range(1, E_BLOCKS):
+            scatter(b, dv[b], 0, N)

@@ -20,7 +20,7 @@ PACK = 4
 PASSES = R // (P * PACK)
 HALVES = 2
 HALF = N // HALVES
-RUN = 2
+RUN = 4
 E_BLOCKS = DV // P
 WINDOWS = 3
 Q_LOADS = [(0, 0, 64), (0, 64, 128), (1, 0, 64), (1, 64, 128)]
@@ -50,6 +50,7 @@ def tile_attend_gat_lse_v_kernel(tc, qT, kT, lse, rw, dom, offs, out):
             q_raw[(g, m0)] = sb.tile([P, PACK, (m1 - m0) * PACK], F32, name="q_raw%d_%d" % (g, m0), align_bytes=64)
         k_plane = [sb.tile([P, T], F32, name="k_plane%d" % j) for j in range(PACK)]
         dom_raw = {(g, u): sb.tile([P, PACK, DV // 2], F32, name="dom_raw%d%d" % (g, u)) for u in range(2) for g in range(PASSES)}
+        nc.scalar.dma_start(lse_sb[:], lse[0].rearrange("(g p t) o -> p g (t o)", p=P, t=PACK))
         nc.sync.dma_start(k_plane[0][:], k_rows[0])
         nc.sync.dma_start(offsets[:], offs)
         nc.sync.dma_start(k_plane[1][:], k_rows[1])
@@ -57,8 +58,6 @@ def tile_attend_gat_lse_v_kernel(tc, qT, kT, lse, rw, dom, offs, out):
         nc.sync.dma_start(k_plane[3][:], k_rows[3])
         for g, m0, m1 in Q_LOADS:
             nc.sync.dma_start(q_raw[(g, m0)][:], q_rows[g][:, :, m0 * PACK : m1 * PACK])
-            if (g, m0) == (0, 0):
-                nc.sync.dma_start(lse_sb[:], lse[0].rearrange("(g p t) o -> p g (t o)", p=P, t=PACK))
         nc.sync.dma_start(rw_sb[:], rw[0].rearrange("(g p t) o -> p g (t o)", p=P, t=PACK))
         for u in range(2):
             for g in range(PASSES):
@@ -158,8 +157,11 @@ def tile_attend_gat_lse_v_kernel(tc, qT, kT, lse, rw, dom, offs, out):
         def scatter(b, dv, i0, i1):
             win = window[b % WINDOWS]
             nc.vector.tensor_copy(win[:].indirect(offsets[:, i0 // 16 : i1 // 16]), dv[:])
-            if i1 == N:
+            if i1 == N and b + 1 < E_BLOCKS:
                 nc.sync.dma_start(out[b * P : (b + 1) * P, :], win[:])
+            elif i1 == N:
+                nc.sync.dma_start(out[b * P : (b + 1) * P, : T // 2], win[:, : T // 2])
+                nc.scalar.dma_start(out[b * P : (b + 1) * P, T // 2 :], win[:, T // 2 :])
 
         cast_q(nc.scalar.copy, 0, 0, 64)
         cast_q(nc.vector.tensor_copy, 0, 64, 104)

@@ -1,6 +1,7 @@
 from contextlib import ExitStack
 
 import concourse.mybir as mybir
+from concourse.masks import make_identity
 
 N, T, D, DV, R = 512, 2048, 512, 512, 1024
 FLOPS = 2 * D * R * N + 2 * R * DV * N
@@ -13,6 +14,7 @@ U8 = mybir.dt.uint8
 E4M3 = mybir.dt.float8_e4m3fn_x4
 E5M2 = mybir.dt.float8_e5m2_x4
 EXP = mybir.ActivationFunctionType.Exp
+COPY = mybir.ActivationFunctionType.Copy
 MULT = mybir.AluOpType.mult
 
 P = 128
@@ -30,7 +32,8 @@ def tile_attend_gat_lse_v_kernel(tc, qT, kT, lse, rw, dom, offs, out):
     nc = tc.nc
     with ExitStack() as ctx:
         sb = ctx.enter_context(tc.tile_pool(name="sb", bufs=1))
-        ps = ctx.enter_context(tc.psum_pool(name="ps", bufs=PASSES * PACK))
+        ps = ctx.enter_context(tc.psum_pool(name="ps", bufs=PASSES * PACK - 1))
+        ps_gate = ctx.enter_context(tc.psum_pool(name="ps_gate", bufs=1))
 
         def quantise(name, grouped, words, fmt):
             codes = sb.tile([P, words], U32, name=name + "_codes", align_bytes=64)
@@ -51,6 +54,7 @@ def tile_attend_gat_lse_v_kernel(tc, qT, kT, lse, rw, dom, offs, out):
         k_plane = [sb.tile([P, T], F32, name="k_plane%d" % j) for j in range(PACK)]
         dom_raw = {(g, u): sb.tile([P, PACK, DV // 2], F32, name="dom_raw%d%d" % (g, u)) for u in range(2) for g in range(PASSES)}
         nc.scalar.dma_start(lse_sb[:], lse[0].rearrange("(g p t) o -> p g (t o)", p=P, t=PACK))
+        nc.scalar.dma_start(rw_sb[:], rw[0].rearrange("(g p t) o -> p g (t o)", p=P, t=PACK))
         nc.sync.dma_start(k_plane[0][:], k_rows[0])
         nc.sync.dma_start(offsets[:], offs)
         nc.sync.dma_start(k_plane[1][:], k_rows[1])
@@ -58,7 +62,6 @@ def tile_attend_gat_lse_v_kernel(tc, qT, kT, lse, rw, dom, offs, out):
         nc.sync.dma_start(k_plane[3][:], k_rows[3])
         for g, m0, m1 in Q_LOADS:
             nc.sync.dma_start(q_raw[(g, m0)][:], q_rows[g][:, :, m0 * PACK : m1 * PACK])
-        nc.sync.dma_start(rw_sb[:], rw[0].rearrange("(g p t) o -> p g (t o)", p=P, t=PACK))
         for u in range(2):
             for g in range(PASSES):
                 nc.sync.dma_start(dom_raw[(g, u)][:], dom_rows[g][:, :, u * DV // 2 : (u + 1) * DV // 2])
@@ -68,8 +71,18 @@ def tile_attend_gat_lse_v_kernel(tc, qT, kT, lse, rw, dom, offs, out):
             nc.vector.memset(window[b][:], 0.0)
         pw_codes = [sb.tile([P, N], U32, name="pw_codes%d" % g, align_bytes=64) for g in range(PASSES)]
         pw_scales = [sb.tile([P, N], U8, name="pw_scales%d" % g, align_bytes=64) for g in range(PASSES)]
-        nc.vector.memset(pw_codes[1][:, HALF:], 0)
-        nc.vector.memset(pw_scales[1][:, HALF:].bitcast(U32), 0)
+        for g in range(PASSES):
+            nc.vector.memset(pw_codes[g][:, HALF:], 0)
+            nc.vector.memset(pw_scales[g][:, HALF:].bitcast(U32), 0)
+        identity = sb.tile([P, P], F32, name="identity")
+        make_identity(nc, identity[:])
+        rw_wide = sb.tile([P, P // 8, 8], F32, name="rw_wide")
+        nc.scalar.copy(rw_wide[:], rw_sb[:].rearrange("p g t -> p (g t)").unsqueeze(1).to_broadcast([P, P // 8, 8]))
+        gate_bank = ps_gate.tile([P, 2, P], F32, name="gate_bank")
+        nc.tensor.transpose(gate_bank[:, 0, :], rw_wide[:].rearrange("p a x -> p (a x)"), identity[:])
+        rw_turned = sb.tile([P, P], F32, name="rw_turned")
+        nc.scalar.copy(rw_turned[:], gate_bank[:, 0, :])
+        nc.tensor.transpose(gate_bank[:, 1, :], rw_turned[:], identity[:])
         neg_lse = sb.tile([P, PASSES, PACK], F32, name="neg_lse")
         nc.scalar.mul(neg_lse[:], lse_sb[:], -1.0)
 
@@ -117,9 +130,19 @@ def tile_attend_gat_lse_v_kernel(tc, qT, kT, lse, rw, dom, offs, out):
         def weigh(g, h):
             if h == 0:
                 pw[g] = sb.tile([P, N, PACK], BF16, name="pw%d" % g, tag="q_raw1_64" if g == 0 else "pw1", align_bytes=64)
-            gate = rw_sb[:, g, :].unsqueeze(1).unsqueeze(3).to_broadcast([P, HALF // RUN, PACK, RUN])
+            gate = gate_bank[:, 1, g * PACK : (g + 1) * PACK].unsqueeze(1).unsqueeze(3).to_broadcast([P, HALF // RUN, PACK, RUN])
             nc.vector.tensor_tensor(pw[g][:, h * HALF : (h + 1) * HALF, :].rearrange("p (c i) t -> p c t i", i=RUN),
                                     p32[(g, h)][:].rearrange("p t (c i) -> p c t i", i=RUN), gate, MULT)
+
+        def weigh_on_scalar(g, h):
+            flat = sb.tile([P, PACK, HALF], BF16, name="pw_flat")
+            for t in range(PACK):
+                nc.scalar.activation(flat[:, t, :], p32[(g, h)][:, t, :], COPY, scale=rw_sb[:, g, t : t + 1])
+            return flat
+
+        def interleave(g, h, flat):
+            nc.vector.tensor_copy(pw[g][:, h * HALF : (h + 1) * HALF, :].rearrange("p (c i) t -> p c t i", i=RUN),
+                                  flat[:].rearrange("p t (c i) -> p c t i", i=RUN))
 
         def quantise_pw(g, i0, i1):
             nc.vector.quantize_mx(out=pw_codes[g][:, i0:i1].bitcast(E4M3), scales=pw_scales[g][:, i0:i1],
@@ -133,11 +156,15 @@ def tile_attend_gat_lse_v_kernel(tc, qT, kT, lse, rw, dom, offs, out):
                 first = sb.tile([P, PASSES, P, PACK], BF16, name="dom_first", tag="q_grouped", align_bytes=64)
                 dom_grouped[0] = first[:]
             if b == 1 and g == 0:
-                rest = sb.tile([P, E_BLOCKS - 1, PASSES, P, PACK], BF16, name="dom_rest", tag="p32_10", align_bytes=64)
+                rest = sb.tile([P, E_BLOCKS - 1, PASSES, P, PACK], BF16, name="dom_rest", tag="p32_11", align_bytes=64)
                 for blk in range(1, E_BLOCKS):
                     dom_grouped[blk] = rest[:, blk - 1]
-            nc.scalar.copy(dom_grouped[b][:, g].rearrange("p (c i) j -> p c j i", i=RUN),
-                           dom_raw[(g, b // 2)][:, :, b % 2 * P : (b % 2 + 1) * P].rearrange("p j (c i) -> p c j i", i=RUN))
+            src = dom_raw[(g, b // 2)][:, :, b % 2 * P : (b % 2 + 1) * P]
+            if b == 0:
+                nc.gpsimd.tensor_copy(dom_grouped[b][:, g], src.rearrange("p j e -> p e j"))
+            else:
+                nc.scalar.copy(dom_grouped[b][:, g].rearrange("p (c i) j -> p c j i", i=RUN),
+                               src.rearrange("p j (c i) -> p c j i", i=RUN))
 
         def quantise_dom(b):
             dom_mx[b] = quantise("dom%d" % b, dom_grouped[b].rearrange("p g e j -> p (g e j)"), PASSES * P, E5M2)
@@ -145,7 +172,7 @@ def tile_attend_gat_lse_v_kernel(tc, qT, kT, lse, rw, dom, offs, out):
         def product(b, i0, i1):
             d_codes, d_scales = dom_mx[b]
             acc = ps.tile([P, N], F32, name="bank")
-            for n, g in enumerate(reversed(range(PASSES))):
+            for n, g in enumerate(range(PASSES) if i1 == N else reversed(range(PASSES))):
                 m = slice(g * P, (g + 1) * P)
                 nc.tensor.matmul_mx(out=acc[:], lhsT=d_codes[:, m].bitcast(E5M2), lhsT_scale=d_scales[:, m],
                                     rhs=pw_codes[g][:].bitcast(E4M3), rhs_scale=pw_scales[g][:],
@@ -157,11 +184,8 @@ def tile_attend_gat_lse_v_kernel(tc, qT, kT, lse, rw, dom, offs, out):
         def scatter(b, dv, i0, i1):
             win = window[b % WINDOWS]
             nc.vector.tensor_copy(win[:].indirect(offsets[:, i0 // 16 : i1 // 16]), dv[:])
-            if i1 == N and b + 1 < E_BLOCKS:
+            if i1 == N:
                 nc.sync.dma_start(out[b * P : (b + 1) * P, :], win[:])
-            elif i1 == N:
-                nc.sync.dma_start(out[b * P : (b + 1) * P, : T // 2], win[:, : T // 2])
-                nc.scalar.dma_start(out[b * P : (b + 1) * P, T // 2 :], win[:, T // 2 :])
 
         cast_q(nc.scalar.copy, 0, 0, 64)
         cast_q(nc.vector.tensor_copy, 0, 64, 104)
@@ -175,30 +199,31 @@ def tile_attend_gat_lse_v_kernel(tc, qT, kT, lse, rw, dom, offs, out):
         weigh(0, 0)
         probs(1, 0)
         weigh(0, 1)
-        cast_dom(0, 0)
-        cast_dom(0, 1)
-        quantise_pw(0, 0, HALF)
-        weigh(1, 0)
-        quantise_pw(0, HALF, N)
-        quantise_pw(1, 0, HALF)
-        quantise_dom(0)
+        for g in range(PASSES):
+            cast_dom(0, g)
         probs(1, 1)
+        flat = weigh_on_scalar(1, 1)
+        weigh(1, 0)
+        quantise_dom(0)
+        quantise_pw(1, 0, HALF)
+        quantise_pw(0, 0, HALF)
         for g in range(PASSES):
             cast_dom(1, g)
         early = product(0, 0, HALF)
-        weigh(1, 1)
-        quantise_dom(1)
+        interleave(1, 1, flat)
+        quantise_pw(0, HALF, N)
         quantise_pw(1, HALF, N)
+        quantise_dom(1)
         scatter(0, early, 0, HALF)
         for g in range(PASSES):
             cast_dom(2, g)
         late = product(0, HALF, N)
         quantise_dom(2)
-        dv = [None, product(1, 0, N)]
         scatter(0, late, HALF, N)
         for g in range(PASSES):
             cast_dom(3, g)
+        dv = product(1, 0, N)
         quantise_dom(3)
-        dv.extend(product(b, 0, N) for b in (2, 3))
-        for b in range(1, E_BLOCKS):
-            scatter(b, dv[b], 0, N)
+        scatter(1, dv, 0, N)
+        for b in range(2, E_BLOCKS):
+            scatter(b, product(b, 0, N), 0, N)

@@ -202,28 +202,32 @@ def tile_attend_gat_lse_v_kernel(tc, qT, kT, lse, rw, dom, offs, out):
         for g in range(PASSES):
             cast_dom(0, g)
         probs(1, 1)
+        for t in range(PACK):
+            nc.tensor.matmul_mx(out=scores[1][t][:, :HALF], lhsT=q_mx[1][t][0].bitcast(E4M3), lhsT_scale=q_mx[1][t][1],
+                                rhs=k_mx[0][0][:].bitcast(E4M3), rhs_scale=k_mx[0][1][:], start=True, stop=True)
         flat = weigh_on_scalar(1, 1)
         weigh(1, 0)
         quantise_dom(0)
         quantise_pw(1, 0, HALF)
         quantise_pw(0, 0, HALF)
-        for g in range(PASSES):
-            cast_dom(1, g)
+        cast_dom(1, 0)
         early = product(0, 0, HALF)
+        cast_dom(1, 1)
         interleave(1, 1, flat)
         quantise_pw(0, HALF, N)
         quantise_pw(1, HALF, N)
-        quantise_dom(1)
         scatter(0, early, 0, HALF)
-        for g in range(PASSES):
-            cast_dom(2, g)
         late = product(0, HALF, N)
-        quantise_dom(2)
+        quantise_dom(1)
         scatter(0, late, HALF, N)
         for g in range(PASSES):
-            cast_dom(3, g)
+            cast_dom(2, g)
         dv = product(1, 0, N)
-        quantise_dom(3)
+        quantise_dom(2)
         scatter(1, dv, 0, N)
-        for b in range(2, E_BLOCKS):
-            scatter(b, product(b, 0, N), 0, N)
+        for g in range(PASSES):
+            cast_dom(3, g)
+        dv = product(2, 0, N)
+        quantise_dom(3)
+        scatter(2, dv, 0, N)
+        scatter(3, product(3, 0, N), 0, N)

@@ -52,7 +52,8 @@ def tile_attend_gat_lse_v_kernel(tc, qT, kT, lse, rw, dom, offs, out):
         for g, m0, m1 in Q_LOADS:
             q_raw[(g, m0)] = sb.tile([P, PACK, (m1 - m0) * PACK], F32, name="q_raw%d_%d" % (g, m0), align_bytes=64)
         k_plane = [sb.tile([P, T], F32, name="k_plane%d" % j) for j in range(PACK)]
-        dom_raw = {(g, u): sb.tile([P, PACK, DV // 2], F32, name="dom_raw%d%d" % (g, u)) for u in range(2) for g in range(PASSES)}
+        dom_cuts = [(0, P), (P, DV)]
+        dom_raw = {(g, e0): sb.tile([P, PACK, e1 - e0], F32, name="dom_raw%d_%d" % (g, e0)) for e0, e1 in dom_cuts for g in range(PASSES)}
         nc.scalar.dma_start(lse_sb[:], lse[0].rearrange("(g p t) o -> p g (t o)", p=P, t=PACK))
         nc.scalar.dma_start(rw_sb[:], rw[0].rearrange("(g p t) o -> p g (t o)", p=P, t=PACK))
         nc.sync.dma_start(k_plane[0][:], k_rows[0])
@@ -62,9 +63,9 @@ def tile_attend_gat_lse_v_kernel(tc, qT, kT, lse, rw, dom, offs, out):
         nc.sync.dma_start(k_plane[3][:], k_rows[3])
         for g, m0, m1 in Q_LOADS:
             nc.sync.dma_start(q_raw[(g, m0)][:], q_rows[g][:, :, m0 * PACK : m1 * PACK])
-        for u in range(2):
+        for e0, e1 in dom_cuts:
             for g in range(PASSES):
-                nc.sync.dma_start(dom_raw[(g, u)][:], dom_rows[g][:, :, u * DV // 2 : (u + 1) * DV // 2])
+                nc.sync.dma_start(dom_raw[(g, e0)][:], dom_rows[g][:, :, e0:e1])
 
         window = [sb.tile([P, T], F32, name="window%d" % b) for b in range(WINDOWS)]
         for b in range(WINDOWS):
@@ -159,7 +160,7 @@ def tile_attend_gat_lse_v_kernel(tc, qT, kT, lse, rw, dom, offs, out):
                 rest = sb.tile([P, E_BLOCKS - 1, PASSES, P, PACK], BF16, name="dom_rest", tag="p32_11", align_bytes=64)
                 for blk in range(1, E_BLOCKS):
                     dom_grouped[blk] = rest[:, blk - 1]
-            src = dom_raw[(g, b // 2)][:, :, b % 2 * P : (b % 2 + 1) * P]
+            src = dom_raw[(g, 0)][:] if b == 0 else dom_raw[(g, P)][:, :, (b - 1) * P : b * P]
             if b == 0:
                 nc.gpsimd.tensor_copy(dom_grouped[b][:, g], src.rearrange("p j e -> p e j"))
             else:

@@ -23,6 +23,7 @@ PASSES = R // (P * PACK)
 HALVES = 2
 HALF = N // HALVES
 RUN = 4
+SCALAR_SLOTS = 160
 E_BLOCKS = DV // P
 WINDOWS = 3
 Q_LOADS = [(0, 0, 64), (0, 64, 128), (1, 0, 64), (1, 64, 128)]
@@ -90,13 +91,13 @@ def tile_attend_gat_lse_v_kernel(tc, qT, kT, lse, rw, dom, offs, out):
         q_grouped = {}
         q_mx = [None] * PASSES
 
-        def cast_q(copy, g, m0, m1):
+        def cast_q(copy, g, m0, m1, t0=0, t1=PACK):
             base = max(l0 for lg, l0, l1 in Q_LOADS if lg == g and l0 <= m0)
             if g not in q_grouped:
-                q_grouped[g] = sb.tile([P, PACK, P, PACK], BF16, name="q_grouped", align_bytes=64)
+                q_grouped[g] = sb.tile([P, PACK, P, PACK], BF16, name="q_grouped", tag="q_grouped" if g == 0 else "q_raw0_64", align_bytes=64)
             dst = q_grouped[g][:].rearrange("p t m j -> p m j t")
             src = q_raw[(g, base)][:].rearrange("p j (m t) -> p m j t", t=PACK)
-            copy(dst[:, m0:m1], src[:, m0 - base : m1 - base])
+            copy(dst[:, m0:m1, :, t0:t1], src[:, m0 - base : m1 - base, :, t0:t1])
 
         def quantise_q(g, tiles):
             q_mx[g] = []
@@ -128,21 +129,21 @@ def tile_attend_gat_lse_v_kernel(tc, qT, kT, lse, rw, dom, offs, out):
             for t in range(PACK):
                 nc.scalar.activation(p32[(g, h)][:, t, :], scores[g][t][:, slots], EXP, bias=neg_lse[:, g, t : t + 1])
 
-        def weigh(g, h):
+        def weigh(g, h, skip=0):
             if h == 0:
                 pw[g] = sb.tile([P, N, PACK], BF16, name="pw%d" % g, tag="q_raw1_64" if g == 0 else "pw1", align_bytes=64)
-            gate = gate_bank[:, 1, g * PACK : (g + 1) * PACK].unsqueeze(1).unsqueeze(3).to_broadcast([P, HALF // RUN, PACK, RUN])
-            nc.vector.tensor_tensor(pw[g][:, h * HALF : (h + 1) * HALF, :].rearrange("p (c i) t -> p c t i", i=RUN),
-                                    p32[(g, h)][:].rearrange("p t (c i) -> p c t i", i=RUN), gate, MULT)
+            gate = gate_bank[:, 1, g * PACK : (g + 1) * PACK].unsqueeze(1).unsqueeze(3).to_broadcast([P, (HALF - skip) // RUN, PACK, RUN])
+            nc.vector.tensor_tensor(pw[g][:, h * HALF + skip : (h + 1) * HALF, :].rearrange("p (c i) t -> p c t i", i=RUN),
+                                    p32[(g, h)][:, :, skip:].rearrange("p t (c i) -> p c t i", i=RUN), gate, MULT)
 
         def weigh_on_scalar(g, h):
-            flat = sb.tile([P, PACK, HALF], BF16, name="pw_flat")
+            flat = sb.tile([P, PACK, SCALAR_SLOTS], BF16, name="pw_flat")
             for t in range(PACK):
-                nc.scalar.activation(flat[:, t, :], p32[(g, h)][:, t, :], COPY, scale=rw_sb[:, g, t : t + 1])
+                nc.scalar.activation(flat[:, t, :], p32[(g, h)][:, t, :SCALAR_SLOTS], COPY, scale=rw_sb[:, g, t : t + 1])
             return flat
 
         def interleave(g, h, flat):
-            nc.vector.tensor_copy(pw[g][:, h * HALF : (h + 1) * HALF, :].rearrange("p (c i) t -> p c t i", i=RUN),
+            nc.vector.tensor_copy(pw[g][:, h * HALF : h * HALF + SCALAR_SLOTS, :].rearrange("p (c i) t -> p c t i", i=RUN),
                                   flat[:].rearrange("p t (c i) -> p c t i", i=RUN))
 
         def quantise_pw(g, i0, i1):
@@ -154,10 +155,10 @@ def tile_attend_gat_lse_v_kernel(tc, qT, kT, lse, rw, dom, offs, out):
 
         def cast_dom(b, g):
             if b == 0 and g == 0:
-                first = sb.tile([P, PASSES, P, PACK], BF16, name="dom_first", tag="q_grouped", align_bytes=64)
+                first = sb.tile([P, PASSES, P, PACK], BF16, name="dom_first", tag="q_raw0_64", align_bytes=64)
                 dom_grouped[0] = first[:]
             if b == 1 and g == 0:
-                rest = sb.tile([P, E_BLOCKS - 1, PASSES, P, PACK], BF16, name="dom_rest", tag="p32_11", align_bytes=64)
+                rest = sb.tile([P, E_BLOCKS - 1, PASSES, P, PACK], BF16, name="dom_rest", tag="p32_10", align_bytes=64)
                 for blk in range(1, E_BLOCKS):
                     dom_grouped[blk] = rest[:, blk - 1]
             src = dom_raw[(g, 0)][:] if b == 0 else dom_raw[(g, P)][:, :, (b - 1) * P : b * P]
@@ -189,12 +190,14 @@ def tile_attend_gat_lse_v_kernel(tc, qT, kT, lse, rw, dom, offs, out):
                 nc.sync.dma_start(out[b * P : (b + 1) * P, :], win[:])
 
         cast_q(nc.scalar.copy, 0, 0, 64)
-        cast_q(nc.vector.tensor_copy, 0, 64, 104)
-        cast_q(nc.scalar.copy, 0, 104, P)
+        cast_q(nc.vector.tensor_copy, 0, 64, P, 0, 2)
+        cast_q(nc.vector.tensor_copy, 0, 64, 80, 2, PACK)
+        cast_q(nc.scalar.copy, 0, 80, P, 2, PACK)
         quantise_q(0, 1)
         probs(0, 0)
         cast_q(nc.vector.tensor_copy, 1, 0, 64)
-        cast_q(nc.vector.tensor_copy, 1, 64, P)
+        cast_q(nc.vector.tensor_copy, 1, 64, P, 0, 2)
+        cast_q(nc.vector.tensor_copy, 1, 64, P, 2, PACK)
         quantise_q(1, 2)
         probs(0, 1)
         weigh(0, 0)
@@ -211,6 +214,7 @@ def tile_attend_gat_lse_v_kernel(tc, qT, kT, lse, rw, dom, offs, out):
         quantise_dom(0)
         quantise_pw(1, 0, HALF)
         quantise_pw(0, 0, HALF)
+        weigh(1, 1, SCALAR_SLOTS)
         cast_dom(1, 0)
         early = product(0, 0, HALF)
         cast_dom(1, 1)

@@ -23,7 +23,7 @@ PASSES = R // (P * PACK)
 HALVES = 2
 HALF = N // HALVES
 RUN = 4
-SCALAR_SLOTS = 160
+SCALAR_SLOTS = 176
 E_BLOCKS = DV // P
 WINDOWS = 3
 Q_LOADS = [(0, 0, 64), (0, 64, 128), (1, 0, 64), (1, 64, 128)]
@@ -71,11 +71,11 @@ def tile_attend_gat_lse_v_kernel(tc, qT, kT, lse, rw, dom, offs, out):
         window = [sb.tile([P, T], F32, name="window%d" % b) for b in range(WINDOWS)]
         for b in range(WINDOWS):
             nc.vector.memset(window[b][:], 0.0)
-        pw_codes = [sb.tile([P, N], U32, name="pw_codes%d" % g, align_bytes=64) for g in range(PASSES)]
-        pw_scales = [sb.tile([P, N], U8, name="pw_scales%d" % g, align_bytes=64) for g in range(PASSES)]
+        pw_codes = [sb.tile([P, HALF + N], U32, name="pw_codes%d" % g, align_bytes=64) for g in range(PASSES)]
+        pw_scales = [sb.tile([P, HALF + N], U8, name="pw_scales%d" % g, align_bytes=64) for g in range(PASSES)]
         for g in range(PASSES):
-            nc.vector.memset(pw_codes[g][:, HALF:], 0)
-            nc.vector.memset(pw_scales[g][:, HALF:].bitcast(U32), 0)
+            nc.vector.memset(pw_codes[g][:, :HALF], 0)
+            nc.vector.memset(pw_scales[g][:, :HALF].bitcast(U32), 0)
         identity = sb.tile([P, P], F32, name="identity")
         make_identity(nc, identity[:])
         rw_wide = sb.tile([P, P // 8, 8], F32, name="rw_wide")
@@ -143,11 +143,11 @@ def tile_attend_gat_lse_v_kernel(tc, qT, kT, lse, rw, dom, offs, out):
             return flat
 
         def interleave(g, h, flat):
-            nc.vector.tensor_copy(pw[g][:, h * HALF : h * HALF + SCALAR_SLOTS, :].rearrange("p (c i) t -> p c t i", i=RUN),
-                                  flat[:].rearrange("p t (c i) -> p c t i", i=RUN))
+            nc.scalar.copy(pw[g][:, h * HALF : h * HALF + SCALAR_SLOTS, :].rearrange("p (c i) t -> p c t i", i=RUN),
+                           flat[:].rearrange("p t (c i) -> p c t i", i=RUN))
 
         def quantise_pw(g, i0, i1):
-            nc.vector.quantize_mx(out=pw_codes[g][:, i0:i1].bitcast(E4M3), scales=pw_scales[g][:, i0:i1],
+            nc.vector.quantize_mx(out=pw_codes[g][:, HALF + i0 : HALF + i1].bitcast(E4M3), scales=pw_scales[g][:, HALF + i0 : HALF + i1],
                                   in_=pw[g][:, i0:i1, :].rearrange("p i t -> p (i t)"))
 
         dom_grouped = {}
@@ -158,7 +158,7 @@ def tile_attend_gat_lse_v_kernel(tc, qT, kT, lse, rw, dom, offs, out):
                 first = sb.tile([P, PASSES, P, PACK], BF16, name="dom_first", tag="q_raw0_64", align_bytes=64)
                 dom_grouped[0] = first[:]
             if b == 1 and g == 0:
-                rest = sb.tile([P, E_BLOCKS - 1, PASSES, P, PACK], BF16, name="dom_rest", tag="p32_10", align_bytes=64)
+                rest = sb.tile([P, E_BLOCKS - 1, PASSES, P, PACK], BF16, name="dom_rest", tag="q_raw1_64", align_bytes=64)
                 for blk in range(1, E_BLOCKS):
                     dom_grouped[blk] = rest[:, blk - 1]
             src = dom_raw[(g, 0)][:] if b == 0 else dom_raw[(g, P)][:, :, (b - 1) * P : b * P]
@@ -174,13 +174,14 @@ def tile_attend_gat_lse_v_kernel(tc, qT, kT, lse, rw, dom, offs, out):
         def product(b, i0, i1):
             d_codes, d_scales = dom_mx[b]
             acc = ps.tile([P, N], F32, name="bank")
+            cols = slice(i1 + HALF - N, i1 + HALF)
             for n, g in enumerate(range(PASSES) if i1 == N else reversed(range(PASSES))):
                 m = slice(g * P, (g + 1) * P)
                 nc.tensor.matmul_mx(out=acc[:], lhsT=d_codes[:, m].bitcast(E5M2), lhsT_scale=d_scales[:, m],
-                                    rhs=pw_codes[g][:].bitcast(E4M3), rhs_scale=pw_scales[g][:],
+                                    rhs=pw_codes[g][:, cols].bitcast(E4M3), rhs_scale=pw_scales[g][:, cols],
                                     start=(n == 0), stop=(n == PASSES - 1))
             dv = sb.tile([P, i1 - i0], F32, name="dv%d_%d" % (b, i0))
-            nc.scalar.copy(dv[:], acc[:, i0:i1])
+            nc.scalar.copy(dv[:], acc[:, N - (i1 - i0) :])
             return dv
 
         def scatter(b, dv, i0, i1):
@@ -211,16 +212,16 @@ def tile_attend_gat_lse_v_kernel(tc, qT, kT, lse, rw, dom, offs, out):
                                 rhs=k_mx[0][0][:].bitcast(E4M3), rhs_scale=k_mx[0][1][:], start=True, stop=True)
         flat = weigh_on_scalar(1, 1)
         weigh(1, 0)
+        interleave(1, 1, flat)
         quantise_dom(0)
         quantise_pw(1, 0, HALF)
         quantise_pw(0, 0, HALF)
         weigh(1, 1, SCALAR_SLOTS)
-        cast_dom(1, 0)
         early = product(0, 0, HALF)
-        cast_dom(1, 1)
-        interleave(1, 1, flat)
         quantise_pw(0, HALF, N)
         quantise_pw(1, HALF, N)
+        cast_dom(1, 0)
+        cast_dom(1, 1)
         scatter(0, early, 0, HALF)
         late = product(0, HALF, N)
         quantise_dom(1)

@@ -43,8 +43,8 @@ def tile_attend_gat_lse_v_kernel(tc, qT, kT, lse, rw, dom, offs, out):
             return codes, scales
 
         offsets = sb.tile([P, N // 16], U16, name="offsets")
-        lse_sb = sb.tile([P, PASSES, PACK], F32, name="lse_sb")
-        rw_sb = sb.tile([P, PASSES, PACK], F32, name="rw_sb")
+        rows = sb.tile([P, P * PACK], F32, name="rows")
+        nc.gpsimd.memset(rows[:], 0.0)
 
         q_rows = qT[0].rearrange("(p j) (g c) -> g p j c", j=PACK, g=PASSES)
         k_rows = kT.rearrange("(p j) c -> j p c", j=PACK)
@@ -55,8 +55,8 @@ def tile_attend_gat_lse_v_kernel(tc, qT, kT, lse, rw, dom, offs, out):
         k_plane = [sb.tile([P, T], F32, name="k_plane%d" % j) for j in range(PACK)]
         dom_cuts = [(0, P), (P, DV)]
         dom_raw = {(g, e0): sb.tile([P, PACK, e1 - e0], F32, name="dom_raw%d_%d" % (g, e0)) for e0, e1 in dom_cuts for g in range(PASSES)}
-        nc.scalar.dma_start(lse_sb[:], lse[0].rearrange("(g p t) o -> p g (t o)", p=P, t=PACK))
-        nc.scalar.dma_start(rw_sb[:], rw[0].rearrange("(g p t) o -> p g (t o)", p=P, t=PACK))
+        nc.scalar.dma_start(rows[0:PASSES, :], lse[0].rearrange("(g c) o -> g (c o)", g=PASSES))
+        nc.scalar.dma_start(rows[PASSES : 2 * PASSES, :], rw[0].rearrange("(g c) o -> g (c o)", g=PASSES))
         nc.sync.dma_start(k_plane[0][:], k_rows[0])
         nc.sync.dma_start(offsets[:], offs)
         nc.sync.dma_start(k_plane[1][:], k_rows[1])
@@ -78,15 +78,13 @@ def tile_attend_gat_lse_v_kernel(tc, qT, kT, lse, rw, dom, offs, out):
             nc.vector.memset(pw_scales[g][:, :HALF].bitcast(U32), 0)
         identity = sb.tile([P, P], F32, name="identity")
         make_identity(nc, identity[:])
-        rw_wide = sb.tile([P, P // 8, 8], F32, name="rw_wide")
-        nc.scalar.copy(rw_wide[:], rw_sb[:].rearrange("p g t -> p (g t)").unsqueeze(1).to_broadcast([P, P // 8, 8]))
-        gate_bank = ps_gate.tile([P, 2, P], F32, name="gate_bank")
-        nc.tensor.transpose(gate_bank[:, 0, :], rw_wide[:].rearrange("p a x -> p (a x)"), identity[:])
-        rw_turned = sb.tile([P, P], F32, name="rw_turned")
-        nc.scalar.copy(rw_turned[:], gate_bank[:, 0, :])
-        nc.tensor.transpose(gate_bank[:, 1, :], rw_turned[:], identity[:])
+        gate_bank = ps_gate.tile([P, PACK, P], F32, name="gate_bank")
+        for t in range(PACK):
+            nc.tensor.transpose(gate_bank[:, t, :], rows[:, t : P * PACK : PACK], identity[:])
         neg_lse = sb.tile([P, PASSES, PACK], F32, name="neg_lse")
-        nc.scalar.mul(neg_lse[:], lse_sb[:], -1.0)
+        nc.scalar.mul(neg_lse[:], gate_bank[:, :, 0:PASSES].rearrange("p t g -> p g t"), -1.0)
+        rw_sb = sb.tile([P, PASSES, PACK], F32, name="rw_sb")
+        nc.scalar.copy(rw_sb[:], gate_bank[:, :, PASSES : 2 * PASSES].rearrange("p t g -> p g t"))
 
         q_grouped = {}
         q_mx = [None] * PASSES
@@ -132,7 +130,7 @@ def tile_attend_gat_lse_v_kernel(tc, qT, kT, lse, rw, dom, offs, out):
         def weigh(g, h, skip=0):
             if h == 0:
                 pw[g] = sb.tile([P, N, PACK], BF16, name="pw%d" % g, tag="q_raw1_64" if g == 0 else "pw1", align_bytes=64)
-            gate = gate_bank[:, 1, g * PACK : (g + 1) * PACK].unsqueeze(1).unsqueeze(3).to_broadcast([P, (HALF - skip) // RUN, PACK, RUN])
+            gate = gate_bank[:, :, PASSES + g : PASSES + g + 1].unsqueeze(1).to_broadcast([P, (HALF - skip) // RUN, PACK, RUN])
             nc.vector.tensor_tensor(pw[g][:, h * HALF + skip : (h + 1) * HALF, :].rearrange("p (c i) t -> p c t i", i=RUN),
                                     p32[(g, h)][:, :, skip:].rearrange("p t (c i) -> p c t i", i=RUN), gate, MULT)
 

@@ -45,6 +45,7 @@ def tile_attend_gat_lse_v_kernel(tc, qT, kT, lse, rw, dom, offs, out):
         offsets = sb.tile([P, N // 16], U16, name="offsets")
         rows = sb.tile([P, P * PACK], F32, name="rows")
         nc.gpsimd.memset(rows[:], 0.0)
+        landed = sb.tile([2 * PASSES, P * PACK], F32, name="landed")
 
         q_rows = qT[0].rearrange("(p j) (g c) -> g p j c", j=PACK, g=PASSES)
         k_rows = kT.rearrange("(p j) c -> j p c", j=PACK)
@@ -55,8 +56,8 @@ def tile_attend_gat_lse_v_kernel(tc, qT, kT, lse, rw, dom, offs, out):
         k_plane = [sb.tile([P, T], F32, name="k_plane%d" % j) for j in range(PACK)]
         dom_cuts = [(0, P), (P, DV)]
         dom_raw = {(g, e0): sb.tile([P, PACK, e1 - e0], F32, name="dom_raw%d_%d" % (g, e0)) for e0, e1 in dom_cuts for g in range(PASSES)}
-        nc.scalar.dma_start(rows[0:PASSES, :], lse[0].rearrange("(g c) o -> g (c o)", g=PASSES))
-        nc.scalar.dma_start(rows[PASSES : 2 * PASSES, :], rw[0].rearrange("(g c) o -> g (c o)", g=PASSES))
+        nc.scalar.dma_start(landed[0:PASSES, :], lse[0].rearrange("(g c) o -> g (c o)", g=PASSES))
+        nc.scalar.dma_start(landed[PASSES : 2 * PASSES, :], rw[0].rearrange("(g c) o -> g (c o)", g=PASSES))
         nc.sync.dma_start(k_plane[0][:], k_rows[0])
         nc.sync.dma_start(offsets[:], offs)
         nc.sync.dma_start(k_plane[1][:], k_rows[1])
@@ -78,6 +79,7 @@ def tile_attend_gat_lse_v_kernel(tc, qT, kT, lse, rw, dom, offs, out):
             nc.vector.memset(pw_scales[g][:, :HALF].bitcast(U32), 0)
         identity = sb.tile([P, P], F32, name="identity")
         make_identity(nc, identity[:])
+        nc.scalar.copy(rows[0 : 2 * PASSES, :], landed[:])
         gate_bank = ps_gate.tile([P, PACK, P], F32, name="gate_bank")
         for t in range(PACK):
             nc.tensor.transpose(gate_bank[:, t, :], rows[:, t : P * PACK : PACK], identity[:])

@@ -26,7 +26,9 @@ RUN = 4
 SCALAR_SLOTS = 176
 E_BLOCKS = DV // P
 WINDOWS = 3
-Q_LOADS = [(0, 0, 64), (0, 64, 128), (1, 0, 64), (1, 64, 128)]
+Q_CUT = 96
+Q_SHARE = 40
+Q_LOADS = [(0, 0, P), (1, 0, Q_CUT), (1, Q_CUT, P)]
 
 
 def tile_attend_gat_lse_v_kernel(tc, qT, kT, lse, rw, dom, offs, out):
@@ -94,7 +96,7 @@ def tile_attend_gat_lse_v_kernel(tc, qT, kT, lse, rw, dom, offs, out):
         def cast_q(copy, g, m0, m1, t0=0, t1=PACK):
             base = max(l0 for lg, l0, l1 in Q_LOADS if lg == g and l0 <= m0)
             if g not in q_grouped:
-                q_grouped[g] = sb.tile([P, PACK, P, PACK], BF16, name="q_grouped", tag="q_grouped" if g == 0 else "q_raw0_64", align_bytes=64)
+                q_grouped[g] = sb.tile([P, PACK, P, PACK], BF16, name="q_grouped", tag="q_grouped" if g == 0 else "q_raw0_0", align_bytes=64)
             dst = q_grouped[g][:].rearrange("p t m j -> p m j t")
             src = q_raw[(g, base)][:].rearrange("p j (m t) -> p m j t", t=PACK)
             copy(dst[:, m0:m1, :, t0:t1], src[:, m0 - base : m1 - base, :, t0:t1])
@@ -131,7 +133,7 @@ def tile_attend_gat_lse_v_kernel(tc, qT, kT, lse, rw, dom, offs, out):
 
         def weigh(g, h, skip=0):
             if h == 0:
-                pw[g] = sb.tile([P, N, PACK], BF16, name="pw%d" % g, tag="q_raw1_64" if g == 0 else "pw1", align_bytes=64)
+                pw[g] = sb.tile([P, N, PACK], BF16, name="pw%d" % g, tag="q_raw1_%d" % Q_CUT if g == 0 else "pw1", align_bytes=64)
             gate = gate_bank[:, :, PASSES + g : PASSES + g + 1].unsqueeze(1).to_broadcast([P, (HALF - skip) // RUN, PACK, RUN])
             nc.vector.tensor_tensor(pw[g][:, h * HALF + skip : (h + 1) * HALF, :].rearrange("p (c i) t -> p c t i", i=RUN),
                                     p32[(g, h)][:, :, skip:].rearrange("p t (c i) -> p c t i", i=RUN), gate, MULT)
@@ -155,10 +157,10 @@ def tile_attend_gat_lse_v_kernel(tc, qT, kT, lse, rw, dom, offs, out):
 
         def cast_dom(b, g):
             if b == 0 and g == 0:
-                first = sb.tile([P, PASSES, P, PACK], BF16, name="dom_first", tag="q_raw0_64", align_bytes=64)
+                first = sb.tile([P, PASSES, P, PACK], BF16, name="dom_first", tag="q_raw0_0", align_bytes=64)
                 dom_grouped[0] = first[:]
             if b == 1 and g == 0:
-                rest = sb.tile([P, E_BLOCKS - 1, PASSES, P, PACK], BF16, name="dom_rest", tag="q_raw1_64", align_bytes=64)
+                rest = sb.tile([P, E_BLOCKS - 1, PASSES, P, PACK], BF16, name="dom_rest", tag="q_raw1_%d" % Q_CUT, align_bytes=64)
                 for blk in range(1, E_BLOCKS):
                     dom_grouped[blk] = rest[:, blk - 1]
             src = dom_raw[(g, 0)][:] if b == 0 else dom_raw[(g, P)][:, :, (b - 1) * P : b * P]
@@ -190,15 +192,14 @@ def tile_attend_gat_lse_v_kernel(tc, qT, kT, lse, rw, dom, offs, out):
             if i1 == N:
                 nc.sync.dma_start(out[b * P : (b + 1) * P, :], win[:])
 
-        cast_q(nc.scalar.copy, 0, 0, 64)
-        cast_q(nc.vector.tensor_copy, 0, 64, P, 0, 2)
-        cast_q(nc.vector.tensor_copy, 0, 64, 80, 2, PACK)
-        cast_q(nc.scalar.copy, 0, 80, P, 2, PACK)
+        cast_q(nc.vector.tensor_copy, 0, 0, P, 0, 2)
+        cast_q(nc.vector.tensor_copy, 0, 0, Q_SHARE, 2, PACK)
+        cast_q(nc.scalar.copy, 0, Q_SHARE, P, 2, PACK)
         quantise_q(0, 1)
         probs(0, 0)
-        cast_q(nc.vector.tensor_copy, 1, 0, 64)
-        cast_q(nc.vector.tensor_copy, 1, 64, P, 0, 2)
-        cast_q(nc.vector.tensor_copy, 1, 64, P, 2, PACK)
+        cast_q(nc.vector.tensor_copy, 1, 0, Q_CUT)
+        cast_q(nc.vector.tensor_copy, 1, Q_CUT, P, 0, 2)
+        cast_q(nc.vector.tensor_copy, 1, Q_CUT, P, 2, PACK)
         quantise_q(1, 2)
         probs(0, 1)
         weigh(0, 0)

@@ -24,6 +24,7 @@ HALVES = 2
 HALF = N // HALVES
 RUN = 4
 SCALAR_SLOTS = 176
+LATE_SLOTS = 64
 E_BLOCKS = DV // P
 WINDOWS = 3
 Q_CUT = 96
@@ -131,12 +132,10 @@ def tile_attend_gat_lse_v_kernel(tc, qT, kT, lse, rw, dom, offs, out):
             for t in range(PACK):
                 nc.scalar.activation(p32[(g, h)][:, t, :], scores[g][t][:, slots], EXP, bias=neg_lse[:, g, t : t + 1])
 
-        def weigh(g, h, skip=0):
-            if h == 0:
-                pw[g] = sb.tile([P, N, PACK], BF16, name="pw%d" % g, tag="q_raw1_%d" % Q_CUT if g == 0 else "pw1", align_bytes=64)
-            gate = gate_bank[:, :, PASSES + g : PASSES + g + 1].unsqueeze(1).to_broadcast([P, (HALF - skip) // RUN, PACK, RUN])
-            nc.vector.tensor_tensor(pw[g][:, h * HALF + skip : (h + 1) * HALF, :].rearrange("p (c i) t -> p c t i", i=RUN),
-                                    p32[(g, h)][:, :, skip:].rearrange("p t (c i) -> p c t i", i=RUN), gate, MULT)
+        def weigh(g, h, skip=0, end=HALF):
+            gate = gate_bank[:, :, PASSES + g : PASSES + g + 1].unsqueeze(1).to_broadcast([P, (end - skip) // RUN, PACK, RUN])
+            nc.vector.tensor_tensor(pw[g][:, h * HALF + skip : h * HALF + end, :].rearrange("p (c i) t -> p c t i", i=RUN),
+                                    p32[(g, h)][:, :, skip:end].rearrange("p t (c i) -> p c t i", i=RUN), gate, MULT)
 
         def weigh_on_scalar(g, h):
             flat = sb.tile([P, PACK, SCALAR_SLOTS], BF16, name="pw_flat")
@@ -202,9 +201,12 @@ def tile_attend_gat_lse_v_kernel(tc, qT, kT, lse, rw, dom, offs, out):
         cast_q(nc.vector.tensor_copy, 1, Q_CUT, P, 2, PACK)
         quantise_q(1, 2)
         probs(0, 1)
+        both = sb.tile([P, 2 * N - LATE_SLOTS, PACK], BF16, name="pw_both", tag="q_raw1_%d" % Q_CUT, align_bytes=64)
+        pw[0] = both[:, :N]
+        pw[1] = both[:, N - LATE_SLOTS :]
         weigh(0, 0)
         probs(1, 0)
-        weigh(0, 1)
+        weigh(0, 1, 0, HALF - LATE_SLOTS)
         for g in range(PASSES):
             cast_dom(0, g)
         probs(1, 1)
@@ -217,6 +219,7 @@ def tile_attend_gat_lse_v_kernel(tc, qT, kT, lse, rw, dom, offs, out):
         quantise_dom(0)
         quantise_pw(1, 0, HALF)
         quantise_pw(0, 0, HALF)
+        weigh(0, 1, HALF - LATE_SLOTS)
         weigh(1, 1, SCALAR_SLOTS)
         early = product(0, 0, HALF)
         quantise_pw(0, HALF, N)

@@ -23,7 +23,7 @@ PASSES = R // (P * PACK)
 HALVES = 2
 HALF = N // HALVES
 RUN = 4
-SCALAR_SLOTS = 176
+SCALAR_SLOTS = 208
 LATE_SLOTS = 64
 E_BLOCKS = DV // P
 WINDOWS = 3
@@ -196,7 +196,8 @@ def tile_attend_gat_lse_v_kernel(tc, qT, kT, lse, rw, dom, offs, out):
         cast_q(nc.scalar.copy, 0, Q_SHARE, P, 2, PACK)
         quantise_q(0, 1)
         probs(0, 0)
-        cast_q(nc.vector.tensor_copy, 1, 0, Q_CUT)
+        cast_q(nc.vector.tensor_copy, 1, 0, Q_CUT, 0, 2)
+        cast_q(nc.vector.tensor_copy, 1, 0, Q_CUT, 2, PACK)
         cast_q(nc.vector.tensor_copy, 1, Q_CUT, P, 0, 2)
         cast_q(nc.vector.tensor_copy, 1, Q_CUT, P, 2, PACK)
         quantise_q(1, 2)

@@ -57,7 +57,7 @@ def tile_attend_gat_lse_v_kernel(tc, qT, kT, lse, rw, dom, offs, out):
         for g, m0, m1 in Q_LOADS:
             q_raw[(g, m0)] = sb.tile([P, PACK, (m1 - m0) * PACK], F32, name="q_raw%d_%d" % (g, m0), align_bytes=64)
         k_plane = [sb.tile([P, T], F32, name="k_plane%d" % j) for j in range(PACK)]
-        dom_cuts = [(0, P), (P, DV)]
+        dom_cuts = [(0, P), (P, 2 * P), (2 * P, DV)]
         dom_raw = {(g, e0): sb.tile([P, PACK, e1 - e0], F32, name="dom_raw%d_%d" % (g, e0)) for e0, e1 in dom_cuts for g in range(PASSES)}
         nc.scalar.dma_start(landed[0:PASSES, :], lse[0].rearrange("(g c) o -> g (c o)", g=PASSES))
         nc.scalar.dma_start(landed[PASSES : 2 * PASSES, :], rw[0].rearrange("(g c) o -> g (c o)", g=PASSES))
@@ -162,7 +162,7 @@ def tile_attend_gat_lse_v_kernel(tc, qT, kT, lse, rw, dom, offs, out):
                 rest = sb.tile([P, E_BLOCKS - 1, PASSES, P, PACK], BF16, name="dom_rest", tag="q_raw1_%d" % Q_CUT, align_bytes=64)
                 for blk in range(1, E_BLOCKS):
                     dom_grouped[blk] = rest[:, blk - 1]
-            src = dom_raw[(g, 0)][:] if b == 0 else dom_raw[(g, P)][:, :, (b - 1) * P : b * P]
+            src = dom_raw[(g, b * P)][:] if b < 2 else dom_raw[(g, 2 * P)][:, :, (b - 2) * P : (b - 1) * P]
             if b == 0:
                 nc.gpsimd.tensor_copy(dom_grouped[b][:, g], src.rearrange("p j e -> p e j"))
             else:

@@ -28,7 +28,6 @@ LATE_SLOTS = 64
 E_BLOCKS = DV // P
 WINDOWS = 3
 Q_CUT = 96
-Q_SHARE = 40
 Q_LOADS = [(0, 0, P), (1, 0, Q_CUT), (1, Q_CUT, P)]
 
 
@@ -113,7 +112,7 @@ def tile_attend_gat_lse_v_kernel(tc, qT, kT, lse, rw, dom, offs, out):
             for h in range(HALVES):
                 entries = offsets[:, h * HALF // 16 : (h + 1) * HALF // 16]
                 nc.vector.tensor_copy(k_grouped[h][:, :, j], k_plane[j][:].indirect(entries))
-        k_mx = [quantise("k%d" % h, k_grouped[h][:].rearrange("p i j -> p (i j)"), HALF, E4M3) for h in range(HALVES)]
+        k_mx = [quantise("k0", k_grouped[0][:].rearrange("p i j -> p (i j)"), HALF, E4M3)]
 
         pw = {}
         p32 = {}
@@ -192,8 +191,8 @@ def tile_attend_gat_lse_v_kernel(tc, qT, kT, lse, rw, dom, offs, out):
                 nc.sync.dma_start(out[b * P : (b + 1) * P, :], win[:])
 
         cast_q(nc.vector.tensor_copy, 0, 0, P, 0, 2)
-        cast_q(nc.vector.tensor_copy, 0, 0, Q_SHARE, 2, PACK)
-        cast_q(nc.scalar.copy, 0, Q_SHARE, P, 2, PACK)
+        cast_q(nc.scalar.copy, 0, 0, P, 2, PACK)
+        k_mx.append(quantise("k1", k_grouped[1][:].rearrange("p i j -> p (i j)"), HALF, E4M3))
         quantise_q(0, 1)
         probs(0, 0)
         cast_q(nc.vector.tensor_copy, 1, 0, Q_CUT, 0, 2)

@@ -101,9 +101,9 @@ def tile_attend_gat_lse_v_kernel(tc, qT, kT, lse, rw, dom, offs, out):
             src = q_raw[(g, base)][:].rearrange("p j (m t) -> p m j t", t=PACK)
             copy(dst[:, m0:m1, :, t0:t1], src[:, m0 - base : m1 - base, :, t0:t1])
 
-        def quantise_q(g, tiles):
+        def quantise_q(g, runs):
             q_mx[g] = []
-            for t in range(0, PACK, tiles):
+            for t, tiles in runs:
                 codes, scales = quantise("q%d%d" % (g, t), q_grouped[g][:, t : t + tiles].rearrange("p t m j -> p (t m j)"), tiles * P, E4M3)
                 q_mx[g].extend((codes[:, u * P : (u + 1) * P], scales[:, u * P : (u + 1) * P]) for u in range(tiles))
 
@@ -168,16 +168,20 @@ def tile_attend_gat_lse_v_kernel(tc, qT, kT, lse, rw, dom, offs, out):
                 nc.scalar.copy(dom_grouped[b][:, g].rearrange("p (c i) j -> p c j i", i=RUN),
                                src.rearrange("p j (c i) -> p c j i", i=RUN))
 
-        def quantise_dom(b):
-            dom_mx[b] = quantise("dom%d" % b, dom_grouped[b].rearrange("p g e j -> p (g e j)"), PASSES * P, E5M2)
+        def quantise_dom(b, by_pass=False):
+            if by_pass:
+                dom_mx[b] = [quantise("dom%d%d" % (b, g), dom_grouped[b][:, g].rearrange("p e j -> p (e j)"), P, E5M2) for g in range(PASSES)]
+                dom_mx[b] = [(codes[:], scales[:]) for codes, scales in dom_mx[b]]
+            else:
+                codes, scales = quantise("dom%d" % b, dom_grouped[b].rearrange("p g e j -> p (g e j)"), PASSES * P, E5M2)
+                dom_mx[b] = [(codes[:, g * P : (g + 1) * P], scales[:, g * P : (g + 1) * P]) for g in range(PASSES)]
 
         def product(b, i0, i1):
-            d_codes, d_scales = dom_mx[b]
             acc = ps.tile([P, N], F32, name="bank")
             cols = slice(i1 + HALF - N, i1 + HALF)
             for n, g in enumerate(range(PASSES) if i1 == N else reversed(range(PASSES))):
-                m = slice(g * P, (g + 1) * P)
-                nc.tensor.matmul_mx(out=acc[:], lhsT=d_codes[:, m].bitcast(E5M2), lhsT_scale=d_scales[:, m],
+                d_codes, d_scales = dom_mx[b][g]
+                nc.tensor.matmul_mx(out=acc[:], lhsT=d_codes.bitcast(E5M2), lhsT_scale=d_scales,
                                     rhs=pw_codes[g][:, cols].bitcast(E4M3), rhs_scale=pw_scales[g][:, cols],
                                     start=(n == 0), stop=(n == PASSES - 1))
             dv = sb.tile([P, i1 - i0], F32, name="dv%d_%d" % (b, i0))
@@ -193,13 +197,13 @@ def tile_attend_gat_lse_v_kernel(tc, qT, kT, lse, rw, dom, offs, out):
         cast_q(nc.vector.tensor_copy, 0, 0, P, 0, 2)
         cast_q(nc.scalar.copy, 0, 0, P, 2, PACK)
         k_mx.append(quantise("k1", k_grouped[1][:].rearrange("p i j -> p (i j)"), HALF, E4M3))
-        quantise_q(0, 1)
+        quantise_q(0, [(0, 1), (1, 1), (2, 1), (3, 1)])
         probs(0, 0)
         cast_q(nc.vector.tensor_copy, 1, 0, Q_CUT, 0, 2)
         cast_q(nc.vector.tensor_copy, 1, 0, Q_CUT, 2, PACK)
         cast_q(nc.vector.tensor_copy, 1, Q_CUT, P, 0, 2)
         cast_q(nc.vector.tensor_copy, 1, Q_CUT, P, 2, PACK)
-        quantise_q(1, 2)
+        quantise_q(1, [(0, 1), (1, 1), (2, 2)])
         probs(0, 1)
         both = sb.tile([P, 2 * N - LATE_SLOTS, PACK], BF16, name="pw_both", tag="q_raw1_%d" % Q_CUT, align_bytes=64)
         pw[0] = both[:, :N]
@@ -228,7 +232,7 @@ def tile_attend_gat_lse_v_kernel(tc, qT, kT, lse, rw, dom, offs, out):
         cast_dom(1, 1)
         scatter(0, early, 0, HALF)
         late = product(0, HALF, N)
-        quantise_dom(1)
+        quantise_dom(1, by_pass=True)
         scatter(0, late, HALF, N)
         for g in range(PASSES):
             cast_dom(2, g)

@@ -23,7 +23,7 @@ PASSES = R // (P * PACK)
 HALVES = 2
 HALF = N // HALVES
 RUN = 4
-SCALAR_SLOTS = 208
+SCALAR_SLOTS = 184
 LATE_SLOTS = 64
 E_BLOCKS = DV // P
 WINDOWS = 3

@@ -28,6 +28,8 @@ LATE_SLOTS = 64
 E_BLOCKS = DV // P
 WINDOWS = 3
 Q_CUT = 96
+FIRST_SHARE = 96
+SECOND_SHARE = 40
 Q_LOADS = [(0, 0, P), (1, 0, Q_CUT), (1, Q_CUT, P)]
 
 
@@ -91,7 +93,7 @@ def tile_attend_gat_lse_v_kernel(tc, qT, kT, lse, rw, dom, offs, out):
         nc.scalar.copy(rw_sb[:], gate_bank[:, :, PASSES : 2 * PASSES].rearrange("p t g -> p g t"))
 
         q_grouped = {}
-        q_mx = [None] * PASSES
+        q_mx = [[] for g in range(PASSES)]
 
         def cast_q(copy, g, m0, m1, t0=0, t1=PACK):
             base = max(l0 for lg, l0, l1 in Q_LOADS if lg == g and l0 <= m0)
@@ -102,7 +104,6 @@ def tile_attend_gat_lse_v_kernel(tc, qT, kT, lse, rw, dom, offs, out):
             copy(dst[:, m0:m1, :, t0:t1], src[:, m0 - base : m1 - base, :, t0:t1])
 
         def quantise_q(g, runs):
-            q_mx[g] = []
             for t, tiles in runs:
                 codes, scales = quantise("q%d%d" % (g, t), q_grouped[g][:, t : t + tiles].rearrange("p t m j -> p (t m j)"), tiles * P, E4M3)
                 q_mx[g].extend((codes[:, u * P : (u + 1) * P], scales[:, u * P : (u + 1) * P]) for u in range(tiles))
@@ -194,10 +195,13 @@ def tile_attend_gat_lse_v_kernel(tc, qT, kT, lse, rw, dom, offs, out):
             if i1 == N:
                 nc.sync.dma_start(out[b * P : (b + 1) * P, :], win[:])
 
-        cast_q(nc.vector.tensor_copy, 0, 0, P, 0, 2)
-        cast_q(nc.scalar.copy, 0, 0, P, 2, PACK)
+        cast_q(nc.scalar.copy, 0, FIRST_SHARE, P, 0, 2)
+        cast_q(nc.vector.tensor_copy, 0, 0, FIRST_SHARE, 0, 2)
+        cast_q(nc.vector.tensor_copy, 0, 0, SECOND_SHARE, 2, PACK)
+        cast_q(nc.scalar.copy, 0, SECOND_SHARE, P, 2, PACK)
+        quantise_q(0, [(0, 1), (1, 1)])
         k_mx.append(quantise("k1", k_grouped[1][:].rearrange("p i j -> p (i j)"), HALF, E4M3))
-        quantise_q(0, [(0, 1), (1, 1), (2, 1), (3, 1)])
+        quantise_q(0, [(2, 1), (3, 1)])
         probs(0, 0)
         cast_q(nc.vector.tensor_copy, 1, 0, Q_CUT, 0, 2)
         cast_q(nc.vector.tensor_copy, 1, 0, Q_CUT, 2, PACK)

@@ -218,9 +218,6 @@ def tile_attend_gat_lse_v_kernel(tc, qT, kT, lse, rw, dom, offs, out):
         for g in range(PASSES):
             cast_dom(0, g)
         probs(1, 1)
-        for t in range(PACK):
-            nc.tensor.matmul_mx(out=scores[1][t][:, :HALF], lhsT=q_mx[1][t][0].bitcast(E4M3), lhsT_scale=q_mx[1][t][1],
-                                rhs=k_mx[0][0][:].bitcast(E4M3), rhs_scale=k_mx[0][1][:], start=True, stop=True)
         flat = weigh_on_scalar(1, 1)
         weigh(1, 0)
         interleave(1, 1, flat)

@@ -218,6 +218,10 @@ def tile_attend_gat_lse_v_kernel(tc, qT, kT, lse, rw, dom, offs, out):
         for g in range(PASSES):
             cast_dom(0, g)
         probs(1, 1)
+        for t in range(PACK):
+            q_codes, q_scales = q_mx[1][t]
+            nc.tensor.matmul_mx(out=scores[1][t][:, HALF:], lhsT=q_codes.bitcast(E4M3), lhsT_scale=q_scales,
+                                rhs=k_mx[1][0][:].bitcast(E4M3), rhs_scale=k_mx[1][1][:], start=True, stop=True)
         flat = weigh_on_scalar(1, 1)
         weigh(1, 0)
         interleave(1, 1, flat)

@@ -159,9 +159,11 @@ def tile_attend_gat_lse_v_kernel(tc, qT, kT, lse, rw, dom, offs, out):
                 first = sb.tile([P, PASSES, P, PACK], BF16, name="dom_first", tag="q_raw0_0", align_bytes=64)
                 dom_grouped[0] = first[:]
             if b == 1 and g == 0:
-                rest = sb.tile([P, E_BLOCKS - 1, PASSES, P, PACK], BF16, name="dom_rest", tag="q_raw1_%d" % Q_CUT, align_bytes=64)
-                for blk in range(1, E_BLOCKS):
-                    dom_grouped[blk] = rest[:, blk - 1]
+                second = sb.tile([P, PASSES, P, PACK], BF16, name="dom_second", tag="p32_11", align_bytes=64)
+                dom_grouped[1] = second[:]
+                rest = sb.tile([P, E_BLOCKS - 2, PASSES, P, PACK], BF16, name="dom_rest", tag="q_raw1_%d" % Q_CUT, align_bytes=64)
+                for blk in range(2, E_BLOCKS):
+                    dom_grouped[blk] = rest[:, blk - 2]
             src = dom_raw[(g, b * P)][:] if b < 2 else dom_raw[(g, 2 * P)][:, :, (b - 2) * P : (b - 1) * P]
             if b == 0:
                 nc.gpsimd.tensor_copy(dom_grouped[b][:, g], src.rearrange("p j e -> p e j"))

@@ -22,22 +22,26 @@ PACK = 4
 PASSES = R // (P * PACK)
 HALVES = 2
 HALF = N // HALVES
+E_BLOCKS = DV // P
+ENTRIES = 16
 RUN = 4
+PSUM_BANKS = 8
+WINDOWS = 3
 SCALAR_SLOTS = 184
 LATE_SLOTS = 64
-E_BLOCKS = DV // P
-WINDOWS = 3
 Q_CUT = 96
 FIRST_SHARE = 96
 SECOND_SHARE = 40
+WARM_UPS = 3
 Q_LOADS = [(0, 0, P), (1, 0, Q_CUT), (1, Q_CUT, P)]
+DOM_CUTS = [(0, P), (P, 2 * P), (2 * P, DV)]
 
 
 def tile_attend_gat_lse_v_kernel(tc, qT, kT, lse, rw, dom, offs, out):
     nc = tc.nc
     with ExitStack() as ctx:
         sb = ctx.enter_context(tc.tile_pool(name="sb", bufs=1))
-        ps = ctx.enter_context(tc.psum_pool(name="ps", bufs=PASSES * PACK - 1))
+        ps = ctx.enter_context(tc.psum_pool(name="ps", bufs=PSUM_BANKS - 1))
         ps_gate = ctx.enter_context(tc.psum_pool(name="ps_gate", bufs=1))
 
         def quantise(name, grouped, words, fmt):
@@ -46,7 +50,7 @@ def tile_attend_gat_lse_v_kernel(tc, qT, kT, lse, rw, dom, offs, out):
             nc.vector.quantize_mx(out=codes[:].bitcast(fmt), scales=scales[:], in_=grouped)
             return codes, scales
 
-        offsets = sb.tile([P, N // 16], U16, name="offsets")
+        offsets = sb.tile([P, N // ENTRIES], U16, name="offsets")
         rows = sb.tile([P, P * PACK], F32, name="rows")
         nc.gpsimd.memset(rows[:], 0.0)
         landed = sb.tile([2 * PASSES, P * PACK], F32, name="landed")
@@ -58,18 +62,16 @@ def tile_attend_gat_lse_v_kernel(tc, qT, kT, lse, rw, dom, offs, out):
         for g, m0, m1 in Q_LOADS:
             q_raw[(g, m0)] = sb.tile([P, PACK, (m1 - m0) * PACK], F32, name="q_raw%d_%d" % (g, m0), align_bytes=64)
         k_plane = [sb.tile([P, T], F32, name="k_plane%d" % j) for j in range(PACK)]
-        dom_cuts = [(0, P), (P, 2 * P), (2 * P, DV)]
-        dom_raw = {(g, e0): sb.tile([P, PACK, e1 - e0], F32, name="dom_raw%d_%d" % (g, e0)) for e0, e1 in dom_cuts for g in range(PASSES)}
+        dom_raw = {(g, e0): sb.tile([P, PACK, e1 - e0], F32, name="dom_raw%d_%d" % (g, e0)) for e0, e1 in DOM_CUTS for g in range(PASSES)}
         nc.scalar.dma_start(landed[0:PASSES, :], lse[0].rearrange("(g c) o -> g (c o)", g=PASSES))
         nc.scalar.dma_start(landed[PASSES : 2 * PASSES, :], rw[0].rearrange("(g c) o -> g (c o)", g=PASSES))
         nc.sync.dma_start(k_plane[0][:], k_rows[0])
         nc.sync.dma_start(offsets[:], offs)
-        nc.sync.dma_start(k_plane[1][:], k_rows[1])
-        nc.sync.dma_start(k_plane[2][:], k_rows[2])
-        nc.sync.dma_start(k_plane[3][:], k_rows[3])
+        for j in range(1, PACK):
+            nc.sync.dma_start(k_plane[j][:], k_rows[j])
         for g, m0, m1 in Q_LOADS:
             nc.sync.dma_start(q_raw[(g, m0)][:], q_rows[g][:, :, m0 * PACK : m1 * PACK])
-        for e0, e1 in dom_cuts:
+        for e0, e1 in DOM_CUTS:
             for g in range(PASSES):
                 nc.sync.dma_start(dom_raw[(g, e0)][:], dom_rows[g][:, :, e0:e1])
 
@@ -81,6 +83,7 @@ def tile_attend_gat_lse_v_kernel(tc, qT, kT, lse, rw, dom, offs, out):
         for g in range(PASSES):
             nc.vector.memset(pw_codes[g][:, :HALF], 0)
             nc.vector.memset(pw_scales[g][:, :HALF].bitcast(U32), 0)
+
         identity = sb.tile([P, P], F32, name="identity")
         make_identity(nc, identity[:])
         nc.scalar.copy(rows[0 : 2 * PASSES, :], landed[:])
@@ -95,7 +98,7 @@ def tile_attend_gat_lse_v_kernel(tc, qT, kT, lse, rw, dom, offs, out):
         q_grouped = {}
         q_mx = [[] for g in range(PASSES)]
 
-        def cast_q(copy, g, m0, m1, t0=0, t1=PACK):
+        def cast_q(copy, g, m0, m1, t0, t1):
             base = max(l0 for lg, l0, l1 in Q_LOADS if lg == g and l0 <= m0)
             if g not in q_grouped:
                 q_grouped[g] = sb.tile([P, PACK, P, PACK], BF16, name="q_grouped", tag="q_grouped" if g == 0 else "q_raw0_0", align_bytes=64)
@@ -111,31 +114,37 @@ def tile_attend_gat_lse_v_kernel(tc, qT, kT, lse, rw, dom, offs, out):
         k_grouped = [sb.tile([P, HALF, PACK], BF16, name="k_grouped%d" % h, align_bytes=64) for h in range(HALVES)]
         for j in range(PACK):
             for h in range(HALVES):
-                entries = offsets[:, h * HALF // 16 : (h + 1) * HALF // 16]
+                entries = offsets[:, h * HALF // ENTRIES : (h + 1) * HALF // ENTRIES]
                 nc.vector.tensor_copy(k_grouped[h][:, :, j], k_plane[j][:].indirect(entries))
-        k_mx = [quantise("k0", k_grouped[0][:].rearrange("p i j -> p (i j)"), HALF, E4M3)]
+
+        def quantise_k(h):
+            return quantise("k%d" % h, k_grouped[h][:].rearrange("p i j -> p (i j)"), HALF, E4M3)
+
+        k_mx = [quantise_k(0)]
 
         pw = {}
         p32 = {}
         scores = {}
 
+        def score(g, h, t):
+            q_codes, q_scales = q_mx[g][t]
+            k_codes, k_scales = k_mx[h]
+            nc.tensor.matmul_mx(out=scores[g][t][:, h * HALF : (h + 1) * HALF], lhsT=q_codes.bitcast(E4M3), lhsT_scale=q_scales,
+                                rhs=k_codes[:].bitcast(E4M3), rhs_scale=k_scales[:], start=True, stop=True)
+
         def probs(g, h):
             if h == 0:
                 scores[g] = [ps.tile([P, N], F32, name="bank") for t in range(PACK)]
-            slots = slice(h * HALF, (h + 1) * HALF)
-            k_codes, k_scales = k_mx[h]
             for t in range(PACK):
-                q_codes, q_scales = q_mx[g][t]
-                nc.tensor.matmul_mx(out=scores[g][t][:, slots], lhsT=q_codes.bitcast(E4M3), lhsT_scale=q_scales,
-                                    rhs=k_codes[:].bitcast(E4M3), rhs_scale=k_scales[:], start=True, stop=True)
+                score(g, h, t)
             p32[(g, h)] = sb.tile([P, PACK, HALF], F32, name="p32_%d%d" % (g, h), align_bytes=64)
             for t in range(PACK):
-                nc.scalar.activation(p32[(g, h)][:, t, :], scores[g][t][:, slots], EXP, bias=neg_lse[:, g, t : t + 1])
+                nc.scalar.activation(p32[(g, h)][:, t, :], scores[g][t][:, h * HALF : (h + 1) * HALF], EXP, bias=neg_lse[:, g, t : t + 1])
 
-        def weigh(g, h, skip=0, end=HALF):
-            gate = gate_bank[:, :, PASSES + g : PASSES + g + 1].unsqueeze(1).to_broadcast([P, (end - skip) // RUN, PACK, RUN])
-            nc.vector.tensor_tensor(pw[g][:, h * HALF + skip : h * HALF + end, :].rearrange("p (c i) t -> p c t i", i=RUN),
-                                    p32[(g, h)][:, :, skip:end].rearrange("p t (c i) -> p c t i", i=RUN), gate, MULT)
+        def weigh(g, h, i0=0, i1=HALF):
+            gate = gate_bank[:, :, PASSES + g : PASSES + g + 1].unsqueeze(1).to_broadcast([P, (i1 - i0) // RUN, PACK, RUN])
+            nc.vector.tensor_tensor(pw[g][:, h * HALF + i0 : h * HALF + i1, :].rearrange("p (c i) t -> p c t i", i=RUN),
+                                    p32[(g, h)][:, :, i0:i1].rearrange("p t (c i) -> p c t i", i=RUN), gate, MULT)
 
         def weigh_on_scalar(g, h):
             flat = sb.tile([P, PACK, SCALAR_SLOTS], BF16, name="pw_flat")
@@ -147,37 +156,40 @@ def tile_attend_gat_lse_v_kernel(tc, qT, kT, lse, rw, dom, offs, out):
             nc.scalar.copy(pw[g][:, h * HALF : h * HALF + SCALAR_SLOTS, :].rearrange("p (c i) t -> p c t i", i=RUN),
                            flat[:].rearrange("p t (c i) -> p c t i", i=RUN))
 
-        def quantise_pw(g, i0, i1):
+        def quantise_pw(g, h):
+            i0, i1 = h * HALF, (h + 1) * HALF
             nc.vector.quantize_mx(out=pw_codes[g][:, HALF + i0 : HALF + i1].bitcast(E4M3), scales=pw_scales[g][:, HALF + i0 : HALF + i1],
                                   in_=pw[g][:, i0:i1, :].rearrange("p i t -> p (i t)"))
 
         dom_grouped = {}
         dom_mx = [None] * E_BLOCKS
 
-        def cast_dom(b, g):
-            if b == 0 and g == 0:
+        def cast_dom(b):
+            if b == 0:
                 first = sb.tile([P, PASSES, P, PACK], BF16, name="dom_first", tag="q_raw0_0", align_bytes=64)
                 dom_grouped[0] = first[:]
-            if b == 1 and g == 0:
+            if b == 1:
                 second = sb.tile([P, PASSES, P, PACK], BF16, name="dom_second", tag="p32_11", align_bytes=64)
                 dom_grouped[1] = second[:]
                 rest = sb.tile([P, E_BLOCKS - 2, PASSES, P, PACK], BF16, name="dom_rest", tag="q_raw1_%d" % Q_CUT, align_bytes=64)
                 for blk in range(2, E_BLOCKS):
                     dom_grouped[blk] = rest[:, blk - 2]
-            src = dom_raw[(g, b * P)][:] if b < 2 else dom_raw[(g, 2 * P)][:, :, (b - 2) * P : (b - 1) * P]
-            if b == 0:
-                nc.gpsimd.tensor_copy(dom_grouped[b][:, g], src.rearrange("p j e -> p e j"))
-            else:
-                nc.scalar.copy(dom_grouped[b][:, g].rearrange("p (c i) j -> p c j i", i=RUN),
-                               src.rearrange("p j (c i) -> p c j i", i=RUN))
+            e0 = max(c0 for c0, c1 in DOM_CUTS if c0 <= b * P)
+            for g in range(PASSES):
+                src = dom_raw[(g, e0)][:, :, b * P - e0 : (b + 1) * P - e0]
+                if b == 0:
+                    nc.gpsimd.tensor_copy(dom_grouped[b][:, g], src.rearrange("p j e -> p e j"))
+                else:
+                    nc.scalar.copy(dom_grouped[b][:, g].rearrange("p (c i) j -> p c j i", i=RUN),
+                                   src.rearrange("p j (c i) -> p c j i", i=RUN))
 
-        def quantise_dom(b, by_pass=False):
-            if by_pass:
-                dom_mx[b] = [quantise("dom%d%d" % (b, g), dom_grouped[b][:, g].rearrange("p e j -> p (e j)"), P, E5M2) for g in range(PASSES)]
-                dom_mx[b] = [(codes[:], scales[:]) for codes, scales in dom_mx[b]]
-            else:
-                codes, scales = quantise("dom%d" % b, dom_grouped[b].rearrange("p g e j -> p (g e j)"), PASSES * P, E5M2)
-                dom_mx[b] = [(codes[:, g * P : (g + 1) * P], scales[:, g * P : (g + 1) * P]) for g in range(PASSES)]
+        def quantise_dom(b):
+            codes, scales = quantise("dom%d" % b, dom_grouped[b].rearrange("p g e j -> p (g e j)"), PASSES * P, E5M2)
+            dom_mx[b] = [(codes[:, g * P : (g + 1) * P], scales[:, g * P : (g + 1) * P]) for g in range(PASSES)]
+
+        def quantise_dom_by_pass(b):
+            made = [quantise("dom%d%d" % (b, g), dom_grouped[b][:, g].rearrange("p e j -> p (e j)"), P, E5M2) for g in range(PASSES)]
+            dom_mx[b] = [(codes[:], scales[:]) for codes, scales in made]
 
         def product(b, i0, i1):
             acc = ps.tile([P, N], F32, name="bank")
@@ -193,62 +205,56 @@ def tile_attend_gat_lse_v_kernel(tc, qT, kT, lse, rw, dom, offs, out):
 
         def scatter(b, dv, i0, i1):
             win = window[b % WINDOWS]
-            nc.vector.tensor_copy(win[:].indirect(offsets[:, i0 // 16 : i1 // 16]), dv[:])
+            nc.vector.tensor_copy(win[:].indirect(offsets[:, i0 // ENTRIES : i1 // ENTRIES]), dv[:])
             if i1 == N:
                 nc.sync.dma_start(out[b * P : (b + 1) * P, :], win[:])
 
-        cast_q(nc.scalar.copy, 0, FIRST_SHARE, P, 0, 2)
-        cast_q(nc.vector.tensor_copy, 0, 0, FIRST_SHARE, 0, 2)
-        cast_q(nc.vector.tensor_copy, 0, 0, SECOND_SHARE, 2, PACK)
-        cast_q(nc.scalar.copy, 0, SECOND_SHARE, P, 2, PACK)
+        pair = PACK // 2
+        cast_q(nc.scalar.copy, 0, FIRST_SHARE, P, 0, pair)
+        cast_q(nc.vector.tensor_copy, 0, 0, FIRST_SHARE, 0, pair)
+        cast_q(nc.vector.tensor_copy, 0, 0, SECOND_SHARE, pair, PACK)
+        cast_q(nc.scalar.copy, 0, SECOND_SHARE, P, pair, PACK)
         quantise_q(0, [(0, 1), (1, 1)])
-        k_mx.append(quantise("k1", k_grouped[1][:].rearrange("p i j -> p (i j)"), HALF, E4M3))
+        k_mx.append(quantise_k(1))
         quantise_q(0, [(2, 1), (3, 1)])
         probs(0, 0)
-        cast_q(nc.vector.tensor_copy, 1, 0, Q_CUT, 0, 2)
-        cast_q(nc.vector.tensor_copy, 1, 0, Q_CUT, 2, PACK)
-        cast_q(nc.vector.tensor_copy, 1, Q_CUT, P, 0, 2)
-        cast_q(nc.vector.tensor_copy, 1, Q_CUT, P, 2, PACK)
+
+        for m0, m1 in ((0, Q_CUT), (Q_CUT, P)):
+            cast_q(nc.vector.tensor_copy, 1, m0, m1, 0, pair)
+            cast_q(nc.vector.tensor_copy, 1, m0, m1, pair, PACK)
         quantise_q(1, [(0, 1), (1, 1), (2, 2)])
         probs(0, 1)
+
         both = sb.tile([P, 2 * N - LATE_SLOTS, PACK], BF16, name="pw_both", tag="q_raw1_%d" % Q_CUT, align_bytes=64)
         pw[0] = both[:, :N]
         pw[1] = both[:, N - LATE_SLOTS :]
         weigh(0, 0)
         probs(1, 0)
         weigh(0, 1, 0, HALF - LATE_SLOTS)
-        for g in range(PASSES):
-            cast_dom(0, g)
+        cast_dom(0)
         probs(1, 1)
-        for t in range(PACK):
-            q_codes, q_scales = q_mx[1][t]
-            nc.tensor.matmul_mx(out=scores[1][t][:, HALF:], lhsT=q_codes.bitcast(E4M3), lhsT_scale=q_scales,
-                                rhs=k_mx[1][0][:].bitcast(E4M3), rhs_scale=k_mx[1][1][:], start=True, stop=True)
+        for t in range(PACK - WARM_UPS, PACK):
+            score(1, 1, t)
         flat = weigh_on_scalar(1, 1)
         weigh(1, 0)
         interleave(1, 1, flat)
         quantise_dom(0)
-        quantise_pw(1, 0, HALF)
-        quantise_pw(0, 0, HALF)
+        quantise_pw(1, 0)
+        quantise_pw(0, 0)
         weigh(0, 1, HALF - LATE_SLOTS)
         weigh(1, 1, SCALAR_SLOTS)
         early = product(0, 0, HALF)
-        quantise_pw(0, HALF, N)
-        quantise_pw(1, HALF, N)
-        cast_dom(1, 0)
-        cast_dom(1, 1)
+        quantise_pw(0, 1)
+        quantise_pw(1, 1)
+
+        cast_dom(1)
         scatter(0, early, 0, HALF)
         late = product(0, HALF, N)
-        quantise_dom(1, by_pass=True)
+        quantise_dom_by_pass(1)
         scatter(0, late, HALF, N)
-        for g in range(PASSES):
-            cast_dom(2, g)
-        dv = product(1, 0, N)
-        quantise_dom(2)
-        scatter(1, dv, 0, N)
-        for g in range(PASSES):
-            cast_dom(3, g)
-        dv = product(2, 0, N)
-        quantise_dom(3)
-        scatter(2, dv, 0, N)
-        scatter(3, product(3, 0, N), 0, N)
+        for b in range(1, E_BLOCKS - 1):
+            cast_dom(b + 1)
+            dv = product(b, 0, N)
+            quantise_dom(b + 1)
+            scatter(b, dv, 0, N)
+        scatter(E_BLOCKS - 1, product(E_BLOCKS - 1, 0, N), 0, N)

@@ -26,13 +26,9 @@ E_BLOCKS = DV // P
 ENTRIES = 16
 RUN = 4
 PSUM_BANKS = 8
-WINDOWS = 3
-SCALAR_SLOTS = 184
-LATE_SLOTS = 64
 Q_CUT = 96
 FIRST_SHARE = 96
 SECOND_SHARE = 40
-WARM_UPS = 3
 Q_LOADS = [(0, 0, P), (1, 0, Q_CUT), (1, Q_CUT, P)]
 DOM_CUTS = [(0, P), (P, 2 * P), (2 * P, DV)]
 
@@ -44,8 +40,8 @@ def tile_attend_gat_lse_v_kernel(tc, qT, kT, lse, rw, dom, offs, out):
         ps = ctx.enter_context(tc.psum_pool(name="ps", bufs=PSUM_BANKS - 1))
         ps_gate = ctx.enter_context(tc.psum_pool(name="ps_gate", bufs=1))
 
-        def quantise(name, grouped, words, fmt):
-            codes = sb.tile([P, words], U32, name=name + "_codes", align_bytes=64)
+        def quantise(name, grouped, words, fmt, tag=""):
+            codes = sb.tile([P, words], U32, name=name + "_codes", tag=tag, align_bytes=64)
             scales = sb.tile([P, words], U8, name=name + "_scales", align_bytes=64)
             nc.vector.quantize_mx(out=codes[:].bitcast(fmt), scales=scales[:], in_=grouped)
             return codes, scales
@@ -75,14 +71,9 @@ def tile_attend_gat_lse_v_kernel(tc, qT, kT, lse, rw, dom, offs, out):
             for g in range(PASSES):
                 nc.sync.dma_start(dom_raw[(g, e0)][:], dom_rows[g][:, :, e0:e1])
 
-        window = [sb.tile([P, T], F32, name="window%d" % b) for b in range(WINDOWS)]
-        for b in range(WINDOWS):
+        window = [sb.tile([P, T], F32, name="window%d" % b) for b in range(E_BLOCKS)]
+        for b in range(E_BLOCKS):
             nc.vector.memset(window[b][:], 0.0)
-        pw_codes = [sb.tile([P, HALF + N], U32, name="pw_codes%d" % g, align_bytes=64) for g in range(PASSES)]
-        pw_scales = [sb.tile([P, HALF + N], U8, name="pw_scales%d" % g, align_bytes=64) for g in range(PASSES)]
-        for g in range(PASSES):
-            nc.vector.memset(pw_codes[g][:, :HALF], 0)
-            nc.vector.memset(pw_scales[g][:, :HALF].bitcast(U32), 0)
 
         identity = sb.tile([P, P], F32, name="identity")
         make_identity(nc, identity[:])
@@ -92,8 +83,9 @@ def tile_attend_gat_lse_v_kernel(tc, qT, kT, lse, rw, dom, offs, out):
             nc.tensor.transpose(gate_bank[:, t, :], rows[:, t : P * PACK : PACK], identity[:])
         neg_lse = sb.tile([P, PASSES, PACK], F32, name="neg_lse")
         nc.scalar.mul(neg_lse[:], gate_bank[:, :, 0:PASSES].rearrange("p t g -> p g t"), -1.0)
-        rw_sb = sb.tile([P, PASSES, PACK], F32, name="rw_sb")
-        nc.scalar.copy(rw_sb[:], gate_bank[:, :, PASSES : 2 * PASSES].rearrange("p t g -> p g t"))
+
+        def entries(i0, i1):
+            return offsets[:, i0 // ENTRIES : i1 // ENTRIES]
 
         q_grouped = {}
         q_mx = [[] for g in range(PASSES)]
@@ -113,110 +105,82 @@ def tile_attend_gat_lse_v_kernel(tc, qT, kT, lse, rw, dom, offs, out):
 
         k_grouped = [sb.tile([P, HALF, PACK], BF16, name="k_grouped%d" % h, align_bytes=64) for h in range(HALVES)]
         for j in range(PACK):
-            for h in range(HALVES):
-                entries = offsets[:, h * HALF // ENTRIES : (h + 1) * HALF // ENTRIES]
-                nc.vector.tensor_copy(k_grouped[h][:, :, j], k_plane[j][:].indirect(entries))
-
-        def quantise_k(h):
-            return quantise("k%d" % h, k_grouped[h][:].rearrange("p i j -> p (i j)"), HALF, E4M3)
-
-        k_mx = [quantise_k(0)]
+            nc.vector.tensor_copy(k_grouped[0][:, :, j], k_plane[j][:].indirect(entries(0, HALF)))
+            nc.scalar.activation(k_grouped[1][:, :, j], k_plane[j][:].indirect(entries(HALF, N)), COPY)
+        k_mx = [quantise("k%d" % h, k_grouped[h][:].rearrange("p i j -> p (i j)"), HALF, E4M3) for h in range(HALVES)]
 
         pw = {}
         p32 = {}
         scores = {}
-
-        def score(g, h, t):
-            q_codes, q_scales = q_mx[g][t]
-            k_codes, k_scales = k_mx[h]
-            nc.tensor.matmul_mx(out=scores[g][t][:, h * HALF : (h + 1) * HALF], lhsT=q_codes.bitcast(E4M3), lhsT_scale=q_scales,
-                                rhs=k_codes[:].bitcast(E4M3), rhs_scale=k_scales[:], start=True, stop=True)
+        pw_codes = [sb.tile([P, N], U32, name="pw_codes%d" % g, align_bytes=64) for g in range(PASSES)]
+        pw_scales = [sb.tile([P, N], U8, name="pw_scales%d" % g, align_bytes=64) for g in range(PASSES)]
 
         def probs(g, h):
             if h == 0:
                 scores[g] = [ps.tile([P, N], F32, name="bank") for t in range(PACK)]
+            k_codes, k_scales = k_mx[h]
             for t in range(PACK):
-                score(g, h, t)
+                q_codes, q_scales = q_mx[g][t]
+                nc.tensor.matmul_mx(out=scores[g][t][:, h * HALF : (h + 1) * HALF], lhsT=q_codes.bitcast(E4M3), lhsT_scale=q_scales,
+                                    rhs=k_codes[:].bitcast(E4M3), rhs_scale=k_scales[:], start=True, stop=True)
             p32[(g, h)] = sb.tile([P, PACK, HALF], F32, name="p32_%d%d" % (g, h), align_bytes=64)
             for t in range(PACK):
                 nc.scalar.activation(p32[(g, h)][:, t, :], scores[g][t][:, h * HALF : (h + 1) * HALF], EXP, bias=neg_lse[:, g, t : t + 1])
 
-        def weigh(g, h, i0=0, i1=HALF):
-            gate = gate_bank[:, :, PASSES + g : PASSES + g + 1].unsqueeze(1).to_broadcast([P, (i1 - i0) // RUN, PACK, RUN])
-            nc.vector.tensor_tensor(pw[g][:, h * HALF + i0 : h * HALF + i1, :].rearrange("p (c i) t -> p c t i", i=RUN),
-                                    p32[(g, h)][:, :, i0:i1].rearrange("p t (c i) -> p c t i", i=RUN), gate, MULT)
-
-        def weigh_on_scalar(g, h):
-            flat = sb.tile([P, PACK, SCALAR_SLOTS], BF16, name="pw_flat")
-            for t in range(PACK):
-                nc.scalar.activation(flat[:, t, :], p32[(g, h)][:, t, :SCALAR_SLOTS], COPY, scale=rw_sb[:, g, t : t + 1])
-            return flat
-
-        def interleave(g, h, flat):
-            nc.scalar.copy(pw[g][:, h * HALF : h * HALF + SCALAR_SLOTS, :].rearrange("p (c i) t -> p c t i", i=RUN),
-                           flat[:].rearrange("p t (c i) -> p c t i", i=RUN))
+        def weigh(g, h):
+            gate = gate_bank[:, :, PASSES + g : PASSES + g + 1].unsqueeze(1).to_broadcast([P, HALF // RUN, PACK, RUN])
+            nc.vector.tensor_tensor(pw[(g, h)].rearrange("p (c i) t -> p c t i", i=RUN),
+                                    p32[(g, h)][:].rearrange("p t (c i) -> p c t i", i=RUN), gate, MULT)
 
         def quantise_pw(g, h):
             i0, i1 = h * HALF, (h + 1) * HALF
-            nc.vector.quantize_mx(out=pw_codes[g][:, HALF + i0 : HALF + i1].bitcast(E4M3), scales=pw_scales[g][:, HALF + i0 : HALF + i1],
-                                  in_=pw[g][:, i0:i1, :].rearrange("p i t -> p (i t)"))
+            nc.vector.quantize_mx(out=pw_codes[g][:, i0:i1].bitcast(E4M3), scales=pw_scales[g][:, i0:i1],
+                                  in_=pw[(g, h)].rearrange("p i t -> p (i t)"))
 
         dom_grouped = {}
         dom_mx = [None] * E_BLOCKS
 
-        def cast_dom(b):
-            if b == 0:
-                first = sb.tile([P, PASSES, P, PACK], BF16, name="dom_first", tag="q_raw0_0", align_bytes=64)
-                dom_grouped[0] = first[:]
-            if b == 1:
-                second = sb.tile([P, PASSES, P, PACK], BF16, name="dom_second", tag="p32_11", align_bytes=64)
-                dom_grouped[1] = second[:]
-                rest = sb.tile([P, E_BLOCKS - 2, PASSES, P, PACK], BF16, name="dom_rest", tag="q_raw1_%d" % Q_CUT, align_bytes=64)
-                for blk in range(2, E_BLOCKS):
-                    dom_grouped[blk] = rest[:, blk - 2]
+        def dom_source(b, g):
             e0 = max(c0 for c0, c1 in DOM_CUTS if c0 <= b * P)
-            for g in range(PASSES):
-                src = dom_raw[(g, e0)][:, :, b * P - e0 : (b + 1) * P - e0]
-                if b == 0:
-                    nc.gpsimd.tensor_copy(dom_grouped[b][:, g], src.rearrange("p j e -> p e j"))
-                else:
-                    nc.scalar.copy(dom_grouped[b][:, g].rearrange("p (c i) j -> p c j i", i=RUN),
-                                   src.rearrange("p j (c i) -> p c j i", i=RUN))
+            return dom_raw[(g, e0)][:, :, b * P - e0 : (b + 1) * P - e0]
 
-        def quantise_dom(b):
-            codes, scales = quantise("dom%d" % b, dom_grouped[b].rearrange("p g e j -> p (g e j)"), PASSES * P, E5M2)
+        def cast_dom_gpsimd(b, g):
+            nc.gpsimd.tensor_copy(dom_grouped[b][:, g], dom_source(b, g).rearrange("p j e -> p e j"))
+
+        def cast_dom_scalar(b, g):
+            nc.scalar.copy(dom_grouped[b][:, g].rearrange("p (c i) j -> p c j i", i=RUN),
+                           dom_source(b, g).rearrange("p j (c i) -> p c j i", i=RUN))
+
+        def quantise_dom(b, tag=""):
+            codes, scales = quantise("dom%d" % b, dom_grouped[b].rearrange("p g e j -> p (g e j)"), PASSES * P, E5M2, tag)
             dom_mx[b] = [(codes[:, g * P : (g + 1) * P], scales[:, g * P : (g + 1) * P]) for g in range(PASSES)]
 
-        def quantise_dom_by_pass(b):
-            made = [quantise("dom%d%d" % (b, g), dom_grouped[b][:, g].rearrange("p e j -> p (e j)"), P, E5M2) for g in range(PASSES)]
-            dom_mx[b] = [(codes[:], scales[:]) for codes, scales in made]
-
-        def product(b, i0, i1):
+        def product(b, i0, i1, copy):
             acc = ps.tile([P, N], F32, name="bank")
-            cols = slice(i1 + HALF - N, i1 + HALF)
-            for n, g in enumerate(range(PASSES) if i1 == N else reversed(range(PASSES))):
+            for g in range(PASSES):
                 d_codes, d_scales = dom_mx[b][g]
-                nc.tensor.matmul_mx(out=acc[:], lhsT=d_codes.bitcast(E5M2), lhsT_scale=d_scales,
-                                    rhs=pw_codes[g][:, cols].bitcast(E4M3), rhs_scale=pw_scales[g][:, cols],
-                                    start=(n == 0), stop=(n == PASSES - 1))
-            dv = sb.tile([P, i1 - i0], F32, name="dv%d_%d" % (b, i0))
-            nc.scalar.copy(dv[:], acc[:, N - (i1 - i0) :])
+                nc.tensor.matmul_mx(out=acc[:, : i1 - i0], lhsT=d_codes.bitcast(E5M2), lhsT_scale=d_scales,
+                                    rhs=pw_codes[g][:, i0:i1].bitcast(E4M3), rhs_scale=pw_scales[g][:, i0:i1],
+                                    start=(g == 0), stop=(g == PASSES - 1))
+            dv = sb.tile([P, i1 - i0], F32, name="dv%d_%d" % (b, i0), align_bytes=64)
+            copy(dv[:], acc[:, : i1 - i0])
             return dv
 
-        def scatter(b, dv, i0, i1):
-            win = window[b % WINDOWS]
-            nc.vector.tensor_copy(win[:].indirect(offsets[:, i0 // ENTRIES : i1 // ENTRIES]), dv[:])
-            if i1 == N:
-                nc.sync.dma_start(out[b * P : (b + 1) * P, :], win[:])
+        def scatter_vector(b, values, i0, i1):
+            nc.vector.tensor_copy(window[b][:].indirect(entries(i0, i1)), values)
+
+        def scatter_scalar(b, values, i0, i1):
+            nc.scalar.activation(window[b][:].indirect(entries(i0, i1)), values, COPY)
+
+        def store(b):
+            nc.sync.dma_start(out[b * P : (b + 1) * P, :], window[b][:])
 
         pair = PACK // 2
         cast_q(nc.scalar.copy, 0, FIRST_SHARE, P, 0, pair)
         cast_q(nc.vector.tensor_copy, 0, 0, FIRST_SHARE, 0, pair)
         cast_q(nc.vector.tensor_copy, 0, 0, SECOND_SHARE, pair, PACK)
         cast_q(nc.scalar.copy, 0, SECOND_SHARE, P, pair, PACK)
-        quantise_q(0, [(0, 1), (1, 1)])
-        k_mx.append(quantise_k(1))
-        quantise_q(0, [(2, 1), (3, 1)])
+        quantise_q(0, [(0, 1), (1, 1), (2, 1), (3, 1)])
         probs(0, 0)
 
         for m0, m1 in ((0, Q_CUT), (Q_CUT, P)):
@@ -225,36 +189,50 @@ def tile_attend_gat_lse_v_kernel(tc, qT, kT, lse, rw, dom, offs, out):
         quantise_q(1, [(0, 1), (1, 1), (2, 2)])
         probs(0, 1)
 
-        both = sb.tile([P, 2 * N - LATE_SLOTS, PACK], BF16, name="pw_both", tag="q_raw1_%d" % Q_CUT, align_bytes=64)
-        pw[0] = both[:, :N]
-        pw[1] = both[:, N - LATE_SLOTS :]
+        first_pass = sb.tile([P, N, PACK], BF16, name="pw0", tag="q_raw1_%d" % Q_CUT, align_bytes=64)
+        for h in range(HALVES):
+            pw[(0, h)] = first_pass[:, h * HALF : (h + 1) * HALF]
+            quarter = sb.tile([P, HALF, PACK], BF16, name="pw1%d" % h, align_bytes=64)
+            pw[(1, h)] = quarter[:]
+        early = sb.tile([P, 2, PASSES, P, PACK], BF16, name="dom_early", tag="q_raw0_0", align_bytes=64)
         weigh(0, 0)
         probs(1, 0)
-        weigh(0, 1, 0, HALF - LATE_SLOTS)
-        cast_dom(0)
+        weigh(0, 1)
+        for b in range(2):
+            dom_grouped[b] = early[:, b]
+            for g in range(PASSES):
+                cast_dom_gpsimd(b, g)
         probs(1, 1)
-        for t in range(PACK - WARM_UPS, PACK):
-            score(1, 1, t)
-        flat = weigh_on_scalar(1, 1)
         weigh(1, 0)
-        interleave(1, 1, flat)
         quantise_dom(0)
-        quantise_pw(1, 0)
         quantise_pw(0, 0)
-        weigh(0, 1, HALF - LATE_SLOTS)
-        weigh(1, 1, SCALAR_SLOTS)
-        early = product(0, 0, HALF)
+        quantise_pw(1, 0)
+        last = sb.tile([P, PASSES, P, PACK], BF16, name="dom_last", tag="p32_01", align_bytes=64)
+        dom_grouped[3] = last[:]
+        third = sb.tile([P, PASSES, P, PACK], BF16, name="dom_third", tag="pw10", align_bytes=64)
+        dom_grouped[2] = third[:]
+        for g in range(PASSES):
+            cast_dom_scalar(3, g)
+        cast_dom_gpsimd(2, 0)
+        cast_dom_gpsimd(2, 1)
+        weigh(1, 1)
+        scatter_scalar(0, product(0, 0, HALF, nc.scalar.copy)[:], 0, HALF)
         quantise_pw(0, 1)
         quantise_pw(1, 1)
 
-        cast_dom(1)
-        scatter(0, early, 0, HALF)
-        late = product(0, HALF, N)
-        quantise_dom_by_pass(1)
-        scatter(0, late, HALF, N)
-        for b in range(1, E_BLOCKS - 1):
-            cast_dom(b + 1)
-            dv = product(b, 0, N)
-            quantise_dom(b + 1)
-            scatter(b, dv, 0, N)
-        scatter(E_BLOCKS - 1, product(E_BLOCKS - 1, 0, N), 0, N)
+        late = product(0, HALF, N, nc.scalar.copy)
+        quantise_dom(1)
+        quantise_dom(2)
+        scatter_vector(0, late[:], HALF, N)
+        store(0)
+        dv = product(1, 0, N, nc.scalar.copy)
+        for h in range(HALVES):
+            scatter_scalar(1, dv[:, h * HALF : (h + 1) * HALF], h * HALF, (h + 1) * HALF)
+        store(1)
+        quantise_dom(3, tag="dv0_%d" % HALF)
+        scatter_vector(2, product(2, 0, N, nc.vector.tensor_copy)[:], 0, N)
+        store(2)
+        dv = product(3, 0, N, nc.scalar.copy)
+        for h in range(HALVES):
+            scatter_scalar(3, dv[:, h * HALF : (h + 1) * HALF], h * HALF, (h + 1) * HALF)
+        store(3)

@@ -27,9 +27,10 @@ ENTRIES = 16
 RUN = 4
 PSUM_BANKS = 8
 Q_CUT = 96
-FIRST_SHARE = 96
-SECOND_SHARE = 40
-Q_LOADS = [(0, 0, P), (1, 0, Q_CUT), (1, Q_CUT, P)]
+Q0_CUT = 64
+FIRST_SHARE = 112
+SECOND_SHARE = 84
+Q_LOADS = [(0, 0, Q0_CUT), (0, Q0_CUT, P), (1, 0, Q0_CUT), (1, Q0_CUT, Q_CUT), (1, Q_CUT, P)]
 DOM_CUTS = [(0, P), (P, 2 * P), (2 * P, DV)]
 
 
@@ -75,6 +76,9 @@ def tile_attend_gat_lse_v_kernel(tc, qT, kT, lse, rw, dom, offs, out):
         for b in range(E_BLOCKS):
             nc.vector.memset(window[b][:], 0.0)
 
+        ones = sb.tile([P, 1], F32, name="ones")
+        nc.gpsimd.memset(ones[:], 1.0)
+
         identity = sb.tile([P, P], F32, name="identity")
         make_identity(nc, identity[:])
         nc.scalar.copy(rows[0 : 2 * PASSES, :], landed[:])
@@ -93,7 +97,7 @@ def tile_attend_gat_lse_v_kernel(tc, qT, kT, lse, rw, dom, offs, out):
         def cast_q(copy, g, m0, m1, t0, t1):
             base = max(l0 for lg, l0, l1 in Q_LOADS if lg == g and l0 <= m0)
             if g not in q_grouped:
-                q_grouped[g] = sb.tile([P, PACK, P, PACK], BF16, name="q_grouped", tag="q_grouped" if g == 0 else "q_raw0_0", align_bytes=64)
+                q_grouped[g] = sb.tile([P, PACK, P, PACK], BF16, name="q_grouped", tag="q_grouped" if g == 0 else "q_raw0_%d" % Q0_CUT, align_bytes=64)
             dst = q_grouped[g][:].rearrange("p t m j -> p m j t")
             src = q_raw[(g, base)][:].rearrange("p j (m t) -> p m j t", t=PACK)
             copy(dst[:, m0:m1, :, t0:t1], src[:, m0 - base : m1 - base, :, t0:t1])
@@ -155,14 +159,14 @@ def tile_attend_gat_lse_v_kernel(tc, qT, kT, lse, rw, dom, offs, out):
             codes, scales = quantise("dom%d" % b, dom_grouped[b].rearrange("p g e j -> p (g e j)"), PASSES * P, E5M2, tag)
             dom_mx[b] = [(codes[:, g * P : (g + 1) * P], scales[:, g * P : (g + 1) * P]) for g in range(PASSES)]
 
-        def product(b, i0, i1, copy):
+        def product(b, i0, i1, copy, tag=""):
             acc = ps.tile([P, N], F32, name="bank")
             for g in range(PASSES):
                 d_codes, d_scales = dom_mx[b][g]
                 nc.tensor.matmul_mx(out=acc[:, : i1 - i0], lhsT=d_codes.bitcast(E5M2), lhsT_scale=d_scales,
                                     rhs=pw_codes[g][:, i0:i1].bitcast(E4M3), rhs_scale=pw_scales[g][:, i0:i1],
                                     start=(g == 0), stop=(g == PASSES - 1))
-            dv = sb.tile([P, i1 - i0], F32, name="dv%d_%d" % (b, i0), align_bytes=64)
+            dv = sb.tile([P, i1 - i0], F32, name="dv%d_%d" % (b, i0), tag=tag, align_bytes=64)
             copy(dv[:], acc[:, : i1 - i0])
             return dv
 
@@ -172,18 +176,23 @@ def tile_attend_gat_lse_v_kernel(tc, qT, kT, lse, rw, dom, offs, out):
         def scatter_scalar(b, values, i0, i1):
             nc.scalar.activation(window[b][:].indirect(entries(i0, i1)), values, COPY)
 
+        def scatter_block_scalar(b, values):
+            nc.scalar.activation(window[b][:].indirect(offsets[:]), values, COPY, scale=ones[:])
+
         def store(b):
             nc.sync.dma_start(out[b * P : (b + 1) * P, :], window[b][:])
 
         pair = PACK // 2
+        cast_q(nc.vector.tensor_copy, 0, 0, Q0_CUT, 0, pair)
+        cast_q(nc.vector.tensor_copy, 0, 0, Q0_CUT, pair, PACK)
         cast_q(nc.scalar.copy, 0, FIRST_SHARE, P, 0, pair)
-        cast_q(nc.vector.tensor_copy, 0, 0, FIRST_SHARE, 0, pair)
-        cast_q(nc.vector.tensor_copy, 0, 0, SECOND_SHARE, pair, PACK)
+        cast_q(nc.vector.tensor_copy, 0, Q0_CUT, FIRST_SHARE, 0, pair)
+        cast_q(nc.vector.tensor_copy, 0, Q0_CUT, SECOND_SHARE, pair, PACK)
         cast_q(nc.scalar.copy, 0, SECOND_SHARE, P, pair, PACK)
         quantise_q(0, [(0, 1), (1, 1), (2, 1), (3, 1)])
         probs(0, 0)
 
-        for m0, m1 in ((0, Q_CUT), (Q_CUT, P)):
+        for m0, m1 in ((0, Q0_CUT), (Q0_CUT, Q_CUT), (Q_CUT, P)):
             cast_q(nc.vector.tensor_copy, 1, m0, m1, 0, pair)
             cast_q(nc.vector.tensor_copy, 1, m0, m1, pair, PACK)
         quantise_q(1, [(0, 1), (1, 1), (2, 2)])
@@ -194,7 +203,7 @@ def tile_attend_gat_lse_v_kernel(tc, qT, kT, lse, rw, dom, offs, out):
             pw[(0, h)] = first_pass[:, h * HALF : (h + 1) * HALF]
             quarter = sb.tile([P, HALF, PACK], BF16, name="pw1%d" % h, align_bytes=64)
             pw[(1, h)] = quarter[:]
-        early = sb.tile([P, 2, PASSES, P, PACK], BF16, name="dom_early", tag="q_raw0_0", align_bytes=64)
+        early = sb.tile([P, 2, PASSES, P, PACK], BF16, name="dom_early", tag="q_raw0_%d" % Q0_CUT, align_bytes=64)
         weigh(0, 0)
         probs(1, 0)
         weigh(0, 1)
@@ -207,32 +216,30 @@ def tile_attend_gat_lse_v_kernel(tc, qT, kT, lse, rw, dom, offs, out):
         quantise_dom(0)
         quantise_pw(0, 0)
         quantise_pw(1, 0)
-        last = sb.tile([P, PASSES, P, PACK], BF16, name="dom_last", tag="p32_01", align_bytes=64)
-        dom_grouped[3] = last[:]
-        third = sb.tile([P, PASSES, P, PACK], BF16, name="dom_third", tag="pw10", align_bytes=64)
+        third = sb.tile([P, PASSES, P, PACK], BF16, name="dom_third", tag="p32_00", align_bytes=64)
         dom_grouped[2] = third[:]
-        for g in range(PASSES):
-            cast_dom_scalar(3, g)
-        cast_dom_gpsimd(2, 0)
-        cast_dom_gpsimd(2, 1)
+        last = [sb.tile([P, P, PACK], BF16, name="dom_last%d" % g, tag=tag, align_bytes=64) for g, tag in enumerate(("p32_11", "pw10"))]
+        cast_dom_scalar(2, 0)
+        cast_dom_scalar(2, 1)
+        nc.gpsimd.tensor_copy(last[1][:], dom_source(3, 1).rearrange("p j e -> p e j"))
         weigh(1, 1)
         scatter_scalar(0, product(0, 0, HALF, nc.scalar.copy)[:], 0, HALF)
         quantise_pw(0, 1)
         quantise_pw(1, 1)
 
         late = product(0, HALF, N, nc.scalar.copy)
-        quantise_dom(1)
-        quantise_dom(2)
+        quantise_dom(1, tag="q_raw1_%d" % Q_CUT)
+        nc.vector.tensor_copy(last[0][:].rearrange("p (c i) j -> p c j i", i=RUN), dom_source(3, 0).rearrange("p j (c i) -> p c j i", i=RUN))
+        quantise_dom(2, tag="pw11")
         scatter_vector(0, late[:], HALF, N)
         store(0)
-        dv = product(1, 0, N, nc.scalar.copy)
         for h in range(HALVES):
-            scatter_scalar(1, dv[:, h * HALF : (h + 1) * HALF], h * HALF, (h + 1) * HALF)
+            scatter_scalar(1, product(1, h * HALF, (h + 1) * HALF, nc.scalar.copy)[:], h * HALF, (h + 1) * HALF)
         store(1)
-        quantise_dom(3, tag="dv0_%d" % HALF)
-        scatter_vector(2, product(2, 0, N, nc.vector.tensor_copy)[:], 0, N)
+        dv = product(2, 0, N, nc.vector.tensor_copy)
+        made = [quantise("dom3%d" % g, last[g][:].rearrange("p e j -> p (e j)"), P, E5M2, tag) for g, tag in enumerate(("dv0_%d" % HALF, "dv0_0"))]
+        dom_mx[3] = [(codes[:], scales[:]) for codes, scales in made]
+        scatter_vector(2, dv[:], 0, N)
         store(2)
-        dv = product(3, 0, N, nc.scalar.copy)
-        for h in range(HALVES):
-            scatter_scalar(3, dv[:, h * HALF : (h + 1) * HALF], h * HALF, (h + 1) * HALF)
+        scatter_block_scalar(3, product(3, 0, N, nc.scalar.copy, tag="dv1_%d" % HALF)[:])
         store(3)

@@ -26,6 +26,7 @@ E_BLOCKS = DV // P
 ENTRIES = 16
 RUN = 4
 PSUM_BANKS = 8
+ALIGN = 256
 Q_CUT = 96
 Q0_CUT = 64
 FIRST_SHARE = 112
@@ -42,8 +43,8 @@ def tile_attend_gat_lse_v_kernel(tc, qT, kT, lse, rw, dom, offs, out):
         ps_gate = ctx.enter_context(tc.psum_pool(name="ps_gate", bufs=1))
 
         def quantise(name, grouped, words, fmt, tag=""):
-            codes = sb.tile([P, words], U32, name=name + "_codes", tag=tag, align_bytes=64)
-            scales = sb.tile([P, words], U8, name=name + "_scales", align_bytes=64)
+            codes = sb.tile([P, words], U32, name=name + "_codes", tag=tag, align_bytes=ALIGN)
+            scales = sb.tile([P, words], U8, name=name + "_scales", align_bytes=ALIGN)
             nc.vector.quantize_mx(out=codes[:].bitcast(fmt), scales=scales[:], in_=grouped)
             return codes, scales
 
@@ -57,9 +58,9 @@ def tile_attend_gat_lse_v_kernel(tc, qT, kT, lse, rw, dom, offs, out):
         dom_rows = dom[0].rearrange("(g p j) e -> g p j e", p=P, j=PACK)
         q_raw = {}
         for g, m0, m1 in Q_LOADS:
-            q_raw[(g, m0)] = sb.tile([P, PACK, (m1 - m0) * PACK], F32, name="q_raw%d_%d" % (g, m0), align_bytes=64)
-        k_plane = [sb.tile([P, T], F32, name="k_plane%d" % j) for j in range(PACK)]
-        dom_raw = {(g, e0): sb.tile([P, PACK, e1 - e0], F32, name="dom_raw%d_%d" % (g, e0)) for e0, e1 in DOM_CUTS for g in range(PASSES)}
+            q_raw[(g, m0)] = sb.tile([P, PACK, (m1 - m0) * PACK], F32, name="q_raw%d_%d" % (g, m0), align_bytes=ALIGN)
+        k_plane = [sb.tile([P, T], F32, name="k_plane%d" % j, align_bytes=ALIGN) for j in range(PACK)]
+        dom_raw = {(g, e0): sb.tile([P, PACK, e1 - e0], F32, name="dom_raw%d_%d" % (g, e0), align_bytes=ALIGN) for e0, e1 in DOM_CUTS for g in range(PASSES)}
         nc.scalar.dma_start(landed[0:PASSES, :], lse[0].rearrange("(g c) o -> g (c o)", g=PASSES))
         nc.scalar.dma_start(landed[PASSES : 2 * PASSES, :], rw[0].rearrange("(g c) o -> g (c o)", g=PASSES))
         nc.sync.dma_start(k_plane[0][:], k_rows[0])
@@ -72,7 +73,7 @@ def tile_attend_gat_lse_v_kernel(tc, qT, kT, lse, rw, dom, offs, out):
             for g in range(PASSES):
                 nc.sync.dma_start(dom_raw[(g, e0)][:], dom_rows[g][:, :, e0:e1])
 
-        window = [sb.tile([P, T], F32, name="window%d" % b) for b in range(E_BLOCKS)]
+        window = [sb.tile([P, T], F32, name="window%d" % b, align_bytes=ALIGN) for b in range(E_BLOCKS)]
         for b in range(E_BLOCKS):
             nc.vector.memset(window[b][:], 0.0)
 
@@ -97,7 +98,7 @@ def tile_attend_gat_lse_v_kernel(tc, qT, kT, lse, rw, dom, offs, out):
         def cast_q(copy, g, m0, m1, t0, t1):
             base = max(l0 for lg, l0, l1 in Q_LOADS if lg == g and l0 <= m0)
             if g not in q_grouped:
-                q_grouped[g] = sb.tile([P, PACK, P, PACK], BF16, name="q_grouped", tag="q_grouped" if g == 0 else "q_raw0_%d" % Q0_CUT, align_bytes=64)
+                q_grouped[g] = sb.tile([P, PACK, P, PACK], BF16, name="q_grouped", tag="q_grouped" if g == 0 else "q_raw0_%d" % Q0_CUT, align_bytes=ALIGN)
             dst = q_grouped[g][:].rearrange("p t m j -> p m j t")
             src = q_raw[(g, base)][:].rearrange("p j (m t) -> p m j t", t=PACK)
             copy(dst[:, m0:m1, :, t0:t1], src[:, m0 - base : m1 - base, :, t0:t1])
@@ -107,7 +108,7 @@ def tile_attend_gat_lse_v_kernel(tc, qT, kT, lse, rw, dom, offs, out):
                 codes, scales = quantise("q%d%d" % (g, t), q_grouped[g][:, t : t + tiles].rearrange("p t m j -> p (t m j)"), tiles * P, E4M3)
                 q_mx[g].extend((codes[:, u * P : (u + 1) * P], scales[:, u * P : (u + 1) * P]) for u in range(tiles))
 
-        k_grouped = [sb.tile([P, HALF, PACK], BF16, name="k_grouped%d" % h, align_bytes=64) for h in range(HALVES)]
+        k_grouped = [sb.tile([P, HALF, PACK], BF16, name="k_grouped%d" % h, align_bytes=ALIGN) for h in range(HALVES)]
         for j in range(PACK):
             nc.vector.tensor_copy(k_grouped[0][:, :, j], k_plane[j][:].indirect(entries(0, HALF)))
             nc.scalar.activation(k_grouped[1][:, :, j], k_plane[j][:].indirect(entries(HALF, N)), COPY)
@@ -116,8 +117,8 @@ def tile_attend_gat_lse_v_kernel(tc, qT, kT, lse, rw, dom, offs, out):
         pw = {}
         p32 = {}
         scores = {}
-        pw_codes = [sb.tile([P, N], U32, name="pw_codes%d" % g, align_bytes=64) for g in range(PASSES)]
-        pw_scales = [sb.tile([P, N], U8, name="pw_scales%d" % g, align_bytes=64) for g in range(PASSES)]
+        pw_codes = [sb.tile([P, N], U32, name="pw_codes%d" % g, align_bytes=ALIGN) for g in range(PASSES)]
+        pw_scales = [sb.tile([P, N], U8, name="pw_scales%d" % g, align_bytes=ALIGN) for g in range(PASSES)]
 
         def probs(g, h):
             if h == 0:
@@ -127,7 +128,7 @@ def tile_attend_gat_lse_v_kernel(tc, qT, kT, lse, rw, dom, offs, out):
                 q_codes, q_scales = q_mx[g][t]
                 nc.tensor.matmul_mx(out=scores[g][t][:, h * HALF : (h + 1) * HALF], lhsT=q_codes.bitcast(E4M3), lhsT_scale=q_scales,
                                     rhs=k_codes[:].bitcast(E4M3), rhs_scale=k_scales[:], start=True, stop=True)
-            p32[(g, h)] = sb.tile([P, PACK, HALF], F32, name="p32_%d%d" % (g, h), align_bytes=64)
+            p32[(g, h)] = sb.tile([P, PACK, HALF], F32, name="p32_%d%d" % (g, h), align_bytes=ALIGN)
             for t in range(PACK):
                 nc.scalar.activation(p32[(g, h)][:, t, :], scores[g][t][:, h * HALF : (h + 1) * HALF], EXP, bias=neg_lse[:, g, t : t + 1])
 
@@ -166,7 +167,7 @@ def tile_attend_gat_lse_v_kernel(tc, qT, kT, lse, rw, dom, offs, out):
                 nc.tensor.matmul_mx(out=acc[:, : i1 - i0], lhsT=d_codes.bitcast(E5M2), lhsT_scale=d_scales,
                                     rhs=pw_codes[g][:, i0:i1].bitcast(E4M3), rhs_scale=pw_scales[g][:, i0:i1],
                                     start=(g == 0), stop=(g == PASSES - 1))
-            dv = sb.tile([P, i1 - i0], F32, name="dv%d_%d" % (b, i0), tag=tag, align_bytes=64)
+            dv = sb.tile([P, i1 - i0], F32, name="dv%d_%d" % (b, i0), tag=tag, align_bytes=ALIGN)
             copy(dv[:], acc[:, : i1 - i0])
             return dv
 
@@ -198,12 +199,12 @@ def tile_attend_gat_lse_v_kernel(tc, qT, kT, lse, rw, dom, offs, out):
         quantise_q(1, [(0, 1), (1, 1), (2, 2)])
         probs(0, 1)
 
-        first_pass = sb.tile([P, N, PACK], BF16, name="pw0", tag="q_raw1_%d" % Q_CUT, align_bytes=64)
+        first_pass = sb.tile([P, N, PACK], BF16, name="pw0", tag="q_raw1_%d" % Q_CUT, align_bytes=ALIGN)
         for h in range(HALVES):
             pw[(0, h)] = first_pass[:, h * HALF : (h + 1) * HALF]
-            quarter = sb.tile([P, HALF, PACK], BF16, name="pw1%d" % h, align_bytes=64)
+            quarter = sb.tile([P, HALF, PACK], BF16, name="pw1%d" % h, align_bytes=ALIGN)
             pw[(1, h)] = quarter[:]
-        early = sb.tile([P, 2, PASSES, P, PACK], BF16, name="dom_early", tag="q_raw0_%d" % Q0_CUT, align_bytes=64)
+        early = sb.tile([P, 2, PASSES, P, PACK], BF16, name="dom_early", tag="q_raw0_%d" % Q0_CUT, align_bytes=ALIGN)
         weigh(0, 0)
         probs(1, 0)
         weigh(0, 1)
@@ -216,9 +217,9 @@ def tile_attend_gat_lse_v_kernel(tc, qT, kT, lse, rw, dom, offs, out):
         quantise_dom(0)
         quantise_pw(0, 0)
         quantise_pw(1, 0)
-        third = sb.tile([P, PASSES, P, PACK], BF16, name="dom_third", tag="p32_00", align_bytes=64)
+        third = sb.tile([P, PASSES, P, PACK], BF16, name="dom_third", tag="p32_00", align_bytes=ALIGN)
         dom_grouped[2] = third[:]
-        last = [sb.tile([P, P, PACK], BF16, name="dom_last%d" % g, tag=tag, align_bytes=64) for g, tag in enumerate(("p32_11", "pw10"))]
+        last = [sb.tile([P, P, PACK], BF16, name="dom_last%d" % g, tag=tag, align_bytes=ALIGN) for g, tag in enumerate(("p32_11", "pw10"))]
         cast_dom_scalar(2, 0)
         cast_dom_scalar(2, 1)
         nc.gpsimd.tensor_copy(last[1][:], dom_source(3, 1).rearrange("p j e -> p e j"))

@@ -28,6 +28,7 @@ RUN = 4
 PSUM_BANKS = 8
 ALIGN = 256
 Q_CUT = 96
+SCALAR_COLUMNS = 32
 Q0_CUT = 64
 FIRST_SHARE = 112
 SECOND_SHARE = 84
@@ -160,14 +161,14 @@ def tile_attend_gat_lse_v_kernel(tc, qT, kT, lse, rw, dom, offs, out):
             codes, scales = quantise("dom%d" % b, dom_grouped[b].rearrange("p g e j -> p (g e j)"), PASSES * P, E5M2, tag)
             dom_mx[b] = [(codes[:, g * P : (g + 1) * P], scales[:, g * P : (g + 1) * P]) for g in range(PASSES)]
 
-        def product(b, i0, i1, copy, tag=""):
+        def product(b, i0, i1, copy, order=(0, 1)):
             acc = ps.tile([P, N], F32, name="bank")
-            for g in range(PASSES):
+            for n, g in enumerate(order):
                 d_codes, d_scales = dom_mx[b][g]
                 nc.tensor.matmul_mx(out=acc[:, : i1 - i0], lhsT=d_codes.bitcast(E5M2), lhsT_scale=d_scales,
                                     rhs=pw_codes[g][:, i0:i1].bitcast(E4M3), rhs_scale=pw_scales[g][:, i0:i1],
-                                    start=(g == 0), stop=(g == PASSES - 1))
-            dv = sb.tile([P, i1 - i0], F32, name="dv%d_%d" % (b, i0), tag=tag, align_bytes=ALIGN)
+                                    start=(n == 0), stop=(n == PASSES - 1))
+            dv = sb.tile([P, i1 - i0], F32, name="dv%d_%d" % (b, i0), align_bytes=ALIGN)
             copy(dv[:], acc[:, : i1 - i0])
             return dv
 
@@ -217,30 +218,33 @@ def tile_attend_gat_lse_v_kernel(tc, qT, kT, lse, rw, dom, offs, out):
         quantise_dom(0)
         quantise_pw(0, 0)
         quantise_pw(1, 0)
-        third = sb.tile([P, PASSES, P, PACK], BF16, name="dom_third", tag="p32_00", align_bytes=ALIGN)
-        dom_grouped[2] = third[:]
-        last = [sb.tile([P, P, PACK], BF16, name="dom_last%d" % g, tag=tag, align_bytes=ALIGN) for g, tag in enumerate(("p32_11", "pw10"))]
-        cast_dom_scalar(2, 0)
-        cast_dom_scalar(2, 1)
-        nc.gpsimd.tensor_copy(last[1][:], dom_source(3, 1).rearrange("p j e -> p e j"))
+        quantise_dom(1)
+        third = sb.tile([P, PASSES * P + SCALAR_COLUMNS, PACK], BF16, name="dom_third", tag="p32_00", align_bytes=ALIGN)
+        dom_grouped[2] = third[:, : PASSES * P].rearrange("p (g e) j -> p g e j", g=PASSES)
+        held = sb.tile([P, P, PACK], BF16, name="dom_last", tag="q_raw0_%d" % Q0_CUT, align_bytes=ALIGN)
+        last = [held[:], third[:, P + SCALAR_COLUMNS :]]
+        for g in range(PASSES):
+            cast_dom_scalar(2, g)
+        nc.scalar.copy(last[1][:, P - SCALAR_COLUMNS :].rearrange("p (c i) j -> p c j i", i=RUN),
+                       dom_source(3, 1)[:, :, P - SCALAR_COLUMNS :].rearrange("p j (c i) -> p c j i", i=RUN))
+        nc.gpsimd.tensor_copy(last[0], dom_source(3, 0).rearrange("p j e -> p e j"))
         weigh(1, 1)
-        scatter_scalar(0, product(0, 0, HALF, nc.scalar.copy)[:], 0, HALF)
+        for b in range(2):
+            scatter_scalar(b, product(b, 0, HALF, nc.scalar.copy)[:], 0, HALF)
         quantise_pw(0, 1)
         quantise_pw(1, 1)
 
-        late = product(0, HALF, N, nc.scalar.copy)
-        quantise_dom(1, tag="q_raw1_%d" % Q_CUT)
-        nc.vector.tensor_copy(last[0][:].rearrange("p (c i) j -> p c j i", i=RUN), dom_source(3, 0).rearrange("p j (c i) -> p c j i", i=RUN))
         quantise_dom(2, tag="pw11")
-        scatter_vector(0, late[:], HALF, N)
+        nc.gpsimd.tensor_copy(last[1][:, : P - SCALAR_COLUMNS], dom_source(3, 1)[:, :, : P - SCALAR_COLUMNS].rearrange("p j e -> p e j"))
+        late = [product(0, HALF, N, nc.vector.tensor_copy), product(1, HALF, N, nc.scalar.copy, order=(1, 0))]
+        scatter_vector(0, late[0][:], HALF, N)
         store(0)
-        for h in range(HALVES):
-            scatter_scalar(1, product(1, h * HALF, (h + 1) * HALF, nc.scalar.copy)[:], h * HALF, (h + 1) * HALF)
-        store(1)
-        dv = product(2, 0, N, nc.vector.tensor_copy)
-        made = [quantise("dom3%d" % g, last[g][:].rearrange("p e j -> p (e j)"), P, E5M2, tag) for g, tag in enumerate(("dv0_%d" % HALF, "dv0_0"))]
+        dv = product(2, 0, N, nc.scalar.copy)
+        made = [quantise("dom3%d" % g, last[g].rearrange("p e j -> p (e j)"), P, E5M2) for g in range(PASSES)]
         dom_mx[3] = [(codes[:], scales[:]) for codes, scales in made]
-        scatter_vector(2, dv[:], 0, N)
+        scatter_vector(1, late[1][:], HALF, N)
+        store(1)
+        scatter_block_scalar(2, dv[:])
         store(2)
-        scatter_block_scalar(3, product(3, 0, N, nc.scalar.copy, tag="dv1_%d" % HALF)[:])
+        scatter_vector(3, product(3, 0, N, nc.vector.tensor_copy)[:], 0, N)
         store(3)

@@ -26,6 +26,7 @@ E_BLOCKS = DV // P
 ENTRIES = 16
 RUN = 4
 PSUM_BANKS = 8
+WARM_UPS = 3
 ALIGN = 256
 Q_CUT = 96
 SCALAR_COLUMNS = 32
@@ -121,14 +122,17 @@ def tile_attend_gat_lse_v_kernel(tc, qT, kT, lse, rw, dom, offs, out):
         pw_codes = [sb.tile([P, N], U32, name="pw_codes%d" % g, align_bytes=ALIGN) for g in range(PASSES)]
         pw_scales = [sb.tile([P, N], U8, name="pw_scales%d" % g, align_bytes=ALIGN) for g in range(PASSES)]
 
+        def score(g, h, t):
+            q_codes, q_scales = q_mx[g][t]
+            k_codes, k_scales = k_mx[h]
+            nc.tensor.matmul_mx(out=scores[g][t][:, h * HALF : (h + 1) * HALF], lhsT=q_codes.bitcast(E4M3), lhsT_scale=q_scales,
+                                rhs=k_codes[:].bitcast(E4M3), rhs_scale=k_scales[:], start=True, stop=True)
+
         def probs(g, h):
             if h == 0:
                 scores[g] = [ps.tile([P, N], F32, name="bank") for t in range(PACK)]
-            k_codes, k_scales = k_mx[h]
             for t in range(PACK):
-                q_codes, q_scales = q_mx[g][t]
-                nc.tensor.matmul_mx(out=scores[g][t][:, h * HALF : (h + 1) * HALF], lhsT=q_codes.bitcast(E4M3), lhsT_scale=q_scales,
-                                    rhs=k_codes[:].bitcast(E4M3), rhs_scale=k_scales[:], start=True, stop=True)
+                score(g, h, t)
             p32[(g, h)] = sb.tile([P, PACK, HALF], F32, name="p32_%d%d" % (g, h), align_bytes=ALIGN)
             for t in range(PACK):
                 nc.scalar.activation(p32[(g, h)][:, t, :], scores[g][t][:, h * HALF : (h + 1) * HALF], EXP, bias=neg_lse[:, g, t : t + 1])
@@ -214,6 +218,8 @@ def tile_attend_gat_lse_v_kernel(tc, qT, kT, lse, rw, dom, offs, out):
             for g in range(PASSES):
                 cast_dom_gpsimd(b, g)
         probs(1, 1)
+        for t in range(PACK - WARM_UPS, PACK):
+            score(1, 1, t)
         weigh(1, 0)
         quantise_dom(0)
         quantise_pw(0, 0)

@@ -30,6 +30,7 @@ WARM_UPS = 3
 ALIGN = 256
 Q_CUT = 96
 SCALAR_COLUMNS = 32
+VECTOR_COLUMNS = 64
 Q0_CUT = 64
 FIRST_SHARE = 112
 SECOND_SHARE = 84
@@ -154,8 +155,8 @@ def tile_attend_gat_lse_v_kernel(tc, qT, kT, lse, rw, dom, offs, out):
             e0 = max(c0 for c0, c1 in DOM_CUTS if c0 <= b * P)
             return dom_raw[(g, e0)][:, :, b * P - e0 : (b + 1) * P - e0]
 
-        def cast_dom_gpsimd(b, g):
-            nc.gpsimd.tensor_copy(dom_grouped[b][:, g], dom_source(b, g).rearrange("p j e -> p e j"))
+        def cast_dom_gpsimd(b, g, columns):
+            nc.gpsimd.tensor_copy(dom_grouped[b][:, g, :columns], dom_source(b, g)[:, :, :columns].rearrange("p j e -> p e j"))
 
         def cast_dom_scalar(b, g):
             nc.scalar.copy(dom_grouped[b][:, g].rearrange("p (c i) j -> p c j i", i=RUN),
@@ -216,13 +217,15 @@ def tile_attend_gat_lse_v_kernel(tc, qT, kT, lse, rw, dom, offs, out):
         for b in range(2):
             dom_grouped[b] = early[:, b]
             for g in range(PASSES):
-                cast_dom_gpsimd(b, g)
+                cast_dom_gpsimd(b, g, P - VECTOR_COLUMNS if (b, g) == (1, 1) else P)
         probs(1, 1)
         for t in range(PACK - WARM_UPS, PACK):
             score(1, 1, t)
         weigh(1, 0)
         quantise_dom(0)
         quantise_pw(0, 0)
+        nc.vector.tensor_copy(dom_grouped[1][:, 1, P - VECTOR_COLUMNS :].rearrange("p (c i) j -> p c j i", i=RUN),
+                              dom_source(1, 1)[:, :, P - VECTOR_COLUMNS :].rearrange("p j (c i) -> p c j i", i=RUN))
         quantise_pw(1, 0)
         quantise_dom(1)
         third = sb.tile([P, PASSES * P + SCALAR_COLUMNS, PACK], BF16, name="dom_third", tag="p32_00", align_bytes=ALIGN)

@@ -29,8 +29,7 @@ PSUM_BANKS = 8
 WARM_UPS = 3
 ALIGN = 256
 Q_CUT = 96
-SCALAR_COLUMNS = 32
-VECTOR_COLUMNS = 64
+SCALAR_COLUMNS = 64
 Q0_CUT = 64
 FIRST_SHARE = 112
 SECOND_SHARE = 84
@@ -166,14 +165,15 @@ def tile_attend_gat_lse_v_kernel(tc, qT, kT, lse, rw, dom, offs, out):
             codes, scales = quantise("dom%d" % b, dom_grouped[b].rearrange("p g e j -> p (g e j)"), PASSES * P, E5M2, tag)
             dom_mx[b] = [(codes[:, g * P : (g + 1) * P], scales[:, g * P : (g + 1) * P]) for g in range(PASSES)]
 
-        def product(b, i0, i1, copy, order=(0, 1)):
+        def product(b, i0, i1, copy, order=(0, 1), dv=None):
             acc = ps.tile([P, N], F32, name="bank")
             for n, g in enumerate(order):
                 d_codes, d_scales = dom_mx[b][g]
                 nc.tensor.matmul_mx(out=acc[:, : i1 - i0], lhsT=d_codes.bitcast(E5M2), lhsT_scale=d_scales,
                                     rhs=pw_codes[g][:, i0:i1].bitcast(E4M3), rhs_scale=pw_scales[g][:, i0:i1],
                                     start=(n == 0), stop=(n == PASSES - 1))
-            dv = sb.tile([P, i1 - i0], F32, name="dv%d_%d" % (b, i0), align_bytes=ALIGN)
+            if dv is None:
+                dv = sb.tile([P, i1 - i0], F32, name="dv%d_%d" % (b, i0), align_bytes=ALIGN)
             copy(dv[:], acc[:, : i1 - i0])
             return dv
 
@@ -217,26 +217,24 @@ def tile_attend_gat_lse_v_kernel(tc, qT, kT, lse, rw, dom, offs, out):
         for b in range(2):
             dom_grouped[b] = early[:, b]
             for g in range(PASSES):
-                cast_dom_gpsimd(b, g, P - VECTOR_COLUMNS if (b, g) == (1, 1) else P)
+                cast_dom_gpsimd(b, g, P - SCALAR_COLUMNS if (b, g) == (1, 1) else P)
         probs(1, 1)
         for t in range(PACK - WARM_UPS, PACK):
             score(1, 1, t)
+        nc.scalar.copy(dom_grouped[1][:, 1, P - SCALAR_COLUMNS :].rearrange("p (c i) j -> p c j i", i=RUN),
+                       dom_source(1, 1)[:, :, P - SCALAR_COLUMNS :].rearrange("p j (c i) -> p c j i", i=RUN))
         weigh(1, 0)
         quantise_dom(0)
         quantise_pw(0, 0)
-        nc.vector.tensor_copy(dom_grouped[1][:, 1, P - VECTOR_COLUMNS :].rearrange("p (c i) j -> p c j i", i=RUN),
-                              dom_source(1, 1)[:, :, P - VECTOR_COLUMNS :].rearrange("p j (c i) -> p c j i", i=RUN))
         quantise_pw(1, 0)
         quantise_dom(1)
-        third = sb.tile([P, PASSES * P + SCALAR_COLUMNS, PACK], BF16, name="dom_third", tag="p32_00", align_bytes=ALIGN)
-        dom_grouped[2] = third[:, : PASSES * P].rearrange("p (g e) j -> p g e j", g=PASSES)
-        held = sb.tile([P, P, PACK], BF16, name="dom_last", tag="q_raw0_%d" % Q0_CUT, align_bytes=ALIGN)
-        last = [held[:], third[:, P + SCALAR_COLUMNS :]]
+        third = sb.tile([P, PASSES, P, PACK], BF16, name="dom_third", tag="p32_00", align_bytes=ALIGN)
+        dom_grouped[2] = third[:]
+        last = [sb.tile([P, P, PACK], BF16, name="dom_last%d" % g, tag=tag, align_bytes=ALIGN)
+                for g, tag in enumerate(("q_raw0_%d" % Q0_CUT, "p32_00"))]
         for g in range(PASSES):
             cast_dom_scalar(2, g)
-        nc.scalar.copy(last[1][:, P - SCALAR_COLUMNS :].rearrange("p (c i) j -> p c j i", i=RUN),
-                       dom_source(3, 1)[:, :, P - SCALAR_COLUMNS :].rearrange("p j (c i) -> p c j i", i=RUN))
-        nc.gpsimd.tensor_copy(last[0], dom_source(3, 0).rearrange("p j e -> p e j"))
+        nc.gpsimd.tensor_copy(last[0][:], dom_source(3, 0).rearrange("p j e -> p e j"))
         weigh(1, 1)
         for b in range(2):
             scatter_scalar(b, product(b, 0, HALF, nc.scalar.copy)[:], 0, HALF)
@@ -244,12 +242,13 @@ def tile_attend_gat_lse_v_kernel(tc, qT, kT, lse, rw, dom, offs, out):
         quantise_pw(1, 1)
 
         quantise_dom(2, tag="pw11")
-        nc.gpsimd.tensor_copy(last[1][:, : P - SCALAR_COLUMNS], dom_source(3, 1)[:, :, : P - SCALAR_COLUMNS].rearrange("p j e -> p e j"))
-        late = [product(0, HALF, N, nc.vector.tensor_copy), product(1, HALF, N, nc.scalar.copy, order=(1, 0))]
+        nc.gpsimd.tensor_copy(last[1][:], dom_source(3, 1).rearrange("p j e -> p e j"))
+        held = sb.tile([P, HALF + N], F32, name="dv_held", tag="dom_raw1_%d" % (2 * P), align_bytes=ALIGN)
+        late = [product(0, HALF, N, nc.vector.tensor_copy), product(1, HALF, N, nc.scalar.copy, order=(1, 0), dv=held[:, :HALF])]
         scatter_vector(0, late[0][:], HALF, N)
         store(0)
-        dv = product(2, 0, N, nc.scalar.copy)
-        made = [quantise("dom3%d" % g, last[g].rearrange("p e j -> p (e j)"), P, E5M2) for g in range(PASSES)]
+        dv = product(2, 0, N, nc.scalar.copy, dv=held[:, HALF:])
+        made = [quantise("dom3%d" % g, last[g][:].rearrange("p e j -> p (e j)"), P, E5M2) for g in range(PASSES)]
         dom_mx[3] = [(codes[:], scales[:]) for codes, scales in made]
         scatter_vector(1, late[1][:], HALF, N)
         store(1)

@@ -154,12 +154,12 @@ def tile_attend_gat_lse_v_kernel(tc, qT, kT, lse, rw, dom, offs, out):
             e0 = max(c0 for c0, c1 in DOM_CUTS if c0 <= b * P)
             return dom_raw[(g, e0)][:, :, b * P - e0 : (b + 1) * P - e0]
 
-        def cast_dom_gpsimd(b, g, columns):
-            nc.gpsimd.tensor_copy(dom_grouped[b][:, g, :columns], dom_source(b, g)[:, :, :columns].rearrange("p j e -> p e j"))
+        def cast_dom(copy, b, g, e0=0, e1=P):
+            copy(dom_grouped[b][:, g, e0:e1].rearrange("p (c i) j -> p c j i", i=RUN),
+                 dom_source(b, g)[:, :, e0:e1].rearrange("p j (c i) -> p c j i", i=RUN))
 
-        def cast_dom_scalar(b, g):
-            nc.scalar.copy(dom_grouped[b][:, g].rearrange("p (c i) j -> p c j i", i=RUN),
-                           dom_source(b, g).rearrange("p j (c i) -> p c j i", i=RUN))
+        def cast_dom_gpsimd(b, g, e0=0):
+            nc.gpsimd.tensor_copy(dom_grouped[b][:, g, e0:], dom_source(b, g)[:, :, e0:].rearrange("p j e -> p e j"))
 
         def quantise_dom(b, tag=""):
             codes, scales = quantise("dom%d" % b, dom_grouped[b].rearrange("p g e j -> p (g e j)"), PASSES * P, E5M2, tag)
@@ -210,31 +210,27 @@ def tile_attend_gat_lse_v_kernel(tc, qT, kT, lse, rw, dom, offs, out):
             pw[(0, h)] = first_pass[:, h * HALF : (h + 1) * HALF]
             quarter = sb.tile([P, HALF, PACK], BF16, name="pw1%d" % h, align_bytes=ALIGN)
             pw[(1, h)] = quarter[:]
-        early = sb.tile([P, 2, PASSES, P, PACK], BF16, name="dom_early", tag="q_raw0_%d" % Q0_CUT, align_bytes=ALIGN)
+        starts = [SCALAR_COLUMNS + 3 * P, SCALAR_COLUMNS + P, SCALAR_COLUMNS, 0]
+        dom_all = sb.tile([P, starts[0] + PASSES * P, PACK], BF16, name="dom_all", tag="q_raw0_%d" % Q0_CUT, align_bytes=ALIGN)
+        for b in range(E_BLOCKS):
+            dom_grouped[b] = dom_all[:, starts[b] : starts[b] + PASSES * P].rearrange("p (g e) j -> p g e j", g=PASSES)
         weigh(0, 0)
         probs(1, 0)
         weigh(0, 1)
-        for b in range(2):
-            dom_grouped[b] = early[:, b]
-            for g in range(PASSES):
-                cast_dom_gpsimd(b, g, P - SCALAR_COLUMNS if (b, g) == (1, 1) else P)
+        for b, g in ((0, 0), (0, 1), (1, 0)):
+            cast_dom_gpsimd(b, g)
         probs(1, 1)
         for t in range(PACK - WARM_UPS, PACK):
             score(1, 1, t)
-        nc.scalar.copy(dom_grouped[1][:, 1, P - SCALAR_COLUMNS :].rearrange("p (c i) j -> p c j i", i=RUN),
-                       dom_source(1, 1)[:, :, P - SCALAR_COLUMNS :].rearrange("p j (c i) -> p c j i", i=RUN))
         weigh(1, 0)
         quantise_dom(0)
         quantise_pw(0, 0)
+        cast_dom(nc.vector.tensor_copy, 1, 1)
         quantise_pw(1, 0)
         quantise_dom(1)
-        third = sb.tile([P, PASSES, P, PACK], BF16, name="dom_third", tag="p32_00", align_bytes=ALIGN)
-        dom_grouped[2] = third[:]
-        last = [sb.tile([P, P, PACK], BF16, name="dom_last%d" % g, tag=tag, align_bytes=ALIGN)
-                for g, tag in enumerate(("q_raw0_%d" % Q0_CUT, "p32_00"))]
-        for g in range(PASSES):
-            cast_dom_scalar(2, g)
-        nc.gpsimd.tensor_copy(last[0][:], dom_source(3, 0).rearrange("p j e -> p e j"))
+        cast_dom(nc.scalar.copy, 2, 0)
+        cast_dom(nc.scalar.copy, 3, 0, 0, SCALAR_COLUMNS)
+        cast_dom_gpsimd(2, 1)
         weigh(1, 1)
         for b in range(2):
             scatter_scalar(b, product(b, 0, HALF, nc.scalar.copy)[:], 0, HALF)
@@ -242,14 +238,14 @@ def tile_attend_gat_lse_v_kernel(tc, qT, kT, lse, rw, dom, offs, out):
         quantise_pw(1, 1)
 
         quantise_dom(2, tag="pw11")
-        nc.gpsimd.tensor_copy(last[1][:], dom_source(3, 1).rearrange("p j e -> p e j"))
+        cast_dom_gpsimd(3, 0, SCALAR_COLUMNS)
+        cast_dom_gpsimd(3, 1)
         held = sb.tile([P, HALF + N], F32, name="dv_held", tag="dom_raw1_%d" % (2 * P), align_bytes=ALIGN)
         late = [product(0, HALF, N, nc.vector.tensor_copy), product(1, HALF, N, nc.scalar.copy, order=(1, 0), dv=held[:, :HALF])]
         scatter_vector(0, late[0][:], HALF, N)
         store(0)
         dv = product(2, 0, N, nc.scalar.copy, dv=held[:, HALF:])
-        made = [quantise("dom3%d" % g, last[g][:].rearrange("p e j -> p (e j)"), P, E5M2) for g in range(PASSES)]
-        dom_mx[3] = [(codes[:], scales[:]) for codes, scales in made]
+        quantise_dom(3)
         scatter_vector(1, late[1][:], HALF, N)
         store(1)
         scatter_block_scalar(2, dv[:])

@@ -158,8 +158,8 @@ def tile_attend_gat_lse_v_kernel(tc, qT, kT, lse, rw, dom, offs, out):
             copy(dom_grouped[b][:, g, e0:e1].rearrange("p (c i) j -> p c j i", i=RUN),
                  dom_source(b, g)[:, :, e0:e1].rearrange("p j (c i) -> p c j i", i=RUN))
 
-        def cast_dom_gpsimd(b, g, e0=0):
-            nc.gpsimd.tensor_copy(dom_grouped[b][:, g, e0:], dom_source(b, g)[:, :, e0:].rearrange("p j e -> p e j"))
+        def cast_dom_gpsimd(b, g, e0=0, e1=P):
+            nc.gpsimd.tensor_copy(dom_grouped[b][:, g, e0:e1], dom_source(b, g)[:, :, e0:e1].rearrange("p j e -> p e j"))
 
         def quantise_dom(b, tag=""):
             codes, scales = quantise("dom%d" % b, dom_grouped[b].rearrange("p g e j -> p (g e j)"), PASSES * P, E5M2, tag)
@@ -219,13 +219,14 @@ def tile_attend_gat_lse_v_kernel(tc, qT, kT, lse, rw, dom, offs, out):
         weigh(0, 1)
         for b, g in ((0, 0), (0, 1), (1, 0)):
             cast_dom_gpsimd(b, g)
+        cast_dom_gpsimd(1, 1, 0, P - SCALAR_COLUMNS)
         probs(1, 1)
         for t in range(PACK - WARM_UPS, PACK):
             score(1, 1, t)
+        cast_dom(nc.scalar.copy, 1, 1, P - SCALAR_COLUMNS)
         weigh(1, 0)
         quantise_dom(0)
         quantise_pw(0, 0)
-        cast_dom(nc.vector.tensor_copy, 1, 1)
         quantise_pw(1, 0)
         quantise_dom(1)
         cast_dom(nc.scalar.copy, 2, 0)

from contextlib import ExitStack

import concourse.mybir as mybir
from concourse.masks import make_identity

N, T, D, DV, R = 512, 2048, 512, 512, 1024
FLOPS = 2 * D * R * N + 2 * R * DV * N

F32 = mybir.dt.float32
BF16 = mybir.dt.bfloat16
U32 = mybir.dt.uint32
U16 = mybir.dt.uint16
U8 = mybir.dt.uint8
E4M3 = mybir.dt.float8_e4m3fn_x4
E5M2 = mybir.dt.float8_e5m2_x4
EXP = mybir.ActivationFunctionType.Exp
COPY = mybir.ActivationFunctionType.Copy
MULT = mybir.AluOpType.mult

P = 128
PACK = 4
PASSES = R // (P * PACK)
HALVES = 2
HALF = N // HALVES
E_BLOCKS = DV // P
ENTRIES = 16
RUN = 4
PSUM_BANKS = 8
WARM_UPS = 3
ALIGN = 256
Q_CUT = 96
SCALAR_COLUMNS = 64
Q0_CUT = 64
FIRST_SHARE = 112
SECOND_SHARE = 84
Q_LOADS = [(0, 0, Q0_CUT), (0, Q0_CUT, P), (1, 0, Q0_CUT), (1, Q0_CUT, Q_CUT), (1, Q_CUT, P)]
DOM_CUTS = [(0, P), (P, 2 * P), (2 * P, DV)]


def tile_attend_gat_lse_v_kernel(tc, qT, kT, lse, rw, dom, offs, out):
    nc = tc.nc
    with ExitStack() as ctx:
        sb = ctx.enter_context(tc.tile_pool(name="sb", bufs=1))
        ps = ctx.enter_context(tc.psum_pool(name="ps", bufs=PSUM_BANKS - 1))
        ps_gate = ctx.enter_context(tc.psum_pool(name="ps_gate", bufs=1))

        def quantise(name, grouped, words, fmt, tag=""):
            codes = sb.tile([P, words], U32, name=name + "_codes", tag=tag, align_bytes=ALIGN)
            scales = sb.tile([P, words], U8, name=name + "_scales", align_bytes=ALIGN)
            nc.vector.quantize_mx(out=codes[:].bitcast(fmt), scales=scales[:], in_=grouped)
            return codes, scales

        offsets = sb.tile([P, N // ENTRIES], U16, name="offsets")
        rows = sb.tile([P, P * PACK], F32, name="rows")
        nc.gpsimd.memset(rows[:], 0.0)
        landed = sb.tile([2 * PASSES, P * PACK], F32, name="landed")

        q_rows = qT[0].rearrange("(p j) (g c) -> g p j c", j=PACK, g=PASSES)
        k_rows = kT.rearrange("(p j) c -> j p c", j=PACK)
        dom_rows = dom[0].rearrange("(g p j) e -> g p j e", p=P, j=PACK)
        q_raw = {}
        for g, m0, m1 in Q_LOADS:
            q_raw[(g, m0)] = sb.tile([P, PACK, (m1 - m0) * PACK], F32, name="q_raw%d_%d" % (g, m0), align_bytes=ALIGN)
        k_plane = [sb.tile([P, T], F32, name="k_plane%d" % j, align_bytes=ALIGN) for j in range(PACK)]
        dom_raw = {(g, e0): sb.tile([P, PACK, e1 - e0], F32, name="dom_raw%d_%d" % (g, e0), align_bytes=ALIGN) for e0, e1 in DOM_CUTS for g in range(PASSES)}
        nc.scalar.dma_start(landed[0:PASSES, :], lse[0].rearrange("(g c) o -> g (c o)", g=PASSES))
        nc.scalar.dma_start(landed[PASSES : 2 * PASSES, :], rw[0].rearrange("(g c) o -> g (c o)", g=PASSES))
        nc.sync.dma_start(k_plane[0][:], k_rows[0])
        nc.sync.dma_start(offsets[:], offs)
        for j in range(1, PACK):
            nc.sync.dma_start(k_plane[j][:], k_rows[j])
        for g, m0, m1 in Q_LOADS:
            nc.sync.dma_start(q_raw[(g, m0)][:], q_rows[g][:, :, m0 * PACK : m1 * PACK])
        for e0, e1 in DOM_CUTS:
            for g in range(PASSES):
                nc.sync.dma_start(dom_raw[(g, e0)][:], dom_rows[g][:, :, e0:e1])

        window = [sb.tile([P, T], F32, name="window%d" % b, align_bytes=ALIGN) for b in range(E_BLOCKS)]
        for b in range(E_BLOCKS):
            nc.vector.memset(window[b][:], 0.0)

        ones = sb.tile([P, 1], F32, name="ones")
        nc.gpsimd.memset(ones[:], 1.0)

        identity = sb.tile([P, P], F32, name="identity")
        make_identity(nc, identity[:])
        nc.scalar.copy(rows[0 : 2 * PASSES, :], landed[:])
        gate_bank = ps_gate.tile([P, PACK, P], F32, name="gate_bank")
        for t in range(PACK):
            nc.tensor.transpose(gate_bank[:, t, :], rows[:, t : P * PACK : PACK], identity[:])
        neg_lse = sb.tile([P, PASSES, PACK], F32, name="neg_lse")
        nc.scalar.mul(neg_lse[:], gate_bank[:, :, 0:PASSES].rearrange("p t g -> p g t"), -1.0)

        def entries(i0, i1):
            return offsets[:, i0 // ENTRIES : i1 // ENTRIES]

        q_grouped = {}
        q_mx = [[] for g in range(PASSES)]

        def cast_q(copy, g, m0, m1, t0, t1):
            base = max(l0 for lg, l0, l1 in Q_LOADS if lg == g and l0 <= m0)
            if g not in q_grouped:
                q_grouped[g] = sb.tile([P, PACK, P, PACK], BF16, name="q_grouped", tag="q_grouped" if g == 0 else "q_raw0_%d" % Q0_CUT, align_bytes=ALIGN)
            dst = q_grouped[g][:].rearrange("p t m j -> p m j t")
            src = q_raw[(g, base)][:].rearrange("p j (m t) -> p m j t", t=PACK)
            copy(dst[:, m0:m1, :, t0:t1], src[:, m0 - base : m1 - base, :, t0:t1])

        def quantise_q(g, runs):
            for t, tiles in runs:
                codes, scales = quantise("q%d%d" % (g, t), q_grouped[g][:, t : t + tiles].rearrange("p t m j -> p (t m j)"), tiles * P, E4M3)
                q_mx[g].extend((codes[:, u * P : (u + 1) * P], scales[:, u * P : (u + 1) * P]) for u in range(tiles))

        k_grouped = [sb.tile([P, HALF, PACK], BF16, name="k_grouped%d" % h, align_bytes=ALIGN) for h in range(HALVES)]
        for j in range(PACK):
            nc.vector.tensor_copy(k_grouped[0][:, :, j], k_plane[j][:].indirect(entries(0, HALF)))
            nc.scalar.activation(k_grouped[1][:, :, j], k_plane[j][:].indirect(entries(HALF, N)), COPY)
        k_mx = [quantise("k%d" % h, k_grouped[h][:].rearrange("p i j -> p (i j)"), HALF, E4M3) for h in range(HALVES)]

        pw = {}
        p32 = {}
        scores = {}
        pw_codes = [sb.tile([P, N], U32, name="pw_codes%d" % g, align_bytes=ALIGN) for g in range(PASSES)]
        pw_scales = [sb.tile([P, N], U8, name="pw_scales%d" % g, align_bytes=ALIGN) for g in range(PASSES)]

        def score(g, h, t):
            q_codes, q_scales = q_mx[g][t]
            k_codes, k_scales = k_mx[h]
            nc.tensor.matmul_mx(out=scores[g][t][:, h * HALF : (h + 1) * HALF], lhsT=q_codes.bitcast(E4M3), lhsT_scale=q_scales,
                                rhs=k_codes[:].bitcast(E4M3), rhs_scale=k_scales[:], start=True, stop=True)

        def probs(g, h):
            if h == 0:
                scores[g] = [ps.tile([P, N], F32, name="bank") for t in range(PACK)]
            for t in range(PACK):
                score(g, h, t)
            p32[(g, h)] = sb.tile([P, PACK, HALF], F32, name="p32_%d%d" % (g, h), align_bytes=ALIGN)
            for t in range(PACK):
                nc.scalar.activation(p32[(g, h)][:, t, :], scores[g][t][:, h * HALF : (h + 1) * HALF], EXP, bias=neg_lse[:, g, t : t + 1])

        def weigh(g, h):
            gate = gate_bank[:, :, PASSES + g : PASSES + g + 1].unsqueeze(1).to_broadcast([P, HALF // RUN, PACK, RUN])
            nc.vector.tensor_tensor(pw[(g, h)].rearrange("p (c i) t -> p c t i", i=RUN),
                                    p32[(g, h)][:].rearrange("p t (c i) -> p c t i", i=RUN), gate, MULT)

        def quantise_pw(g, h):
            i0, i1 = h * HALF, (h + 1) * HALF
            nc.vector.quantize_mx(out=pw_codes[g][:, i0:i1].bitcast(E4M3), scales=pw_scales[g][:, i0:i1],
                                  in_=pw[(g, h)].rearrange("p i t -> p (i t)"))

        dom_grouped = {}
        dom_mx = [None] * E_BLOCKS

        def dom_source(b, g):
            e0 = max(c0 for c0, c1 in DOM_CUTS if c0 <= b * P)
            return dom_raw[(g, e0)][:, :, b * P - e0 : (b + 1) * P - e0]

        def cast_dom(copy, b, g, e0=0, e1=P):
            copy(dom_grouped[b][:, g, e0:e1].rearrange("p (c i) j -> p c j i", i=RUN),
                 dom_source(b, g)[:, :, e0:e1].rearrange("p j (c i) -> p c j i", i=RUN))

        def cast_dom_gpsimd(b, g, e0=0, e1=P):
            nc.gpsimd.tensor_copy(dom_grouped[b][:, g, e0:e1], dom_source(b, g)[:, :, e0:e1].rearrange("p j e -> p e j"))

        def quantise_dom(b, tag=""):
            codes, scales = quantise("dom%d" % b, dom_grouped[b].rearrange("p g e j -> p (g e j)"), PASSES * P, E5M2, tag)
            dom_mx[b] = [(codes[:, g * P : (g + 1) * P], scales[:, g * P : (g + 1) * P]) for g in range(PASSES)]

        def product(b, i0, i1, copy, order=(0, 1), dv=None):
            acc = ps.tile([P, N], F32, name="bank")
            for n, g in enumerate(order):
                d_codes, d_scales = dom_mx[b][g]
                nc.tensor.matmul_mx(out=acc[:, : i1 - i0], lhsT=d_codes.bitcast(E5M2), lhsT_scale=d_scales,
                                    rhs=pw_codes[g][:, i0:i1].bitcast(E4M3), rhs_scale=pw_scales[g][:, i0:i1],
                                    start=(n == 0), stop=(n == PASSES - 1))
            if dv is None:
                dv = sb.tile([P, i1 - i0], F32, name="dv%d_%d" % (b, i0), align_bytes=ALIGN)
            copy(dv[:], acc[:, : i1 - i0])
            return dv

        def scatter_vector(b, values, i0, i1):
            nc.vector.tensor_copy(window[b][:].indirect(entries(i0, i1)), values)

        def scatter_scalar(b, values, i0, i1):
            nc.scalar.activation(window[b][:].indirect(entries(i0, i1)), values, COPY)

        def scatter_block_scalar(b, values):
            nc.scalar.activation(window[b][:].indirect(offsets[:]), values, COPY, scale=ones[:])

        def store(b):
            nc.sync.dma_start(out[b * P : (b + 1) * P, :], window[b][:])

        pair = PACK // 2
        cast_q(nc.vector.tensor_copy, 0, 0, Q0_CUT, 0, pair)
        cast_q(nc.vector.tensor_copy, 0, 0, Q0_CUT, pair, PACK)
        cast_q(nc.scalar.copy, 0, FIRST_SHARE, P, 0, pair)
        cast_q(nc.vector.tensor_copy, 0, Q0_CUT, FIRST_SHARE, 0, pair)
        cast_q(nc.vector.tensor_copy, 0, Q0_CUT, SECOND_SHARE, pair, PACK)
        cast_q(nc.scalar.copy, 0, SECOND_SHARE, P, pair, PACK)
        quantise_q(0, [(0, 1), (1, 1), (2, 1), (3, 1)])
        probs(0, 0)

        for m0, m1 in ((0, Q0_CUT), (Q0_CUT, Q_CUT), (Q_CUT, P)):
            cast_q(nc.vector.tensor_copy, 1, m0, m1, 0, pair)
            cast_q(nc.vector.tensor_copy, 1, m0, m1, pair, PACK)
        quantise_q(1, [(0, 1), (1, 1), (2, 2)])
        probs(0, 1)

        first_pass = sb.tile([P, N, PACK], BF16, name="pw0", tag="q_raw1_%d" % Q_CUT, align_bytes=ALIGN)
        for h in range(HALVES):
            pw[(0, h)] = first_pass[:, h * HALF : (h + 1) * HALF]
            quarter = sb.tile([P, HALF, PACK], BF16, name="pw1%d" % h, align_bytes=ALIGN)
            pw[(1, h)] = quarter[:]
        starts = [SCALAR_COLUMNS + 3 * P, SCALAR_COLUMNS + P, SCALAR_COLUMNS, 0]
        dom_all = sb.tile([P, starts[0] + PASSES * P, PACK], BF16, name="dom_all", tag="q_raw0_%d" % Q0_CUT, align_bytes=ALIGN)
        for b in range(E_BLOCKS):
            dom_grouped[b] = dom_all[:, starts[b] : starts[b] + PASSES * P].rearrange("p (g e) j -> p g e j", g=PASSES)
        weigh(0, 0)
        probs(1, 0)
        weigh(0, 1)
        for b, g in ((0, 0), (0, 1), (1, 0)):
            cast_dom_gpsimd(b, g)
        cast_dom_gpsimd(1, 1, 0, P - SCALAR_COLUMNS)
        probs(1, 1)
        for t in range(PACK - WARM_UPS, PACK):
            score(1, 1, t)
        cast_dom(nc.scalar.copy, 1, 1, P - SCALAR_COLUMNS)
        weigh(1, 0)
        quantise_dom(0)
        quantise_pw(0, 0)
        quantise_pw(1, 0)
        quantise_dom(1)
        cast_dom(nc.scalar.copy, 2, 0)
        cast_dom(nc.scalar.copy, 3, 0, 0, SCALAR_COLUMNS)
        cast_dom_gpsimd(2, 1)
        weigh(1, 1)
        for b in range(2):
            scatter_scalar(b, product(b, 0, HALF, nc.scalar.copy)[:], 0, HALF)
        quantise_pw(0, 1)
        quantise_pw(1, 1)

        quantise_dom(2, tag="pw11")
        cast_dom_gpsimd(3, 0, SCALAR_COLUMNS)
        cast_dom_gpsimd(3, 1)
        held = sb.tile([P, HALF + N], F32, name="dv_held", tag="dom_raw1_%d" % (2 * P), align_bytes=ALIGN)
        late = [product(0, HALF, N, nc.vector.tensor_copy), product(1, HALF, N, nc.scalar.copy, order=(1, 0), dv=held[:, :HALF])]
        scatter_vector(0, late[0][:], HALF, N)
        store(0)
        dv = product(2, 0, N, nc.scalar.copy, dv=held[:, HALF:])
        quantise_dom(3)
        scatter_vector(1, late[1][:], HALF, N)
        store(1)
        scatter_block_scalar(2, dv[:])
        store(2)
        scatter_vector(3, product(3, 0, N, nc.vector.tensor_copy)[:], 0, N)
        store(3)
